import numpy as np
import ml_dtypes


def mxq(x, axis, fmt="e4m3"):
    dtype, down = {"e4m3": (ml_dtypes.float8_e4m3fn, 7), "e5m2": (ml_dtypes.float8_e5m2, 14)}[fmt]
    v = np.moveaxis(np.asarray(x, np.float32).astype(ml_dtypes.bfloat16).astype(np.float64), axis, -1)
    blocks = v.reshape(v.shape[:-1] + (-1, 32))
    amax = np.abs(blocks).max(-1, keepdims=True)
    byte = np.maximum(np.where(amax > 0, np.frexp(amax)[1] - 1 + 127, 0) - down, 1)
    scale = np.exp2(byte - 127.0)
    codes = (blocks / scale).astype(np.float32).astype(dtype).astype(np.float64)
    return np.moveaxis((codes * scale).reshape(v.shape), -1, axis)


WIDE = False


def mx_kscale(k):
    if not WIDE:
        return np.ones(k)
    levels = np.array([10, -10, 5, -5, 0])
    if k % 512:
        return np.exp2(np.random.permutation(np.resize(levels, k // 32))).repeat(32)
    a = np.empty((k // 512, 16))
    for p in range(k // 512):
        a[p, :8] = np.random.permutation(np.resize(levels, 8))
        for g in range(8):
            far = levels[np.abs(levels - a[p, g]) >= 10]
            a[p, g + 8] = far[np.random.randint(len(far))]
    return np.exp2(a.ravel()).repeat(32)


def f64(x):
    return np.asarray(x).astype(np.float64)


def striped(idx):
    return np.tile(idx.reshape(-1, 16).T, (8, 1)).astype(np.uint16)


def unstriped(offs):
    return offs[:16].T.reshape(-1).astype(np.int64)


E2M1 = np.array([0.0, 0.5, 1.0, 1.5, 2.0, 3.0, 4.0, 6.0, -0.0, -0.5, -1.0, -1.5, -2.0, -3.0, -4.0, -6.0])


def pack_weight(w, fmt):
    k, n = w.shape
    w = f64(np.asarray(w, np.float32).astype(ml_dtypes.bfloat16)).reshape(k // 32, 32, n)
    amax = np.abs(w).max(1)
    if fmt == "e4m3":
        byte = np.frexp(amax)[1] - 1 + 127 - 7
    else:
        mant, ex = np.frexp(amax / 6.0)
        byte = np.where(mant > 0.5, ex, ex - 1) + 127
    byte = np.clip(np.where(amax > 0, byte, 1), 1, 254)
    scaled = (w * np.exp2(127.0 - byte)[:, None, :]).reshape(k, n).astype(np.float32)
    by_word = np.ascontiguousarray(scaled.reshape(k // 512, 128, 4, n).transpose(0, 1, 3, 2))
    if fmt == "e4m3":
        words = by_word.astype(ml_dtypes.float8_e4m3fn).view(np.uint8)
    else:
        c = by_word.astype(ml_dtypes.float4_e2m1fn).view(np.uint8) & 0xF
        words = (c[..., 0::2] | (c[..., 1::2] << 4)).reshape(k // 512, 128, 2 * n)
    return np.ascontiguousarray(words), np.ascontiguousarray(byte.astype(np.uint8).reshape(k // 512, 16, n))


def unpack_weight(words, scales, fmt):
    g, _, n = scales.shape
    words = np.ascontiguousarray(words).reshape(g, 128, n, -1)
    if fmt == "e4m3":
        vals = words.view(ml_dtypes.float8_e4m3fn).astype(np.float64)
    else:
        nib = np.empty((g, 128, n, 4), np.uint8)
        nib[..., 0::2] = words & 0xF
        nib[..., 1::2] = words >> 4
        vals = E2M1[nib]
    vals = vals * np.repeat(np.exp2(scales.astype(np.float64) - 127.0), 8, axis=1)[..., None]
    return vals.transpose(0, 1, 3, 2).reshape(g * 512, n)


K, T, E1, C1, E2, C2, H = 1024, 512, 8, 128, 8, 128, 512
N = 128


def deal(E, C):
    first = np.random.permutation(np.repeat(np.arange(E), T // E))
    second = (first + 1 + np.random.permutation(np.repeat(np.arange(E - 1), -(-T // (E - 1)))[:T])) % E
    while np.bincount(second, minlength=E).max() != T // E:
        load = np.bincount(second, minlength=E); hi, lo = int(load.argmax()), int(load.argmin())
        t = np.flatnonzero((second == hi) & (first != lo))[0]; second[t] = lo
    slot_token = np.empty(E * C, np.int64); pos = np.empty((2, T), np.int64); fill = np.zeros(E, np.int64)
    place = np.stack([np.random.permutation(C) for _ in range(E)])
    for r, deal in enumerate((first, second)):
        for t in np.random.permutation(T):
            e = deal[t]; j = e * C + place[e, fill[e]]; fill[e] += 1; slot_token[j] = t; pos[r, t] = j
    g = np.random.uniform(0.2, 0.8, T)
    return slot_token, pos, np.stack([g, 1.0 - g])


def by_expert(wq, xq, E, C):
    return np.concatenate([wq[e].T @ xq[:, e * C:(e + 1) * C] for e in range(E)], axis=1)


def setup_inputs():
    n = np.random.standard_normal
    s = mx_kscale(K)
    u = mx_kscale(H)
    slots1, pos1, g1 = deal(E1, C1)
    slots2, pos2, g2 = deal(E2, C2)
    x = pack_weight(n((K, T)) * s[:, None], "e4m3")
    w1 = [pack_weight(m, "e2m1") for m in n((E1, K, H)) / np.sqrt(K) / s[None, :, None] * u]
    return {
        "x_words": x[0],
        "x_scales": x[1],
        "w1_words": np.stack([m[0] for m in w1]),
        "w1_scales": np.stack([m[1] for m in w1]),
        "w2": (n((E2, H, N)) / np.sqrt(H) / u[None, :, None]).astype(np.float32),
        "gate1": (np.stack([np.tile(r, (128, 1)) for r in g1])).astype(np.float32),
        "gate2": (np.stack([np.tile(r, (128, 1)) for r in g2])).astype(np.float32),
        "offs": striped(slots1),
        "pos1": striped(pos1[0]),
        "pos2": striped(pos1[1]),
        "offs2": striped(slots2),
        "pos3": striped(pos2[0]),
        "pos4": striped(pos2[1]),
    }


def reference(x_words, x_scales, w1_words, w1_scales, w2, gate1, gate2, offs, pos1, pos2, offs2, pos3, pos4):
    w1 = np.stack([unpack_weight(w1_words[e], w1_scales[e], "e2m1") for e in range(E1)])
    w2q = mxq(f64(w2), 1, "e4m3")
    idx, idx2 = unstriped(offs), unstriped(offs2)
    xq = unpack_weight(x_words, x_scales, "e4m3")[:, idx]
    h = by_expert(w1, xq, E1, C1)
    c = sum(f64(gate1[r, :1]) * h[:, unstriped(p)] for r, p in enumerate((pos1, pos2)))
    y = by_expert(w2q, mxq(c[:, idx2], 0, "e4m3"), E2, C2)
    out = sum(f64(gate2[r, :1]) * y[:, unstriped(p)] for r, p in enumerate((pos3, pos4)))
    return out

@@ -1,0 +1,270 @@
+from contextlib import ExitStack
+
+import concourse.mybir as mybir
+from concourse.masks import make_identity
+
+K, T, E, C, H, N = 1024, 512, 8, 128, 512, 128
+S = E * C
+FLOPS = 2 * S * K * H + 2 * S * H * N
+
+F32 = mybir.dt.float32
+BF16 = mybir.dt.bfloat16
+I32 = mybir.dt.int32
+U32 = mybir.dt.uint32
+U16 = mybir.dt.uint16
+U8 = mybir.dt.uint8
+FP8X4 = mybir.dt.float8_e4m3fn_x4
+FP4X4 = mybir.dt.float4_e2m1fn_x4
+MULT = mybir.AluOpType.mult
+ADD = mybir.AluOpType.add
+COPY = mybir.ActivationFunctionType.Copy
+
+P = 128
+PACK = 4
+PASSES = K // (P * PACK)
+ROW_TILES = H // P
+TOKEN_BLOCKS = T // P
+FIRST_GROUPS = ((0, 1), (1, 2), (2, 4), (4, 6), (6, 7), (7, 8))
+SECOND_GROUPS = ((0, 2), (2, 4), (4, 6), (6, 7), (7, 8))
+
+
+def entries(lst, first, last):
+    return lst[:, first // 16 : last // 16]
+
+
+def tile_moe_ser_none_kernel(
+    tc, x_words, x_scales, w1_words, w1_scales, w2, gate1, gate2, offs, pos1, pos2, offs2, pos3, pos4, out
+):
+    nc = tc.nc
+    with ExitStack() as ctx:
+        keep = ctx.enter_context(tc.tile_pool(name="keep", bufs=1))
+        psum = ctx.enter_context(tc.psum_pool(name="psum", bufs=1))
+
+        def bank(tag, bufs):
+            return psum.tile([P, 512], F32, name=tag, tag=tag, bufs=bufs)
+
+        def load_list(name, src):
+            lst = keep.tile(list(src.shape), U16, name=name)
+            nc.sync.dma_start(lst[:], src)
+            return lst
+
+        x_plane = keep.tile([P, PASSES, T], U8, name="x_plane", align_bytes=64)
+        w1_plane = keep.tile([P, E * PASSES, H], U8, name="w1_plane", align_bytes=64)
+        nc.vector.memset(x_plane[:].rearrange("p s t -> p (s t)").bitcast(I32), 0)
+        w1_plane_words = w1_plane[:].rearrange("p g i -> p (g i)").bitcast(I32)
+        half = E * PASSES * H // 8
+        nc.gpsimd.memset(w1_plane_words[:, :384], 0)
+        nc.vector.memset(w1_plane_words[:, 384:half], 0)
+        nc.vector.memset(w1_plane_words[:, half:], 0)
+
+        offs_sb = load_list("offs_sb", offs)
+        x_sb = []
+        for s in range(PASSES):
+            words = keep.tile([P, T], I32, name=f"x_sb{s}", align_bytes=64)
+            nc.sync.dma_start(words[:], x_words[s].rearrange("p t d -> p (t d)").bitcast(I32))
+            x_sb.append(words)
+        x_rows = x_scales.rearrange("s (q r) t -> r q s t", r=4)
+        for r in range(4):
+            nc.sync.dma_start(x_plane[r:P:32, :, :].bitcast(I32), x_rows[r].bitcast(I32))
+        w1_rows = w1_scales.rearrange("e s (q r) i -> r q (e s) i", r=4)
+
+        def load_w1_scales(first, last):
+            groups = slice(first * PASSES, last * PASSES)
+            for r in range(4):
+                nc.sync.dma_start(w1_plane[r:P:32, groups, :].bitcast(I32), w1_rows[r][:, groups, :].bitcast(I32))
+
+        def load_w1(pair):
+            words = keep.tile([P, 2 * PASSES, 2 * H], U8, name=f"w1_sb{pair}", tag=f"pair{pair}", align_bytes=64)
+            nc.sync.dma_start(
+                words[:].bitcast(I32),
+                w1_words[2 * pair : 2 * pair + 2].rearrange("e s p b -> p (e s) b").bitcast(I32),
+            )
+            return words
+
+        def load_w2(pair, tag):
+            raw = keep.tile([P, 2, PACK, N], F32, name=f"w2_sb{pair}", tag=tag)
+            nc.sync.dma_start(
+                raw[:].rearrange("p e j n -> p e (j n)"),
+                w2[2 * pair : 2 * pair + 2].rearrange("e (p j) n -> p e (j n)", j=PACK),
+            )
+            return raw
+
+        w1_sb, w2_sb = [], []
+        w1_sb.append(load_w1(0))
+        load_w1_scales(0, 4)
+        w1_sb.append(load_w1(1))
+        w2_sb.append(load_w2(0, "stage0"))
+        load_w1_scales(4, 8)
+        w1_sb.append(load_w1(2))
+        w1_sb.append(load_w1(3))
+        pos1_sb = load_list("pos1_sb", pos1)
+        pos2_sb = load_list("pos2_sb", pos2)
+
+        ident = keep.tile([P, P], F32, name="ident")
+        gate_rows = keep.tile([P, P], F32, name="gate_rows", tag="stage1")
+        nc.gpsimd.memset(gate_rows[:], 0.0)
+        pieces = gate1.rearrange("r p (q c) -> (r p q) c", c=P)
+        step = P + 1
+        nc.gpsimd.dma_start(gate_rows[0:8, :], pieces[0 : 7 * step + 1 : step, :])
+        make_identity(nc, ident[:])
+        gate_bank = bank("turned", 2)
+        nc.tensor.transpose(gate_bank[:, :P], gate_rows[:], ident[:])
+        gate_cols = keep.tile([P, 8], F32, name="gate_cols")
+        nc.scalar.copy(gate_cols[:], gate_bank[:, :8])
+        w2_sb.append(load_w2(1, "stage1"))
+
+        offs2_sb = load_list("offs2_sb", offs2)
+        pos3_sb = load_list("pos3_sb", pos3)
+        pos4_sb = load_list("pos4_sb", pos4)
+
+        h_sb = keep.tile([P, ROW_TILES, S], F32, name="h_sb", tag="h_slot", align_bytes=64)
+        w2_bf = {}
+
+        def cast_w2(pair, tag):
+            cast = keep.tile([P, 2, N, PACK], BF16, name=f"w2_bf{pair}", tag=tag, align_bytes=64)
+            for e in range(2):
+                nc.scalar.copy(
+                    cast[:, e, :, :].rearrange("p (c i) j -> p c j i", i=4),
+                    w2_sb[pair][:, e, :, :].rearrange("p j (c i) -> p c j i", i=4),
+                )
+            w2_bf[pair] = cast
+
+        def first_layer(e, xg, sg, cols, tiles):
+            acc = bank("acc", 3)
+            for k, m in enumerate(tiles):
+                for s in range(PASSES):
+                    nc.tensor.matmul_mx(
+                        acc[:, k * C : (k + 1) * C],
+                        lhsT=w1_sb[e // 2][:, (e % 2) * PASSES + s, 2 * m * P : 2 * (m + 1) * P].bitcast(FP4X4),
+                        lhsT_scale=w1_plane[:, e * PASSES + s, m * P : (m + 1) * P],
+                        rhs=xg[:, s, cols].bitcast(FP8X4),
+                        rhs_scale=sg[:, s, cols],
+                        start=(s == 0),
+                        stop=(s == PASSES - 1),
+                    )
+            nc.scalar.copy(
+                h_sb[:, tiles.start : tiles.stop, e * C : (e + 1) * C],
+                acc[:, : len(tiles) * C].rearrange("p (m c) -> p m c", c=C),
+            )
+
+        for first, last in FIRST_GROUPS:
+            width = (last - first) * C
+            lst = entries(offs_sb, first * C, last * C)
+            xg = keep.tile([P, PASSES, width], U32, name=f"xg{first}", tag="xg", bufs=3, align_bytes=64)
+            sg = keep.tile([P, PASSES, width], U8, name=f"sg{first}", tag="sg", bufs=3, align_bytes=64)
+            for s in range(PASSES):
+                nc.vector.tensor_copy(xg[:, s, :], x_sb[s][:].bitcast(U32).indirect(lst))
+            for s in range(PASSES):
+                nc.vector.tensor_copy(sg[:, s, :], x_plane[:, s, :].indirect(lst))
+            for e in range(first, last):
+                cols = slice((e - first) * C, (e - first + 1) * C)
+                if e < E - 1:
+                    first_layer(e, xg, sg, cols, range(ROW_TILES))
+                else:
+                    first_layer(e, xg, sg, cols, range(0, 1))
+                    first_layer(e, xg, sg, cols, range(1, 2))
+                    first_layer(e, xg, sg, cols, range(2, 4))
+            if last in (2, 4):
+                cast_w2(last // 2 - 1, f"pair{last // 2 - 1}")
+                w2_sb.append(load_w2(last // 2 + 1, f"stage{last // 2 - 1}"))
+        cast_w2(2, "pair3")
+        gate2_sb = keep.tile([P, 2, T], F32, name="gate2_sb", tag="stage0")
+        nc.sync.dma_start(gate2_sb[:], gate2.rearrange("r p t -> p r t"))
+
+        c_pairs = keep.tile([P, 2, T, 2], BF16, name="c_pairs", align_bytes=64)
+        for q in range(TOKEN_BLOCKS):
+            closing = q == TOKEN_BLOCKS - 1
+            backs = [bank("back", 3), bank("back", 3)] if closing else [bank("back", 3)]
+            for r, pos_sb in enumerate((pos1_sb, pos2_sb)):
+                lst = entries(pos_sb, q * P, (q + 1) * P)
+                picked = keep.tile([P, ROW_TILES, P], F32, name=f"picked{q}_{r}", tag="picked", bufs=3)
+                gated = keep.tile([P, PACK, P], F32, name=f"gated{q}_{r}", tag=f"gated{q}_{r}", align_bytes=64)
+                runs = (range(0, 3), range(3, 4)) if closing and r == 1 else (range(ROW_TILES),)
+                for run in runs:
+                    turned = bank("turned", 2)
+                    for k, m in enumerate(run):
+                        nc.vector.tensor_copy(picked[:, m, :], h_sb[:, m, :].indirect(lst))
+                        nc.tensor.transpose(turned[:, k * P : (k + 1) * P], picked[:, m, :], ident[:])
+                    nc.scalar.activation(
+                        gated[:, :, run.start * 32 : run.stop * 32],
+                        turned[:, : len(run) * P].rearrange("t (p j) -> t j p", j=PACK),
+                        COPY,
+                        scale=gate_cols[:, r * TOKEN_BLOCKS + q : r * TOKEN_BLOCKS + q + 1],
+                    )
+                per_bank = PACK // len(backs)
+                for j in range(PACK):
+                    k = j % per_bank
+                    nc.tensor.matmul(
+                        backs[j // per_bank][:, k * P : (k + 1) * P],
+                        gated[:, j, :],
+                        ident[:],
+                        is_transpose=True,
+                        start=(r == 0 and k == 0),
+                        stop=(r == 1 and k == per_bank - 1),
+                    )
+            halves = 2 // len(backs)
+            for b, back in enumerate(backs):
+                nc.scalar.copy(
+                    c_pairs[:, b * halves : (b + 1) * halves, q * P : (q + 1) * P, :],
+                    back[:, : halves * 2 * P].rearrange("p (u d t) -> p u t d", u=halves, d=2),
+                )
+            if q == 0:
+                cast_w2(3, "gated0_0")
+
+        w2_codes = keep.tile([P, E * N], U32, name="w2_codes", tag="h_slot", align_bytes=64)
+        w2_plane = keep.tile([P, E * N], U8, name="w2_plane", align_bytes=64)
+        for g in range(4):
+            cols = slice(2 * g * N, 2 * (g + 1) * N)
+            nc.vector.quantize_mx(
+                out=w2_codes[:, cols].bitcast(FP8X4),
+                scales=w2_plane[:, cols],
+                in_=w2_bf[g][:].rearrange("p e n j -> p (e n j)"),
+            )
+
+        c_words = c_pairs[:].rearrange("p u t d -> p u (t d)").bitcast(U32)
+        y_sb = keep.tile([P, S], F32, name="y_sb")
+        for first, last in SECOND_GROUPS:
+            width = (last - first) * C
+            lst = entries(offs2_sb, first * C, last * C)
+            woven = keep.tile([P, width, 2], U32, name=f"woven{first}", align_bytes=64)
+            if last < E:
+                cg = keep.tile([P, 2, width], U32, name=f"cg{first}", tag="cg", bufs=3, align_bytes=64)
+                for u in range(2):
+                    nc.vector.tensor_copy(cg[:, u, :], c_words[:, u, :].indirect(lst))
+                nc.scalar.copy(woven[:], cg[:].rearrange("p u s -> p s u"))
+            else:
+                for u in range(2):
+                    nc.vector.tensor_copy(woven[:, :, u], c_words[:, u, :].indirect(lst))
+            codes = keep.tile([P, width], U32, name=f"codes{first}", align_bytes=64)
+            plane = keep.tile([P, width], U8, name=f"plane{first}", align_bytes=64)
+            nc.vector.quantize_mx(
+                out=codes[:].bitcast(FP8X4),
+                scales=plane[:],
+                in_=woven[:].rearrange("p s u -> p (s u)").bitcast(BF16),
+            )
+            acc = bank("acc", 3)
+            for e in range(first, last):
+                cols = slice((e - first) * C, (e - first + 1) * C)
+                nc.tensor.matmul_mx(
+                    acc[:, cols],
+                    lhsT=w2_codes[:, e * N : (e + 1) * N].bitcast(FP8X4),
+                    lhsT_scale=w2_plane[:, e * N : (e + 1) * N],
+                    rhs=codes[:, cols].bitcast(FP8X4),
+                    rhs_scale=plane[:, cols],
+                    start=True,
+                    stop=True,
+                )
+            nc.scalar.copy(y_sb[:, first * C : last * C], acc[:, :width])
+
+        for hh in range(2):
+            toks = slice(hh * T // 2, (hh + 1) * T // 2)
+            parts = []
+            for r, pos_sb in enumerate((pos3_sb, pos4_sb)):
+                part = keep.tile([P, T // 2], F32, name=f"part{hh}_{r}")
+                nc.vector.tensor_tensor(
+                    part[:], y_sb[:].indirect(entries(pos_sb, toks.start, toks.stop)), gate2_sb[:, r, toks], MULT
+                )
+                parts.append(part)
+            total = keep.tile([P, T // 2], F32, name=f"total{hh}")
+            nc.vector.tensor_tensor(total[:], parts[0][:], parts[1][:], ADD)
+            nc.sync.dma_start(out[:, toks], total[:])

@@ -25,6 +25,7 @@ PASSES = K // (P * PACK)
 ROW_TILES = H // P
 TOKEN_BLOCKS = T // P
 FIRST_GROUPS = ((0, 1), (1, 2), (2, 4), (4, 6), (6, 7), (7, 8))
+TURN_BANKS = (0, 1, 2, 0, 1, 2, 1, 2, 1)
 SECOND_GROUPS = ((0, 2), (2, 4), (4, 6), (6, 7), (7, 8))
 
 
@@ -48,7 +49,7 @@ def tile_moe_ser_none_kernel(
             nc.sync.dma_start(lst[:], src)
             return lst
 
-        x_plane = keep.tile([P, PASSES, T], U8, name="x_plane", align_bytes=64)
+        x_plane = keep.tile([P, PASSES, T], U8, name="x_plane", tag="x_plane", align_bytes=64)
         w1_plane = keep.tile([P, E * PASSES, H], U8, name="w1_plane", align_bytes=64)
         nc.vector.memset(x_plane[:].rearrange("p s t -> p (s t)").bitcast(I32), 0)
         w1_plane_words = w1_plane[:].rearrange("p g i -> p (g i)").bitcast(I32)
@@ -105,9 +106,9 @@ def tile_moe_ser_none_kernel(
         nc.gpsimd.memset(gate_rows[:], 0.0)
         pieces = gate1.rearrange("r p (q c) -> (r p q) c", c=P)
         step = P + 1
-        nc.gpsimd.dma_start(gate_rows[0:8, :], pieces[0 : 7 * step + 1 : step, :])
+        nc.scalar.dma_start(gate_rows[0:8, :], pieces[0 : 7 * step + 1 : step, :])
         make_identity(nc, ident[:])
-        gate_bank = bank("turned", 2)
+        gate_bank = bank("turned0", 1)
         nc.tensor.transpose(gate_bank[:, :P], gate_rows[:], ident[:])
         gate_cols = keep.tile([P, 8], F32, name="gate_cols")
         nc.scalar.copy(gate_cols[:], gate_bank[:, :8])
@@ -129,8 +130,16 @@ def tile_moe_ser_none_kernel(
                 )
             w2_bf[pair] = cast
 
+        def cast_w2_vector(pair, tag, bufs):
+            cast = keep.tile([P, 2, N, PACK], BF16, name=f"w2_bf{pair}", tag=tag, bufs=bufs, align_bytes=64)
+            nc.vector.tensor_copy(
+                cast[:].rearrange("p e (c i) j -> p e c j i", i=4),
+                w2_sb[pair][:].rearrange("p e j (c i) -> p e c j i", i=4),
+            )
+            w2_bf[pair] = cast
+
         def first_layer(e, xg, sg, cols, tiles):
-            acc = bank("acc", 3)
+            acc = bank("acc", 5)
             for k, m in enumerate(tiles):
                 for s in range(PASSES):
                     nc.tensor.matmul_mx(
@@ -167,21 +176,23 @@ def tile_moe_ser_none_kernel(
             if last in (2, 4):
                 cast_w2(last // 2 - 1, f"pair{last // 2 - 1}")
                 w2_sb.append(load_w2(last // 2 + 1, f"stage{last // 2 - 1}"))
-        cast_w2(2, "pair3")
+        cast_w2_vector(2, "x_plane", 1)
         gate2_sb = keep.tile([P, 2, T], F32, name="gate2_sb", tag="stage0")
         nc.sync.dma_start(gate2_sb[:], gate2.rearrange("r p t -> p r t"))
 
         c_pairs = keep.tile([P, 2, T, 2], BF16, name="c_pairs", align_bytes=64)
+        turns = []
         for q in range(TOKEN_BLOCKS):
             closing = q == TOKEN_BLOCKS - 1
-            backs = [bank("back", 3), bank("back", 3)] if closing else [bank("back", 3)]
+            backs = [bank("acc", 5), bank("acc", 5)] if closing else [bank("acc", 5)]
             for r, pos_sb in enumerate((pos1_sb, pos2_sb)):
                 lst = entries(pos_sb, q * P, (q + 1) * P)
-                picked = keep.tile([P, ROW_TILES, P], F32, name=f"picked{q}_{r}", tag="picked", bufs=3)
+                picked = keep.tile([P, ROW_TILES, P], F32, name=f"picked{q}_{r}", tag="picked", bufs=3, align_bytes=64)
                 gated = keep.tile([P, PACK, P], F32, name=f"gated{q}_{r}", tag=f"gated{q}_{r}", align_bytes=64)
                 runs = (range(0, 3), range(3, 4)) if closing and r == 1 else (range(ROW_TILES),)
                 for run in runs:
-                    turned = bank("turned", 2)
+                    turned = bank(f"turned{TURN_BANKS[len(turns)]}", 1)
+                    turns.append(turned)
                     for k, m in enumerate(run):
                         nc.vector.tensor_copy(picked[:, m, :], h_sb[:, m, :].indirect(lst))
                         nc.tensor.transpose(turned[:, k * P : (k + 1) * P], picked[:, m, :], ident[:])
@@ -208,8 +219,7 @@ def tile_moe_ser_none_kernel(
                     c_pairs[:, b * halves : (b + 1) * halves, q * P : (q + 1) * P, :],
                     back[:, : halves * 2 * P].rearrange("p (u d t) -> p u t d", u=halves, d=2),
                 )
-            if q == 0:
-                cast_w2(3, "gated0_0")
+        cast_w2_vector(3, "picked", 3)
 
         w2_codes = keep.tile([P, E * N], U32, name="w2_codes", tag="h_slot", align_bytes=64)
         w2_plane = keep.tile([P, E * N], U8, name="w2_plane", align_bytes=64)
@@ -242,7 +252,7 @@ def tile_moe_ser_none_kernel(
                 scales=plane[:],
                 in_=woven[:].rearrange("p s u -> p (s u)").bitcast(BF16),
             )
-            acc = bank("acc", 3)
+            acc = bank("acc", 5)
             for e in range(first, last):
                 cols = slice((e - first) * C, (e - first + 1) * C)
                 nc.tensor.matmul_mx(

@@ -24,9 +24,9 @@ PACK = 4
 PASSES = K // (P * PACK)
 ROW_TILES = H // P
 TOKEN_BLOCKS = T // P
-FIRST_GROUPS = ((0, 1), (1, 2), (2, 4), (4, 6), (6, 7), (7, 8))
-TURN_BANKS = (0, 1, 2, 0, 1, 2, 1, 2, 1)
-SECOND_GROUPS = ((0, 2), (2, 4), (4, 6), (6, 7), (7, 8))
+FIRST_GROUPS = ((0, 3), (3, 6), (6, 8))
+SECOND_GROUPS = ((0, 4), (4, 6), (6, 7), (7, 8))
+SPARE = 192
 
 
 def entries(lst, first, last):
@@ -41,32 +41,34 @@ def tile_moe_ser_none_kernel(
         keep = ctx.enter_context(tc.tile_pool(name="keep", bufs=1))
         psum = ctx.enter_context(tc.psum_pool(name="psum", bufs=1))
 
-        def bank(tag, bufs):
-            return psum.tile([P, 512], F32, name=tag, tag=tag, bufs=bufs)
+        def bank(index):
+            return psum.tile([P, 512], F32, name=f"bank{index}", tag=f"bank{index}")
 
         def load_list(name, src):
             lst = keep.tile(list(src.shape), U16, name=name)
             nc.sync.dma_start(lst[:], src)
             return lst
 
-        x_plane = keep.tile([P, PASSES, T], U8, name="x_plane", tag="x_plane", align_bytes=64)
+        x_plane = keep.tile([P, PASSES, T], U8, name="x_plane", align_bytes=64)
         w1_plane = keep.tile([P, E * PASSES, H], U8, name="w1_plane", align_bytes=64)
         nc.vector.memset(x_plane[:].rearrange("p s t -> p (s t)").bitcast(I32), 0)
         w1_plane_words = w1_plane[:].rearrange("p g i -> p (g i)").bitcast(I32)
-        half = E * PASSES * H // 8
-        nc.gpsimd.memset(w1_plane_words[:, :384], 0)
-        nc.vector.memset(w1_plane_words[:, 384:half], 0)
-        nc.vector.memset(w1_plane_words[:, half:], 0)
+        early = FIRST_GROUPS[0][1] * PASSES * H // 4
+        nc.gpsimd.memset(w1_plane_words[:, : early // 2], 0)
+        nc.vector.memset(w1_plane_words[:, early // 2 : early], 0)
+        nc.vector.memset(w1_plane_words[:, early:], 0)
 
-        offs_sb = load_list("offs_sb", offs)
-        x_sb = []
-        for s in range(PASSES):
+        def load_x(s):
             words = keep.tile([P, T], I32, name=f"x_sb{s}", align_bytes=64)
             nc.sync.dma_start(words[:], x_words[s].rearrange("p t d -> p (t d)").bitcast(I32))
-            x_sb.append(words)
+            return words
+
+        x_sb = [load_x(0)]
         x_rows = x_scales.rearrange("s (q r) t -> r q s t", r=4)
         for r in range(4):
             nc.sync.dma_start(x_plane[r:P:32, :, :].bitcast(I32), x_rows[r].bitcast(I32))
+        offs_sb = load_list("offs_sb", offs)
+        x_sb.append(load_x(1))
         w1_rows = w1_scales.rearrange("e s (q r) i -> r q (e s) i", r=4)
 
         def load_w1_scales(first, last):
@@ -74,177 +76,154 @@ def tile_moe_ser_none_kernel(
             for r in range(4):
                 nc.sync.dma_start(w1_plane[r:P:32, groups, :].bitcast(I32), w1_rows[r][:, groups, :].bitcast(I32))
 
-        def load_w1(pair):
-            words = keep.tile([P, 2 * PASSES, 2 * H], U8, name=f"w1_sb{pair}", tag=f"pair{pair}", align_bytes=64)
+        def load_w1(first, last):
+            words = keep.tile(
+                [P, (last - first) * PASSES, 2 * H], U8, name=f"w1_sb{first}", tag=f"w1_{first}", align_bytes=64
+            )
             nc.sync.dma_start(
-                words[:].bitcast(I32),
-                w1_words[2 * pair : 2 * pair + 2].rearrange("e s p b -> p (e s) b").bitcast(I32),
+                words[:].bitcast(I32), w1_words[first:last].rearrange("e s p b -> p (e s) b").bitcast(I32)
             )
             return words
 
-        def load_w2(pair, tag):
-            raw = keep.tile([P, 2, PACK, N], F32, name=f"w2_sb{pair}", tag=tag)
+        def load_w2(half, tag):
+            raw = keep.tile([P, E // 2, PACK, N], F32, name=f"w2_sb{half}", tag=tag, align_bytes=64)
             nc.sync.dma_start(
                 raw[:].rearrange("p e j n -> p e (j n)"),
-                w2[2 * pair : 2 * pair + 2].rearrange("e (p j) n -> p e (j n)", j=PACK),
+                w2[half * E // 2 : (half + 1) * E // 2].rearrange("e (p j) n -> p e (j n)", j=PACK),
             )
             return raw
 
-        w1_sb, w2_sb = [], []
-        w1_sb.append(load_w1(0))
-        load_w1_scales(0, 4)
-        w1_sb.append(load_w1(1))
-        w2_sb.append(load_w2(0, "stage0"))
-        load_w1_scales(4, 8)
-        w1_sb.append(load_w1(2))
-        w1_sb.append(load_w1(3))
+        def load_gate(name, src, tag):
+            rows = keep.tile([P, 2, T], F32, name=name, tag=tag, align_bytes=64)
+            nc.sync.dma_start(rows[:], src.rearrange("r p t -> p r t"))
+            return rows
+
+        w1_sb = [load_w1(*FIRST_GROUPS[0])]
+        load_w1_scales(*FIRST_GROUPS[0])
+        w1_sb.append(load_w1(*FIRST_GROUPS[1]))
+        load_w1_scales(FIRST_GROUPS[0][1], E)
+        w1_sb.append(load_w1(*FIRST_GROUPS[2]))
         pos1_sb = load_list("pos1_sb", pos1)
         pos2_sb = load_list("pos2_sb", pos2)
-
-        ident = keep.tile([P, P], F32, name="ident")
-        gate_rows = keep.tile([P, P], F32, name="gate_rows", tag="stage1")
-        nc.gpsimd.memset(gate_rows[:], 0.0)
-        pieces = gate1.rearrange("r p (q c) -> (r p q) c", c=P)
-        step = P + 1
-        nc.scalar.dma_start(gate_rows[0:8, :], pieces[0 : 7 * step + 1 : step, :])
-        make_identity(nc, ident[:])
-        gate_bank = bank("turned0", 1)
-        nc.tensor.transpose(gate_bank[:, :P], gate_rows[:], ident[:])
-        gate_cols = keep.tile([P, 8], F32, name="gate_cols")
-        nc.scalar.copy(gate_cols[:], gate_bank[:, :8])
-        w2_sb.append(load_w2(1, "stage1"))
-
         offs2_sb = load_list("offs2_sb", offs2)
         pos3_sb = load_list("pos3_sb", pos3)
         pos4_sb = load_list("pos4_sb", pos4)
 
-        h_sb = keep.tile([P, ROW_TILES, S], F32, name="h_sb", tag="h_slot", align_bytes=64)
-        w2_bf = {}
+        ident = keep.tile([P, P], F32, name="ident")
+        make_identity(nc, ident[:])
+        c_words = keep.tile([P, 2 * T + SPARE], F32, name="c_words", align_bytes=64)
+        nc.gpsimd.memset(c_words[:, 2 * T :], 0.0)
 
-        def cast_w2(pair, tag):
-            cast = keep.tile([P, 2, N, PACK], BF16, name=f"w2_bf{pair}", tag=tag, align_bytes=64)
-            for e in range(2):
-                nc.scalar.copy(
-                    cast[:, e, :, :].rearrange("p (c i) j -> p c j i", i=4),
-                    w2_sb[pair][:, e, :, :].rearrange("p j (c i) -> p c j i", i=4),
-                )
-            w2_bf[pair] = cast
-
-        def cast_w2_vector(pair, tag, bufs):
-            cast = keep.tile([P, 2, N, PACK], BF16, name=f"w2_bf{pair}", tag=tag, bufs=bufs, align_bytes=64)
-            nc.vector.tensor_copy(
-                cast[:].rearrange("p e (c i) j -> p e c j i", i=4),
-                w2_sb[pair][:].rearrange("p e j (c i) -> p e c j i", i=4),
-            )
-            w2_bf[pair] = cast
-
-        def first_layer(e, xg, sg, cols, tiles):
-            acc = bank("acc", 5)
-            for k, m in enumerate(tiles):
-                for s in range(PASSES):
-                    nc.tensor.matmul_mx(
-                        acc[:, k * C : (k + 1) * C],
-                        lhsT=w1_sb[e // 2][:, (e % 2) * PASSES + s, 2 * m * P : 2 * (m + 1) * P].bitcast(FP4X4),
-                        lhsT_scale=w1_plane[:, e * PASSES + s, m * P : (m + 1) * P],
-                        rhs=xg[:, s, cols].bitcast(FP8X4),
-                        rhs_scale=sg[:, s, cols],
-                        start=(s == 0),
-                        stop=(s == PASSES - 1),
-                    )
-            nc.scalar.copy(
-                h_sb[:, tiles.start : tiles.stop, e * C : (e + 1) * C],
-                acc[:, : len(tiles) * C].rearrange("p (m c) -> p m c", c=C),
-            )
-
-        for first, last in FIRST_GROUPS:
+        h_sb = [keep.tile([P, S], F32, name=f"h_sb{m}", tag=f"h{m}", align_bytes=64) for m in range(ROW_TILES)]
+        for g, (first, last) in enumerate(FIRST_GROUPS):
             width = (last - first) * C
             lst = entries(offs_sb, first * C, last * C)
-            xg = keep.tile([P, PASSES, width], U32, name=f"xg{first}", tag="xg", bufs=3, align_bytes=64)
-            sg = keep.tile([P, PASSES, width], U8, name=f"sg{first}", tag="sg", bufs=3, align_bytes=64)
-            for s in range(PASSES):
-                nc.vector.tensor_copy(xg[:, s, :], x_sb[s][:].bitcast(U32).indirect(lst))
+            xg = keep.tile([P, PASSES, width], U32, name=f"xg{g}", tag=f"xg{g}", align_bytes=64)
+            sg = keep.tile([P, PASSES, width], U8, name=f"sg{g}", tag=f"sg{g}", align_bytes=64)
+            nc.vector.tensor_copy(xg[:, 0, :], x_sb[0][:].bitcast(U32).indirect(lst))
             for s in range(PASSES):
                 nc.vector.tensor_copy(sg[:, s, :], x_plane[:, s, :].indirect(lst))
-            for e in range(first, last):
-                cols = slice((e - first) * C, (e - first + 1) * C)
-                if e < E - 1:
-                    first_layer(e, xg, sg, cols, range(ROW_TILES))
-                else:
-                    first_layer(e, xg, sg, cols, range(0, 1))
-                    first_layer(e, xg, sg, cols, range(1, 2))
-                    first_layer(e, xg, sg, cols, range(2, 4))
-            if last in (2, 4):
-                cast_w2(last // 2 - 1, f"pair{last // 2 - 1}")
-                w2_sb.append(load_w2(last // 2 + 1, f"stage{last // 2 - 1}"))
-        cast_w2_vector(2, "x_plane", 1)
-        gate2_sb = keep.tile([P, 2, T], F32, name="gate2_sb", tag="stage0")
-        nc.sync.dma_start(gate2_sb[:], gate2.rearrange("r p t -> p r t"))
+            nc.vector.tensor_copy(xg[:, 1, :], x_sb[1][:].bitcast(U32).indirect(lst))
+            for m in range(ROW_TILES):
+                acc = bank((g * ROW_TILES + m) % 8)
+                for e in range(first, last):
+                    cols = slice((e - first) * C, (e - first + 1) * C)
+                    for s in range(PASSES):
+                        nc.tensor.matmul_mx(
+                            acc[:, cols],
+                            lhsT=w1_sb[g][:, (e - first) * PASSES + s, 2 * m * P : 2 * (m + 1) * P].bitcast(FP4X4),
+                            lhsT_scale=w1_plane[:, e * PASSES + s, m * P : (m + 1) * P],
+                            rhs=xg[:, s, cols].bitcast(FP8X4),
+                            rhs_scale=sg[:, s, cols],
+                            start=(s == 0),
+                            stop=(s == PASSES - 1),
+                        )
+                nc.scalar.copy(h_sb[m][:, first * C : last * C], acc[:, :width])
+            if g == 0:
+                gate1_sb = load_gate("gate1_sb", gate1, "xg0")
+                w2_sb = [load_w2(0, "sg0"), load_w2(1, "w1_0")]
+            if g == 1:
+                gate2_sb = load_gate("gate2_sb", gate2, "xg1")
 
-        c_pairs = keep.tile([P, 2, T, 2], BF16, name="c_pairs", align_bytes=64)
-        turns = []
-        for q in range(TOKEN_BLOCKS):
-            closing = q == TOKEN_BLOCKS - 1
-            backs = [bank("acc", 5), bank("acc", 5)] if closing else [bank("acc", 5)]
-            for r, pos_sb in enumerate((pos1_sb, pos2_sb)):
-                lst = entries(pos_sb, q * P, (q + 1) * P)
-                picked = keep.tile([P, ROW_TILES, P], F32, name=f"picked{q}_{r}", tag="picked", bufs=3, align_bytes=64)
-                gated = keep.tile([P, PACK, P], F32, name=f"gated{q}_{r}", tag=f"gated{q}_{r}", align_bytes=64)
-                runs = (range(0, 3), range(3, 4)) if closing and r == 1 else (range(ROW_TILES),)
-                for run in runs:
-                    turned = bank(f"turned{TURN_BANKS[len(turns)]}", 1)
-                    turns.append(turned)
-                    for k, m in enumerate(run):
-                        nc.vector.tensor_copy(picked[:, m, :], h_sb[:, m, :].indirect(lst))
-                        nc.tensor.transpose(turned[:, k * P : (k + 1) * P], picked[:, m, :], ident[:])
-                    nc.scalar.activation(
-                        gated[:, :, run.start * 32 : run.stop * 32],
-                        turned[:, : len(run) * P].rearrange("t (p j) -> t j p", j=PACK),
-                        COPY,
-                        scale=gate_cols[:, r * TOKEN_BLOCKS + q : r * TOKEN_BLOCKS + q + 1],
-                    )
-                per_bank = PACK // len(backs)
-                for j in range(PACK):
-                    k = j % per_bank
-                    nc.tensor.matmul(
-                        backs[j // per_bank][:, k * P : (k + 1) * P],
-                        gated[:, j, :],
-                        ident[:],
-                        is_transpose=True,
-                        start=(r == 0 and k == 0),
-                        stop=(r == 1 and k == per_bank - 1),
-                    )
-            halves = 2 // len(backs)
-            for b, back in enumerate(backs):
-                nc.scalar.copy(
-                    c_pairs[:, b * halves : (b + 1) * halves, q * P : (q + 1) * P, :],
-                    back[:, : halves * 2 * P].rearrange("p (u d t) -> p u t d", u=halves, d=2),
-                )
-        cast_w2_vector(3, "picked", 3)
-
-        w2_codes = keep.tile([P, E * N], U32, name="w2_codes", tag="h_slot", align_bytes=64)
-        w2_plane = keep.tile([P, E * N], U8, name="w2_plane", align_bytes=64)
-        for g in range(4):
-            cols = slice(2 * g * N, 2 * (g + 1) * N)
-            nc.vector.quantize_mx(
-                out=w2_codes[:, cols].bitcast(FP8X4),
-                scales=w2_plane[:, cols],
-                in_=w2_bf[g][:].rearrange("p e n j -> p (e n j)"),
+        w2_bf = keep.tile([P, E, N, PACK], BF16, name="w2_bf", tag="w1_6", align_bytes=64)
+        for e in range(E):
+            nc.scalar.copy(
+                w2_bf[:, e, :, :].rearrange("p (c i) j -> p c j i", i=4),
+                w2_sb[e // 4][:, e % 4, :, :].rearrange("p j (c i) -> p c j i", i=4),
             )
 
-        c_words = c_pairs[:].rearrange("p u t d -> p u (t d)").bitcast(U32)
+        def gather_and_turn(blocks, tiles, sums):
+            toks = slice(blocks.start * P, blocks.stop * P)
+            for k, m in enumerate(tiles):
+                for r, pos_sb in enumerate((pos1_sb, pos2_sb)):
+                    part = keep.tile([P, len(blocks) * P], F32, name=f"part{m}_{r}", tag=f"part{m}_{r}", align_bytes=64)
+                    nc.vector.tensor_tensor(
+                        part[:], h_sb[m][:].indirect(entries(pos_sb, toks.start, toks.stop)), gate1_sb[:, r, toks], MULT
+                    )
+                    for b in range(len(blocks)):
+                        nc.tensor.matmul(
+                            sums[b][:, k * P : (k + 1) * P],
+                            part[:, b * P : (b + 1) * P],
+                            ident[:],
+                            is_transpose=True,
+                            start=(k == 0 and r == 0),
+                            stop=(k == len(tiles) - 1 and r == 1),
+                        )
+
+        def round_rows(copy, c_rows, total, tiles):
+            copy(
+                c_rows[:, :, tiles.start * 32 : tiles.stop * 32, :],
+                total[:, : len(tiles) * P].rearrange("t (p u d) -> t u p d", u=2, d=2),
+            )
+
+        def turn_back(copy, c_rows, q):
+            back = bank(q)
+            for u in range(2):
+                nc.tensor.transpose(
+                    back[:, u * P : (u + 1) * P], c_rows[:, u, :, :].rearrange("t p d -> t (p d)").bitcast(F32), ident[:]
+                )
+            planes = c_words[:, : 2 * T].rearrange("p (u t) -> p u t", u=2)
+            copy(planes[:, :, q * P : (q + 1) * P], back[:, : 2 * P].rearrange("p (u t) -> p u t", t=P))
+
+        sums = [bank(4 + q) for q in range(3)]
+        gather_and_turn(range(0, 3), range(ROW_TILES), sums)
+        for q in range(3):
+            c_rows = keep.tile([P, 2, P, 2], BF16, name=f"c_rows{q}", align_bytes=64)
+            round_rows(nc.scalar.copy, c_rows, sums[q], range(ROW_TILES))
+            turn_back(nc.scalar.copy, c_rows, q)
+        c_rows = keep.tile([P, 2, P, 2], BF16, name="c_rows3", align_bytes=64)
+        for tiles, index, copy in ((range(0, 3), 5, nc.scalar.copy), (range(3, 4), 6, nc.vector.tensor_copy)):
+            total = bank(index)
+            gather_and_turn(range(3, 4), tiles, [total])
+            round_rows(copy, c_rows, total, tiles)
+        turn_back(nc.vector.tensor_copy, c_rows, 3)
+
+        w2_codes = []
+        w2_plane = keep.tile([P, E * N], U8, name="w2_plane", align_bytes=64)
+        for g, tag in enumerate(("h3", "part3_1")):
+            cols = slice(4 * g * N, 4 * (g + 1) * N)
+            w2_codes.append(keep.tile([P, 4 * N], U32, name=f"w2_codes{g}", tag=tag, align_bytes=64))
+            nc.vector.quantize_mx(
+                out=w2_codes[g][:].bitcast(FP8X4),
+                scales=w2_plane[:, cols],
+                in_=w2_bf[:, 4 * g : 4 * g + 4, :, :].rearrange("p e n j -> p (e n j)"),
+            )
+
+        windows = [c_words[:, u * T : (u + 1) * T + SPARE].bitcast(U32) for u in range(2)]
         y_sb = keep.tile([P, S], F32, name="y_sb")
-        for first, last in SECOND_GROUPS:
+        for g, (first, last) in enumerate(SECOND_GROUPS):
             width = (last - first) * C
             lst = entries(offs2_sb, first * C, last * C)
-            woven = keep.tile([P, width, 2], U32, name=f"woven{first}", align_bytes=64)
             if last < E:
-                cg = keep.tile([P, 2, width], U32, name=f"cg{first}", tag="cg", bufs=3, align_bytes=64)
+                woven = keep.tile([P, width, 2], U32, name=f"woven{first}", align_bytes=64)
+                cg = keep.tile([P, 2, width], U32, name=f"cg{first}", tag="cg", bufs=2, align_bytes=64)
                 for u in range(2):
-                    nc.vector.tensor_copy(cg[:, u, :], c_words[:, u, :].indirect(lst))
+                    nc.vector.tensor_copy(cg[:, u, :], windows[u].indirect(lst))
                 nc.scalar.copy(woven[:], cg[:].rearrange("p u s -> p s u"))
             else:
+                woven = keep.tile([P, width, 2], U32, name=f"woven{first}", tag="cg", bufs=2, align_bytes=64)
                 for u in range(2):
-                    nc.vector.tensor_copy(woven[:, :, u], c_words[:, u, :].indirect(lst))
+                    nc.vector.tensor_copy(woven[:, :, u], windows[u].indirect(lst))
             codes = keep.tile([P, width], U32, name=f"codes{first}", align_bytes=64)
             plane = keep.tile([P, width], U8, name=f"plane{first}", align_bytes=64)
             nc.vector.quantize_mx(
@@ -252,12 +231,12 @@ def tile_moe_ser_none_kernel(
                 scales=plane[:],
                 in_=woven[:].rearrange("p s u -> p (s u)").bitcast(BF16),
             )
-            acc = bank("acc", 5)
+            acc = bank(g)
             for e in range(first, last):
                 cols = slice((e - first) * C, (e - first + 1) * C)
                 nc.tensor.matmul_mx(
                     acc[:, cols],
-                    lhsT=w2_codes[:, e * N : (e + 1) * N].bitcast(FP8X4),
+                    lhsT=w2_codes[e // 4][:, (e % 4) * N : (e % 4 + 1) * N].bitcast(FP8X4),
                     lhsT_scale=w2_plane[:, e * N : (e + 1) * N],
                     rhs=codes[:, cols].bitcast(FP8X4),
                     rhs_scale=plane[:, cols],
@@ -266,15 +245,14 @@ def tile_moe_ser_none_kernel(
                 )
             nc.scalar.copy(y_sb[:, first * C : last * C], acc[:, :width])
 
+        first_part = keep.tile([P, T], F32, name="first_part")
+        nc.vector.tensor_tensor(first_part[:], y_sb[:].indirect(pos3_sb[:]), gate2_sb[:, 0, :], MULT)
         for hh in range(2):
             toks = slice(hh * T // 2, (hh + 1) * T // 2)
-            parts = []
-            for r, pos_sb in enumerate((pos3_sb, pos4_sb)):
-                part = keep.tile([P, T // 2], F32, name=f"part{hh}_{r}")
-                nc.vector.tensor_tensor(
-                    part[:], y_sb[:].indirect(entries(pos_sb, toks.start, toks.stop)), gate2_sb[:, r, toks], MULT
-                )
-                parts.append(part)
+            part = keep.tile([P, T // 2], F32, name=f"second_part{hh}")
+            nc.vector.tensor_tensor(
+                part[:], y_sb[:].indirect(entries(pos4_sb, toks.start, toks.stop)), gate2_sb[:, 1, toks], MULT
+            )
             total = keep.tile([P, T // 2], F32, name=f"total{hh}")
-            nc.vector.tensor_tensor(total[:], parts[0][:], parts[1][:], ADD)
+            nc.vector.tensor_tensor(total[:], first_part[:, toks], part[:], ADD)
             nc.sync.dma_start(out[:, toks], total[:])

@@ -25,8 +25,7 @@ PASSES = K // (P * PACK)
 ROW_TILES = H // P
 TOKEN_BLOCKS = T // P
 FIRST_GROUPS = ((0, 3), (3, 6), (6, 8))
-SECOND_GROUPS = ((0, 4), (4, 6), (6, 7), (7, 8))
-SPARE = 192
+SECOND_GROUPS = ((0, 2), (2, 4), (4, 6), (6, 7), (7, 8))
 
 
 def entries(lst, first, last):
@@ -109,10 +108,11 @@ def tile_moe_ser_none_kernel(
         pos3_sb = load_list("pos3_sb", pos3)
         pos4_sb = load_list("pos4_sb", pos4)
 
+        w2_sb = [load_w2(0, "w2_first")]
+
         ident = keep.tile([P, P], F32, name="ident")
         make_identity(nc, ident[:])
-        c_words = keep.tile([P, 2 * T + SPARE], F32, name="c_words", align_bytes=64)
-        nc.gpsimd.memset(c_words[:, 2 * T :], 0.0)
+        c_words = keep.tile([P, 2, T], F32, name="c_words", align_bytes=64)
 
         h_sb = [keep.tile([P, S], F32, name=f"h_sb{m}", tag=f"h{m}", align_bytes=64) for m in range(ROW_TILES)]
         for g, (first, last) in enumerate(FIRST_GROUPS):
@@ -141,7 +141,7 @@ def tile_moe_ser_none_kernel(
                 nc.scalar.copy(h_sb[m][:, first * C : last * C], acc[:, :width])
             if g == 0:
                 gate1_sb = load_gate("gate1_sb", gate1, "xg0")
-                w2_sb = [load_w2(0, "sg0"), load_w2(1, "w1_0")]
+                w2_sb.append(load_w2(1, "w1_0"))
             if g == 1:
                 gate2_sb = load_gate("gate2_sb", gate2, "xg1")
 
@@ -176,27 +176,27 @@ def tile_moe_ser_none_kernel(
                 total[:, : len(tiles) * P].rearrange("t (p u d) -> t u p d", u=2, d=2),
             )
 
-        def turn_back(copy, c_rows, q):
-            back = bank(q)
+        def turn_back(copy, c_rows, q, index):
+            back = bank(index)
             for u in range(2):
                 nc.tensor.transpose(
                     back[:, u * P : (u + 1) * P], c_rows[:, u, :, :].rearrange("t p d -> t (p d)").bitcast(F32), ident[:]
                 )
-            planes = c_words[:, : 2 * T].rearrange("p (u t) -> p u t", u=2)
-            copy(planes[:, :, q * P : (q + 1) * P], back[:, : 2 * P].rearrange("p (u t) -> p u t", t=P))
+            copy(c_words[:, :, q * P : (q + 1) * P], back[:, : 2 * P].rearrange("p (u t) -> p u t", t=P))
 
-        sums = [bank(4 + q) for q in range(3)]
-        gather_and_turn(range(0, 3), range(ROW_TILES), sums)
-        for q in range(3):
-            c_rows = keep.tile([P, 2, P, 2], BF16, name=f"c_rows{q}", align_bytes=64)
-            round_rows(nc.scalar.copy, c_rows, sums[q], range(ROW_TILES))
-            turn_back(nc.scalar.copy, c_rows, q)
-        c_rows = keep.tile([P, 2, P, 2], BF16, name="c_rows3", align_bytes=64)
-        for tiles, index, copy in ((range(0, 3), 5, nc.scalar.copy), (range(3, 4), 6, nc.vector.tensor_copy)):
+        c_rows = [keep.tile([P, 2, P, 2], BF16, name=f"c_rows{q}", align_bytes=64) for q in range(TOKEN_BLOCKS)]
+        for tiles, indices in ((range(0, 2), (4, 5, 6)), (range(2, 4), (7, 0, 1))):
+            sums = [bank(index) for index in indices]
+            gather_and_turn(range(0, 3), tiles, sums)
+            for q in range(3):
+                round_rows(nc.scalar.copy, c_rows[q], sums[q], tiles)
+                if tiles.stop == ROW_TILES:
+                    turn_back(nc.scalar.copy, c_rows[q], q, 4 + q)
+        for tiles, index, copy in ((range(0, 3), 0, nc.scalar.copy), (range(3, 4), 1, nc.vector.tensor_copy)):
             total = bank(index)
             gather_and_turn(range(3, 4), tiles, [total])
-            round_rows(copy, c_rows, total, tiles)
-        turn_back(nc.vector.tensor_copy, c_rows, 3)
+            round_rows(copy, c_rows[3], total, tiles)
+        turn_back(nc.vector.tensor_copy, c_rows[3], 3, 2)
 
         w2_codes = []
         w2_plane = keep.tile([P, E * N], U8, name="w2_plane", align_bytes=64)
@@ -209,7 +209,7 @@ def tile_moe_ser_none_kernel(
                 in_=w2_bf[:, 4 * g : 4 * g + 4, :, :].rearrange("p e n j -> p (e n j)"),
             )
 
-        windows = [c_words[:, u * T : (u + 1) * T + SPARE].bitcast(U32) for u in range(2)]
+        windows = [c_words[:, u, :].bitcast(U32) for u in range(2)]
         y_sb = keep.tile([P, S], F32, name="y_sb")
         for g, (first, last) in enumerate(SECOND_GROUPS):
             width = (last - first) * C
@@ -231,7 +231,7 @@ def tile_moe_ser_none_kernel(
                 scales=plane[:],
                 in_=woven[:].rearrange("p s u -> p (s u)").bitcast(BF16),
             )
-            acc = bank(g)
+            acc = bank(3 + g)
             for e in range(first, last):
                 cols = slice((e - first) * C, (e - first + 1) * C)
                 nc.tensor.matmul_mx(

@@ -50,24 +50,19 @@ def tile_moe_ser_none_kernel(
 
         x_plane = keep.tile([P, PASSES, T], U8, name="x_plane", align_bytes=64)
         w1_plane = keep.tile([P, E * PASSES, H], U8, name="w1_plane", align_bytes=64)
-        nc.vector.memset(x_plane[:].rearrange("p s t -> p (s t)").bitcast(I32), 0)
+        nc.gpsimd.memset(x_plane[:].rearrange("p s t -> p (s t)").bitcast(I32), 0)
         w1_plane_words = w1_plane[:].rearrange("p g i -> p (g i)").bitcast(I32)
         early = FIRST_GROUPS[0][1] * PASSES * H // 4
-        nc.gpsimd.memset(w1_plane_words[:, : early // 2], 0)
-        nc.vector.memset(w1_plane_words[:, early // 2 : early], 0)
+        nc.vector.memset(w1_plane_words[:, :early], 0)
         nc.vector.memset(w1_plane_words[:, early:], 0)
 
-        def load_x(s):
-            words = keep.tile([P, T], I32, name=f"x_sb{s}", align_bytes=64)
-            nc.sync.dma_start(words[:], x_words[s].rearrange("p t d -> p (t d)").bitcast(I32))
-            return words
-
-        x_sb = [load_x(0)]
+        x_sb = keep.tile([P, PASSES, T], I32, name="x_sb", align_bytes=64)
+        nc.scalar.dma_start(x_sb[:], x_words.rearrange("s p t d -> p s (t d)").bitcast(I32))
+        pos1_sb = load_list("pos1_sb", pos1)
         x_rows = x_scales.rearrange("s (q r) t -> r q s t", r=4)
         for r in range(4):
             nc.sync.dma_start(x_plane[r:P:32, :, :].bitcast(I32), x_rows[r].bitcast(I32))
         offs_sb = load_list("offs_sb", offs)
-        x_sb.append(load_x(1))
         w1_rows = w1_scales.rearrange("e s (q r) i -> r q (e s) i", r=4)
 
         def load_w1_scales(first, last):
@@ -102,105 +97,127 @@ def tile_moe_ser_none_kernel(
         w1_sb.append(load_w1(*FIRST_GROUPS[1]))
         load_w1_scales(FIRST_GROUPS[0][1], E)
         w1_sb.append(load_w1(*FIRST_GROUPS[2]))
-        pos1_sb = load_list("pos1_sb", pos1)
         pos2_sb = load_list("pos2_sb", pos2)
+        gate1_sb = load_gate("gate1_sb", gate1, "gate1")
+        w2_sb = [load_w2(0, "w2_first"), load_w2(1, "w2_second")]
         offs2_sb = load_list("offs2_sb", offs2)
+        gate2_sb = load_gate("gate2_sb", gate2, "gate2")
         pos3_sb = load_list("pos3_sb", pos3)
         pos4_sb = load_list("pos4_sb", pos4)
-
-        w2_sb = [load_w2(0, "w2_first")]
 
         ident = keep.tile([P, P], F32, name="ident")
         make_identity(nc, ident[:])
         c_words = keep.tile([P, 2, T], F32, name="c_words", align_bytes=64)
 
         h_sb = [keep.tile([P, S], F32, name=f"h_sb{m}", tag=f"h{m}", align_bytes=64) for m in range(ROW_TILES)]
+        def first_layer(g, m, first, last, index, copy):
+            start = FIRST_GROUPS[g][0]
+            acc = bank(index)
+            for e in range(first, last):
+                cols = slice((e - start) * C, (e - start + 1) * C)
+                for s in range(PASSES):
+                    nc.tensor.matmul_mx(
+                        acc[:, (e - first) * C : (e - first + 1) * C],
+                        lhsT=w1_sb[g][:, (e - start) * PASSES + s, 2 * m * P : 2 * (m + 1) * P].bitcast(FP4X4),
+                        lhsT_scale=w1_plane[:, e * PASSES + s, m * P : (m + 1) * P],
+                        rhs=xg[g][:, s, cols].bitcast(FP8X4),
+                        rhs_scale=sg[g][:, s, cols],
+                        start=(s == 0),
+                        stop=(s == PASSES - 1),
+                    )
+            copy(h_sb[m][:, first * C : last * C], acc[:, : (last - first) * C])
+
+        xg, sg = [], []
         for g, (first, last) in enumerate(FIRST_GROUPS):
             width = (last - first) * C
             lst = entries(offs_sb, first * C, last * C)
-            xg = keep.tile([P, PASSES, width], U32, name=f"xg{g}", tag=f"xg{g}", align_bytes=64)
-            sg = keep.tile([P, PASSES, width], U8, name=f"sg{g}", tag=f"sg{g}", align_bytes=64)
-            nc.vector.tensor_copy(xg[:, 0, :], x_sb[0][:].bitcast(U32).indirect(lst))
+            xg.append(keep.tile([P, PASSES, width], U32, name=f"xg{g}", align_bytes=64))
+            sg.append(keep.tile([P, PASSES, width], U8, name=f"sg{g}", align_bytes=64))
             for s in range(PASSES):
-                nc.vector.tensor_copy(sg[:, s, :], x_plane[:, s, :].indirect(lst))
-            nc.vector.tensor_copy(xg[:, 1, :], x_sb[1][:].bitcast(U32).indirect(lst))
-            for m in range(ROW_TILES):
-                acc = bank((g * ROW_TILES + m) % 8)
+                nc.vector.tensor_copy(sg[g][:, s, :], x_plane[:, s, :].indirect(lst))
+            nc.vector.tensor_copy(xg[g][:, 0, :], x_sb[:, 0, :].bitcast(U32).indirect(lst))
+            if last < E:
+                nc.vector.tensor_copy(xg[g][:, 1, :], x_sb[:, 1, :].bitcast(U32).indirect(lst))
+                for m in range(ROW_TILES):
+                    first_layer(g, m, first, last, (g * ROW_TILES + m) % 8, nc.scalar.copy)
+            else:
                 for e in range(first, last):
-                    cols = slice((e - first) * C, (e - first + 1) * C)
-                    for s in range(PASSES):
-                        nc.tensor.matmul_mx(
-                            acc[:, cols],
-                            lhsT=w1_sb[g][:, (e - first) * PASSES + s, 2 * m * P : 2 * (m + 1) * P].bitcast(FP4X4),
-                            lhsT_scale=w1_plane[:, e * PASSES + s, m * P : (m + 1) * P],
-                            rhs=xg[:, s, cols].bitcast(FP8X4),
-                            rhs_scale=sg[:, s, cols],
-                            start=(s == 0),
-                            stop=(s == PASSES - 1),
-                        )
-                nc.scalar.copy(h_sb[m][:, first * C : last * C], acc[:, :width])
-            if g == 0:
-                gate1_sb = load_gate("gate1_sb", gate1, "xg0")
-                w2_sb.append(load_w2(1, "w1_0"))
-            if g == 1:
-                gate2_sb = load_gate("gate2_sb", gate2, "xg1")
+                    nc.vector.tensor_copy(
+                        xg[g][:, 1, (e - first) * C : (e - first + 1) * C],
+                        x_sb[:, 1, :].bitcast(U32).indirect(entries(offs_sb, e * C, (e + 1) * C)),
+                    )
+                first_layer(g, 0, first, last - 1, 0, nc.scalar.copy)
+                first_layer(g, 0, last - 1, last, 1, nc.vector.tensor_copy)
+                for m in range(1, ROW_TILES):
+                    first_layer(g, m, first, last, 1 + m, nc.scalar.copy)
 
-        w2_bf = keep.tile([P, E, N, PACK], BF16, name="w2_bf", tag="w1_6", align_bytes=64)
+        w2_bf = keep.tile([P, E, N, PACK], BF16, name="w2_bf", align_bytes=64)
         for e in range(E):
             nc.scalar.copy(
                 w2_bf[:, e, :, :].rearrange("p (c i) j -> p c j i", i=4),
                 w2_sb[e // 4][:, e % 4, :, :].rearrange("p j (c i) -> p c j i", i=4),
             )
 
-        def gather_and_turn(blocks, tiles, sums):
+        def gather_and_turn(blocks, tiles, total):
             toks = slice(blocks.start * P, blocks.stop * P)
             for k, m in enumerate(tiles):
                 for r, pos_sb in enumerate((pos1_sb, pos2_sb)):
-                    part = keep.tile([P, len(blocks) * P], F32, name=f"part{m}_{r}", tag=f"part{m}_{r}", align_bytes=64)
+                    part = keep.tile([P, len(blocks) * P], F32, name=f"part{m}_{r}_{blocks.start}", align_bytes=64)
                     nc.vector.tensor_tensor(
                         part[:], h_sb[m][:].indirect(entries(pos_sb, toks.start, toks.stop)), gate1_sb[:, r, toks], MULT
                     )
                     for b in range(len(blocks)):
+                        place = b * len(tiles) + k
                         nc.tensor.matmul(
-                            sums[b][:, k * P : (k + 1) * P],
+                            total[:, place * P : (place + 1) * P],
                             part[:, b * P : (b + 1) * P],
                             ident[:],
                             is_transpose=True,
-                            start=(k == 0 and r == 0),
-                            stop=(k == len(tiles) - 1 and r == 1),
+                            start=(k == 0 and r == 0 and b == 0),
+                            stop=(k == len(tiles) - 1 and r == 1 and b == len(blocks) - 1),
                         )
 
-        def round_rows(copy, c_rows, total, tiles):
+        def round_rows(copy, c_rows, total, blocks, tiles):
             copy(
-                c_rows[:, :, tiles.start * 32 : tiles.stop * 32, :],
-                total[:, : len(tiles) * P].rearrange("t (p u d) -> t u p d", u=2, d=2),
+                c_rows[:, :, :, tiles.start * 32 : tiles.stop * 32, :],
+                total[:, : len(blocks) * len(tiles) * P].rearrange("t (q p u d) -> t q u p d", q=len(blocks), u=2, d=2),
             )
 
-        def turn_back(copy, c_rows, q, index):
-            back = bank(index)
-            for u in range(2):
-                nc.tensor.transpose(
-                    back[:, u * P : (u + 1) * P], c_rows[:, u, :, :].rearrange("t p d -> t (p d)").bitcast(F32), ident[:]
-                )
-            copy(c_words[:, :, q * P : (q + 1) * P], back[:, : 2 * P].rearrange("p (u t) -> p u t", t=P))
+        def turn_back(copy, c_rows, token_block, halves, back):
+            for k in range(c_rows.shape[1]):
+                for j, u in enumerate(halves):
+                    place = j * c_rows.shape[1] + k
+                    nc.tensor.transpose(
+                        back[:, place * P : (place + 1) * P],
+                        c_rows[:, k, u, :, :].rearrange("t p d -> t (p d)").bitcast(F32),
+                        ident[:],
+                    )
+            width = c_rows.shape[1] * P
+            copy(
+                c_words[:, halves.start : halves.stop, token_block * P : token_block * P + width],
+                back[:, : len(halves) * width].rearrange("p (u t) -> p u t", t=width),
+            )
 
-        c_rows = [keep.tile([P, 2, P, 2], BF16, name=f"c_rows{q}", align_bytes=64) for q in range(TOKEN_BLOCKS)]
-        for tiles, indices in ((range(0, 2), (4, 5, 6)), (range(2, 4), (7, 0, 1))):
-            sums = [bank(index) for index in indices]
-            gather_and_turn(range(0, 3), tiles, sums)
-            for q in range(3):
-                round_rows(nc.scalar.copy, c_rows[q], sums[q], tiles)
-                if tiles.stop == ROW_TILES:
-                    turn_back(nc.scalar.copy, c_rows[q], q, 4 + q)
-        for tiles, index, copy in ((range(0, 3), 0, nc.scalar.copy), (range(3, 4), 1, nc.vector.tensor_copy)):
+        c_rows = keep.tile([P, TOKEN_BLOCKS, 2, P, 2], BF16, name="c_rows", tag="w2_second", align_bytes=64)
+        for m, index in enumerate((5, 6, 7)):
             total = bank(index)
-            gather_and_turn(range(3, 4), tiles, [total])
-            round_rows(copy, c_rows[3], total, tiles)
-        turn_back(nc.vector.tensor_copy, c_rows[3], 3, 2)
+            gather_and_turn(range(0, 4), range(m, m + 1), total)
+            round_rows(nc.scalar.copy, c_rows[:], total, range(0, 4), range(m, m + 1))
+        last_tile = range(3, 4)
+        for blocks, index in ((range(0, 2), 0), (range(2, 3), 2)):
+            total = bank(index)
+            gather_and_turn(blocks, last_tile, total)
+            round_rows(nc.scalar.copy, c_rows[:, blocks.start : blocks.stop], total, blocks, last_tile)
+            turn_back(nc.scalar.copy, c_rows[:, blocks.start : blocks.stop], blocks.start, range(0, 2), bank(index + 1))
+        total = bank(0)
+        gather_and_turn(range(3, 4), last_tile, total)
+        round_rows(nc.vector.tensor_copy, c_rows[:, 3:4], total, range(3, 4), last_tile)
+        turn_back(nc.vector.tensor_copy, c_rows[:, 3:4], 3, range(0, 1), bank(4))
+        turn_back(nc.scalar.copy, c_rows[:, 3:4], 3, range(1, 2), bank(5))
 
         w2_codes = []
         w2_plane = keep.tile([P, E * N], U8, name="w2_plane", align_bytes=64)
-        for g, tag in enumerate(("h3", "part3_1")):
+        for g, tag in enumerate(("h3", "part3_1_3")):
             cols = slice(4 * g * N, 4 * (g + 1) * N)
             w2_codes.append(keep.tile([P, 4 * N], U32, name=f"w2_codes{g}", tag=tag, align_bytes=64))
             nc.vector.quantize_mx(
@@ -231,7 +248,7 @@ def tile_moe_ser_none_kernel(
                 scales=plane[:],
                 in_=woven[:].rearrange("p s u -> p (s u)").bitcast(BF16),
             )
-            acc = bank(3 + g)
+            acc = bank((6 + g) % 8)
             for e in range(first, last):
                 cols = slice((e - first) * C, (e - first + 1) * C)
                 nc.tensor.matmul_mx(
@@ -247,12 +264,14 @@ def tile_moe_ser_none_kernel(
 
         first_part = keep.tile([P, T], F32, name="first_part")
         nc.vector.tensor_tensor(first_part[:], y_sb[:].indirect(pos3_sb[:]), gate2_sb[:, 0, :], MULT)
-        for hh in range(2):
-            toks = slice(hh * T // 2, (hh + 1) * T // 2)
-            part = keep.tile([P, T // 2], F32, name=f"second_part{hh}")
+        halves = (slice(0, T // 2), slice(T // 2, T))
+        parts = []
+        for hh, toks in enumerate(halves):
+            parts.append(keep.tile([P, T // 2], F32, name=f"second_part{hh}"))
             nc.vector.tensor_tensor(
-                part[:], y_sb[:].indirect(entries(pos4_sb, toks.start, toks.stop)), gate2_sb[:, 1, toks], MULT
+                parts[hh][:], y_sb[:].indirect(entries(pos4_sb, toks.start, toks.stop)), gate2_sb[:, 1, toks], MULT
             )
+        for hh, toks in enumerate(halves):
             total = keep.tile([P, T // 2], F32, name=f"total{hh}")
-            nc.vector.tensor_tensor(total[:], first_part[:, toks], part[:], ADD)
+            nc.vector.tensor_tensor(total[:], first_part[:, toks], parts[hh][:], ADD)
             nc.sync.dma_start(out[:, toks], total[:])

@@ -58,7 +58,8 @@ def tile_moe_ser_none_kernel(
 
         x_sb = keep.tile([P, PASSES, T], I32, name="x_sb", align_bytes=64)
         nc.scalar.dma_start(x_sb[:], x_words.rearrange("s p t d -> p s (t d)").bitcast(I32))
-        pos1_sb = load_list("pos1_sb", pos1)
+        gate1_cols = keep.tile([P, 2, PACK], F32, name="gate1_cols")
+        nc.sync.dma_start(gate1_cols[:], gate1[:, 0, :].rearrange("r (p j) -> p r j", j=PACK))
         x_rows = x_scales.rearrange("s (q r) t -> r q s t", r=4)
         for r in range(4):
             nc.sync.dma_start(x_plane[r:P:32, :, :].bitcast(I32), x_rows[r].bitcast(I32))
@@ -97,8 +98,8 @@ def tile_moe_ser_none_kernel(
         w1_sb.append(load_w1(*FIRST_GROUPS[1]))
         load_w1_scales(FIRST_GROUPS[0][1], E)
         w1_sb.append(load_w1(*FIRST_GROUPS[2]))
+        pos1_sb = load_list("pos1_sb", pos1)
         pos2_sb = load_list("pos2_sb", pos2)
-        gate1_sb = load_gate("gate1_sb", gate1, "gate1")
         w2_sb = [load_w2(0, "w2_first"), load_w2(1, "w2_second")]
         offs2_sb = load_list("offs2_sb", offs2)
         gate2_sb = load_gate("gate2_sb", gate2, "gate2")
@@ -108,6 +109,17 @@ def tile_moe_ser_none_kernel(
         ident = keep.tile([P, P], F32, name="ident")
         make_identity(nc, ident[:])
         c_words = keep.tile([P, 2, T], F32, name="c_words", align_bytes=64)
+
+        gate1_sb = keep.tile([P, 2, T], F32, name="gate1_sb", align_bytes=64)
+        for r in range(2):
+            spread = bank(6 + r)
+            for j in range(PACK):
+                nc.tensor.transpose(
+                    spread[:, j * P : (j + 1) * P], gate1_cols[:, r, j : j + 1].to_broadcast([P, P]), ident[:]
+                )
+            nc.scalar.copy(
+                gate1_sb[:, r, :].rearrange("m (p j) -> m p j", j=PACK), spread[:].rearrange("m (j p) -> m p j", j=PACK)
+            )
 
         h_sb = [keep.tile([P, S], F32, name=f"h_sb{m}", tag=f"h{m}", align_bytes=64) for m in range(ROW_TILES)]
         def first_layer(g, m, first, last, index, copy):

@@ -24,7 +24,9 @@ PACK = 4
 PASSES = K // (P * PACK)
 ROW_TILES = H // P
 TOKEN_BLOCKS = T // P
-FIRST_GROUPS = ((0, 3), (3, 6), (6, 8))
+FIRST_GROUPS = ((0, 4), (4, 8))
+SPARE = 192
+WINDOW = T + SPARE
 SECOND_GROUPS = ((0, 2), (2, 4), (4, 6), (6, 7), (7, 8))
 
 
@@ -48,21 +50,27 @@ def tile_moe_ser_none_kernel(
             nc.sync.dma_start(lst[:], src)
             return lst
 
-        x_plane = keep.tile([P, PASSES, T], U8, name="x_plane", align_bytes=64)
+        x_plane = keep.tile([P, PASSES * T + SPARE], U8, name="x_plane", align_bytes=64)
         w1_plane = keep.tile([P, E * PASSES, H], U8, name="w1_plane", align_bytes=64)
-        nc.gpsimd.memset(x_plane[:].rearrange("p s t -> p (s t)").bitcast(I32), 0)
+        nc.gpsimd.memset(x_plane[:].bitcast(I32), 0)
         w1_plane_words = w1_plane[:].rearrange("p g i -> p (g i)").bitcast(I32)
         early = FIRST_GROUPS[0][1] * PASSES * H // 4
         nc.vector.memset(w1_plane_words[:, :early], 0)
         nc.vector.memset(w1_plane_words[:, early:], 0)
 
-        x_sb = keep.tile([P, PASSES, T], I32, name="x_sb", align_bytes=64)
-        nc.scalar.dma_start(x_sb[:], x_words.rearrange("s p t d -> p s (t d)").bitcast(I32))
+        x_sb = keep.tile([P, PASSES * T + SPARE], I32, name="x_sb", align_bytes=64)
+        nc.vector.memset(x_sb[:, PASSES * T :], 0)
+        nc.scalar.dma_start(
+            x_sb[:, : PASSES * T].rearrange("p (s t) -> p s t", s=PASSES),
+            x_words.rearrange("s p t d -> p s (t d)").bitcast(I32),
+        )
         gate1_cols = keep.tile([P, 2, PACK], F32, name="gate1_cols")
         nc.sync.dma_start(gate1_cols[:], gate1[:, 0, :].rearrange("r (p j) -> p r j", j=PACK))
         x_rows = x_scales.rearrange("s (q r) t -> r q s t", r=4)
         for r in range(4):
-            nc.sync.dma_start(x_plane[r:P:32, :, :].bitcast(I32), x_rows[r].bitcast(I32))
+            nc.sync.dma_start(
+                x_plane[r:P:32, : PASSES * T].rearrange("p (s t) -> p s t", s=PASSES).bitcast(I32), x_rows[r].bitcast(I32)
+            )
         offs_sb = load_list("offs_sb", offs)
         w1_rows = w1_scales.rearrange("e s (q r) i -> r q (e s) i", r=4)
 
@@ -97,7 +105,6 @@ def tile_moe_ser_none_kernel(
         load_w1_scales(*FIRST_GROUPS[0])
         w1_sb.append(load_w1(*FIRST_GROUPS[1]))
         load_w1_scales(FIRST_GROUPS[0][1], E)
-        w1_sb.append(load_w1(*FIRST_GROUPS[2]))
         pos1_sb = load_list("pos1_sb", pos1)
         pos2_sb = load_list("pos2_sb", pos2)
         w2_sb = [load_w2(0, "w2_first"), load_w2(1, "w2_second")]
@@ -125,17 +132,17 @@ def tile_moe_ser_none_kernel(
         def first_layer(g, m, first, last, index, copy):
             start = FIRST_GROUPS[g][0]
             acc = bank(index)
-            for e in range(first, last):
-                cols = slice((e - start) * C, (e - start + 1) * C)
-                for s in range(PASSES):
+            for s in range(PASSES):
+                for e in range(first, last):
+                    cols = slice((e - start) * C, (e - start + 1) * C)
                     nc.tensor.matmul_mx(
                         acc[:, (e - first) * C : (e - first + 1) * C],
                         lhsT=w1_sb[g][:, (e - start) * PASSES + s, 2 * m * P : 2 * (m + 1) * P].bitcast(FP4X4),
                         lhsT_scale=w1_plane[:, e * PASSES + s, m * P : (m + 1) * P],
                         rhs=xg[g][:, s, cols].bitcast(FP8X4),
                         rhs_scale=sg[g][:, s, cols],
-                        start=(s == 0),
-                        stop=(s == PASSES - 1),
+                        start=(s == 0 and e == first),
+                        stop=(s == PASSES - 1 and e == last - 1),
                     )
             copy(h_sb[m][:, first * C : last * C], acc[:, : (last - first) * C])
 
@@ -146,22 +153,22 @@ def tile_moe_ser_none_kernel(
             xg.append(keep.tile([P, PASSES, width], U32, name=f"xg{g}", align_bytes=64))
             sg.append(keep.tile([P, PASSES, width], U8, name=f"sg{g}", align_bytes=64))
             for s in range(PASSES):
-                nc.vector.tensor_copy(sg[g][:, s, :], x_plane[:, s, :].indirect(lst))
-            nc.vector.tensor_copy(xg[g][:, 0, :], x_sb[:, 0, :].bitcast(U32).indirect(lst))
+                nc.vector.tensor_copy(sg[g][:, s, :], x_plane[:, s * T : s * T + WINDOW].indirect(lst))
+            nc.vector.tensor_copy(xg[g][:, 0, :], x_sb[:, :WINDOW].bitcast(U32).indirect(lst))
             if last < E:
-                nc.vector.tensor_copy(xg[g][:, 1, :], x_sb[:, 1, :].bitcast(U32).indirect(lst))
+                nc.vector.tensor_copy(xg[g][:, 1, :], x_sb[:, T:].bitcast(U32).indirect(lst))
                 for m in range(ROW_TILES):
-                    first_layer(g, m, first, last, (g * ROW_TILES + m) % 8, nc.scalar.copy)
+                    first_layer(g, m, first, last, m, nc.scalar.copy)
             else:
-                for e in range(first, last):
+                for lo, hi in ((first, last - 1), (last - 1, last)):
                     nc.vector.tensor_copy(
-                        xg[g][:, 1, (e - first) * C : (e - first + 1) * C],
-                        x_sb[:, 1, :].bitcast(U32).indirect(entries(offs_sb, e * C, (e + 1) * C)),
+                        xg[g][:, 1, (lo - first) * C : (hi - first) * C],
+                        x_sb[:, T:].bitcast(U32).indirect(entries(offs_sb, lo * C, hi * C)),
                     )
-                first_layer(g, 0, first, last - 1, 0, nc.scalar.copy)
-                first_layer(g, 0, last - 1, last, 1, nc.vector.tensor_copy)
+                first_layer(g, 0, first, last - 1, 4, nc.vector.tensor_copy)
+                first_layer(g, 0, last - 1, last, 5, nc.scalar.copy)
                 for m in range(1, ROW_TILES):
-                    first_layer(g, m, first, last, 1 + m, nc.scalar.copy)
+                    first_layer(g, m, first, last, (5 + m) % 8, nc.scalar.copy)
 
         w2_bf = keep.tile([P, E, N, PACK], BF16, name="w2_bf", align_bytes=64)
         for e in range(E):
@@ -211,21 +218,21 @@ def tile_moe_ser_none_kernel(
             )
 
         c_rows = keep.tile([P, TOKEN_BLOCKS, 2, P, 2], BF16, name="c_rows", tag="w2_second", align_bytes=64)
-        for m, index in enumerate((5, 6, 7)):
+        for m, index in enumerate((1, 2, 3)):
             total = bank(index)
             gather_and_turn(range(0, 4), range(m, m + 1), total)
             round_rows(nc.scalar.copy, c_rows[:], total, range(0, 4), range(m, m + 1))
         last_tile = range(3, 4)
-        for blocks, index in ((range(0, 2), 0), (range(2, 3), 2)):
+        for blocks, index in ((range(0, 2), 4), (range(2, 3), 6)):
             total = bank(index)
             gather_and_turn(blocks, last_tile, total)
             round_rows(nc.scalar.copy, c_rows[:, blocks.start : blocks.stop], total, blocks, last_tile)
             turn_back(nc.scalar.copy, c_rows[:, blocks.start : blocks.stop], blocks.start, range(0, 2), bank(index + 1))
-        total = bank(0)
+        total = bank(4)
         gather_and_turn(range(3, 4), last_tile, total)
         round_rows(nc.vector.tensor_copy, c_rows[:, 3:4], total, range(3, 4), last_tile)
-        turn_back(nc.vector.tensor_copy, c_rows[:, 3:4], 3, range(0, 1), bank(4))
-        turn_back(nc.scalar.copy, c_rows[:, 3:4], 3, range(1, 2), bank(5))
+        turn_back(nc.vector.tensor_copy, c_rows[:, 3:4], 3, range(0, 1), bank(0))
+        turn_back(nc.scalar.copy, c_rows[:, 3:4], 3, range(1, 2), bank(1))
 
         w2_codes = []
         w2_plane = keep.tile([P, E * N], U8, name="w2_plane", align_bytes=64)
@@ -260,7 +267,7 @@ def tile_moe_ser_none_kernel(
                 scales=plane[:],
                 in_=woven[:].rearrange("p s u -> p (s u)").bitcast(BF16),
             )
-            acc = bank((6 + g) % 8)
+            acc = bank(2 + g)
             for e in range(first, last):
                 cols = slice((e - first) * C, (e - first + 1) * C)
                 nc.tensor.matmul_mx(
@@ -279,11 +286,11 @@ def tile_moe_ser_none_kernel(
         halves = (slice(0, T // 2), slice(T // 2, T))
         parts = []
         for hh, toks in enumerate(halves):
-            parts.append(keep.tile([P, T // 2], F32, name=f"second_part{hh}"))
+            parts.append(keep.tile([P, toks.stop - toks.start], F32, name=f"second_part{hh}"))
             nc.vector.tensor_tensor(
                 parts[hh][:], y_sb[:].indirect(entries(pos4_sb, toks.start, toks.stop)), gate2_sb[:, 1, toks], MULT
             )
         for hh, toks in enumerate(halves):
-            total = keep.tile([P, T // 2], F32, name=f"total{hh}")
+            total = keep.tile([P, toks.stop - toks.start], F32, name=f"total{hh}")
             nc.vector.tensor_tensor(total[:], first_part[:, toks], parts[hh][:], ADD)
             nc.sync.dma_start(out[:, toks], total[:])

@@ -79,14 +79,16 @@ def tile_moe_ser_none_kernel(
             for r in range(4):
                 nc.sync.dma_start(w1_plane[r:P:32, groups, :].bitcast(I32), w1_rows[r][:, groups, :].bitcast(I32))
 
-        def load_w1(first, last):
+        def load_w1(first, last, tiles):
+            width = 2 * P * len(tiles)
             words = keep.tile(
-                [P, (last - first) * PASSES, 2 * H], U8, name=f"w1_sb{first}", tag=f"w1_{first}", align_bytes=64
+                [P, (last - first) * PASSES, width], U8, name=f"w1_sb{first}_{tiles.start}", align_bytes=64
             )
+            rows = w1_words[first:last].rearrange("e s p b -> p (e s) b")
             nc.sync.dma_start(
-                words[:].bitcast(I32), w1_words[first:last].rearrange("e s p b -> p (e s) b").bitcast(I32)
+                words[:].bitcast(I32), rows[:, :, 2 * P * tiles.start : 2 * P * tiles.stop].bitcast(I32)
             )
-            return words
+            return [words[:, :, 2 * P * k : 2 * P * (k + 1)] for k in range(len(tiles))]
 
         def load_w2(half, tag):
             raw = keep.tile([P, E // 2, PACK, N], F32, name=f"w2_sb{half}", tag=tag, align_bytes=64)
@@ -101,10 +103,11 @@ def tile_moe_ser_none_kernel(
             nc.sync.dma_start(rows[:], src.rearrange("r p t -> p r t"))
             return rows
 
-        w1_sb = [load_w1(*FIRST_GROUPS[0])]
+        w1_sb = [load_w1(*FIRST_GROUPS[0], range(0, 4))]
         load_w1_scales(*FIRST_GROUPS[0])
-        w1_sb.append(load_w1(*FIRST_GROUPS[1]))
+        w1_sb.append(load_w1(*FIRST_GROUPS[1], range(0, 2)))
         load_w1_scales(FIRST_GROUPS[0][1], E)
+        w1_sb[1].extend(load_w1(*FIRST_GROUPS[1], range(2, 4)))
         pos1_sb = load_list("pos1_sb", pos1)
         pos2_sb = load_list("pos2_sb", pos2)
         w2_sb = [load_w2(0, "w2_first"), load_w2(1, "w2_second")]
@@ -137,7 +140,7 @@ def tile_moe_ser_none_kernel(
                     cols = slice((e - start) * C, (e - start + 1) * C)
                     nc.tensor.matmul_mx(
                         acc[:, (e - first) * C : (e - first + 1) * C],
-                        lhsT=w1_sb[g][:, (e - start) * PASSES + s, 2 * m * P : 2 * (m + 1) * P].bitcast(FP4X4),
+                        lhsT=w1_sb[g][m][:, (e - start) * PASSES + s, :].bitcast(FP4X4),
                         lhsT_scale=w1_plane[:, e * PASSES + s, m * P : (m + 1) * P],
                         rhs=xg[g][:, s, cols].bitcast(FP8X4),
                         rhs_scale=sg[g][:, s, cols],
@@ -170,12 +173,16 @@ def tile_moe_ser_none_kernel(
                 for m in range(1, ROW_TILES):
                     first_layer(g, m, first, last, (5 + m) % 8, nc.scalar.copy)
 
-        w2_bf = keep.tile([P, E, N, PACK], BF16, name="w2_bf", align_bytes=64)
-        for e in range(E):
-            nc.scalar.copy(
-                w2_bf[:, e, :, :].rearrange("p (c i) j -> p c j i", i=4),
-                w2_sb[e // 4][:, e % 4, :, :].rearrange("p j (c i) -> p c j i", i=4),
-            )
+        def round_w2(half, tag):
+            grouped = keep.tile([P, E // 2, N, PACK], BF16, name=f"w2_bf{half}", tag=tag, align_bytes=64)
+            for e in range(E // 2):
+                nc.scalar.copy(
+                    grouped[:, e, :, :].rearrange("p (c i) j -> p c j i", i=4),
+                    w2_sb[half][:, e, :, :].rearrange("p j (c i) -> p c j i", i=4),
+                )
+            return grouped
+
+        w2_bf = [round_w2(0, "w2_bf0")]
 
         def gather_and_turn(blocks, tiles, total):
             toks = slice(blocks.start * P, blocks.stop * P)
@@ -217,11 +224,13 @@ def tile_moe_ser_none_kernel(
                 back[:, : len(halves) * width].rearrange("p (u t) -> p u t", t=width),
             )
 
-        c_rows = keep.tile([P, TOKEN_BLOCKS, 2, P, 2], BF16, name="c_rows", tag="w2_second", align_bytes=64)
+        c_rows = keep.tile([P, TOKEN_BLOCKS, 2, P, 2], BF16, name="c_rows", tag="w2_first", align_bytes=64)
         for m, index in enumerate((1, 2, 3)):
             total = bank(index)
             gather_and_turn(range(0, 4), range(m, m + 1), total)
             round_rows(nc.scalar.copy, c_rows[:], total, range(0, 4), range(m, m + 1))
+            if m == 1:
+                w2_bf.append(round_w2(1, "part1_1_0"))
         last_tile = range(3, 4)
         for blocks, index in ((range(0, 2), 4), (range(2, 3), 6)):
             total = bank(index)
@@ -242,7 +251,7 @@ def tile_moe_ser_none_kernel(
             nc.vector.quantize_mx(
                 out=w2_codes[g][:].bitcast(FP8X4),
                 scales=w2_plane[:, cols],
-                in_=w2_bf[:, 4 * g : 4 * g + 4, :, :].rearrange("p e n j -> p (e n j)"),
+                in_=w2_bf[g][:].rearrange("p e n j -> p (e n j)"),
             )
 
         windows = [c_words[:, u, :].bitcast(U32) for u in range(2)]

@@ -27,6 +27,7 @@ TOKEN_BLOCKS = T // P
 FIRST_GROUPS = ((0, 4), (4, 8))
 SPARE = 192
 WINDOW = T + SPARE
+PLANE_WINDOW = 1408
 SECOND_GROUPS = ((0, 2), (2, 4), (4, 6), (6, 7), (7, 8))
 
 
@@ -50,7 +51,7 @@ def tile_moe_ser_none_kernel(
             nc.sync.dma_start(lst[:], src)
             return lst
 
-        x_plane = keep.tile([P, PASSES * T + SPARE], U8, name="x_plane", align_bytes=64)
+        x_plane = keep.tile([P, T + PLANE_WINDOW], U8, name="x_plane", align_bytes=64)
         w1_plane = keep.tile([P, E * PASSES, H], U8, name="w1_plane", align_bytes=64)
         nc.gpsimd.memset(x_plane[:].bitcast(I32), 0)
         w1_plane_words = w1_plane[:].rearrange("p g i -> p (g i)").bitcast(I32)
@@ -60,10 +61,6 @@ def tile_moe_ser_none_kernel(
 
         x_sb = keep.tile([P, PASSES * T + SPARE], I32, name="x_sb", align_bytes=64)
         nc.vector.memset(x_sb[:, PASSES * T :], 0)
-        nc.scalar.dma_start(
-            x_sb[:, : PASSES * T].rearrange("p (s t) -> p s t", s=PASSES),
-            x_words.rearrange("s p t d -> p s (t d)").bitcast(I32),
-        )
         gate1_cols = keep.tile([P, 2, PACK], F32, name="gate1_cols")
         nc.sync.dma_start(gate1_cols[:], gate1[:, 0, :].rearrange("r (p j) -> p r j", j=PACK))
         x_rows = x_scales.rearrange("s (q r) t -> r q s t", r=4)
@@ -72,6 +69,10 @@ def tile_moe_ser_none_kernel(
                 x_plane[r:P:32, : PASSES * T].rearrange("p (s t) -> p s t", s=PASSES).bitcast(I32), x_rows[r].bitcast(I32)
             )
         offs_sb = load_list("offs_sb", offs)
+        nc.sync.dma_start(
+            x_sb[:, : PASSES * T].rearrange("p (s t) -> p s t", s=PASSES),
+            x_words.rearrange("s p t d -> p s (t d)").bitcast(I32),
+        )
         w1_rows = w1_scales.rearrange("e s (q r) i -> r q (e s) i", r=4)
 
         def load_w1_scales(first, last):
@@ -143,43 +144,36 @@ def tile_moe_ser_none_kernel(
                         lhsT=w1_sb[g][m][:, (e - start) * PASSES + s, :].bitcast(FP4X4),
                         lhsT_scale=w1_plane[:, e * PASSES + s, m * P : (m + 1) * P],
                         rhs=xg[g][:, s, cols].bitcast(FP8X4),
-                        rhs_scale=sg[g][:, s, cols],
+                        rhs_scale=sg[:, s, e * C : (e + 1) * C],
                         start=(s == 0 and e == first),
                         stop=(s == PASSES - 1 and e == last - 1),
                     )
             copy(h_sb[m][:, first * C : last * C], acc[:, : (last - first) * C])
 
-        xg, sg = [], []
-        for g, (first, last) in enumerate(FIRST_GROUPS):
-            width = (last - first) * C
-            lst = entries(offs_sb, first * C, last * C)
-            xg.append(keep.tile([P, PASSES, width], U32, name=f"xg{g}", align_bytes=64))
-            sg.append(keep.tile([P, PASSES, width], U8, name=f"sg{g}", align_bytes=64))
-            for s in range(PASSES):
-                nc.vector.tensor_copy(sg[g][:, s, :], x_plane[:, s * T : s * T + WINDOW].indirect(lst))
-            nc.vector.tensor_copy(xg[g][:, 0, :], x_sb[:, :WINDOW].bitcast(U32).indirect(lst))
-            if last < E:
-                nc.vector.tensor_copy(xg[g][:, 1, :], x_sb[:, T:].bitcast(U32).indirect(lst))
-                for m in range(ROW_TILES):
-                    first_layer(g, m, first, last, m, nc.scalar.copy)
-            else:
-                for lo, hi in ((first, last - 1), (last - 1, last)):
-                    nc.vector.tensor_copy(
-                        xg[g][:, 1, (lo - first) * C : (hi - first) * C],
-                        x_sb[:, T:].bitcast(U32).indirect(entries(offs_sb, lo * C, hi * C)),
-                    )
-                first_layer(g, 0, first, last - 1, 4, nc.vector.tensor_copy)
-                first_layer(g, 0, last - 1, last, 5, nc.scalar.copy)
-                for m in range(1, ROW_TILES):
-                    first_layer(g, m, first, last, (5 + m) % 8, nc.scalar.copy)
+        sg = keep.tile([P, PASSES, S], U8, name="sg", align_bytes=64)
+        for s in range(PASSES):
+            nc.vector.tensor_copy(sg[:, s, :], x_plane[:, s * T : s * T + PLANE_WINDOW].indirect(offs_sb[:]))
+        xg = [keep.tile([P, PASSES, 4 * C], U32, name=f"xg{g}", align_bytes=64) for g in range(2)]
+        for g, s, lo, hi in ((0, 0, 0, 4), (0, 1, 0, 4), (1, 0, 4, 8), (1, 1, 4, 7), (1, 1, 7, 8)):
+            nc.vector.tensor_copy(
+                xg[g][:, s, (lo - 4 * g) * C : (hi - 4 * g) * C],
+                x_sb[:, s * T : s * T + WINDOW].bitcast(U32).indirect(entries(offs_sb, lo * C, hi * C)),
+            )
+        first_layer(0, 0, 0, 4, 0, nc.scalar.copy)
+        first_layer(0, 1, 0, 4, 1, nc.scalar.copy)
+        first_layer(1, 0, 4, 7, 4, nc.vector.tensor_copy)
+        first_layer(1, 0, 7, 8, 5, nc.scalar.copy)
+        first_layer(1, 1, 4, 8, 6, nc.scalar.copy)
+        for m in range(2, ROW_TILES):
+            first_layer(0, m, 0, 4, 2 + m, nc.scalar.copy)
+            first_layer(1, m, 4, 8, (5 + m) % 8, nc.scalar.copy)
 
         def round_w2(half, tag):
             grouped = keep.tile([P, E // 2, N, PACK], BF16, name=f"w2_bf{half}", tag=tag, align_bytes=64)
-            for e in range(E // 2):
-                nc.scalar.copy(
-                    grouped[:, e, :, :].rearrange("p (c i) j -> p c j i", i=4),
-                    w2_sb[half][:, e, :, :].rearrange("p j (c i) -> p c j i", i=4),
-                )
+            nc.scalar.copy(
+                grouped[:].rearrange("p e (c i) j -> p e c j i", i=4),
+                w2_sb[half][:].rearrange("p e j (c i) -> p e c j i", i=4),
+            )
             return grouped
 
         w2_bf = [round_w2(0, "w2_bf0")]

@@ -24,7 +24,6 @@ PACK = 4
 PASSES = K // (P * PACK)
 ROW_TILES = H // P
 TOKEN_BLOCKS = T // P
-FIRST_GROUPS = ((0, 4), (4, 8))
 SPARE = 192
 WINDOW = T + SPARE
 PLANE_WINDOW = 1408
@@ -54,38 +53,18 @@ def tile_moe_ser_none_kernel(
         x_plane = keep.tile([P, T + PLANE_WINDOW], U8, name="x_plane", align_bytes=64)
         w1_plane = keep.tile([P, E * PASSES, H], U8, name="w1_plane", align_bytes=64)
         nc.gpsimd.memset(x_plane[:].bitcast(I32), 0)
-        w1_plane_words = w1_plane[:].rearrange("p g i -> p (g i)").bitcast(I32)
-        early = FIRST_GROUPS[0][1] * PASSES * H // 4
-        nc.vector.memset(w1_plane_words[:, :early], 0)
-        nc.vector.memset(w1_plane_words[:, early:], 0)
+        nc.vector.memset(w1_plane[:].rearrange("p g i -> p (g i)").bitcast(I32), 0)
 
-        x_sb = keep.tile([P, PASSES * T + SPARE], I32, name="x_sb", align_bytes=64)
-        nc.vector.memset(x_sb[:, PASSES * T :], 0)
-        gate1_cols = keep.tile([P, 2, PACK], F32, name="gate1_cols")
-        nc.sync.dma_start(gate1_cols[:], gate1[:, 0, :].rearrange("r (p j) -> p r j", j=PACK))
-        x_rows = x_scales.rearrange("s (q r) t -> r q s t", r=4)
-        for r in range(4):
-            nc.sync.dma_start(
-                x_plane[r:P:32, : PASSES * T].rearrange("p (s t) -> p s t", s=PASSES).bitcast(I32), x_rows[r].bitcast(I32)
-            )
-        offs_sb = load_list("offs_sb", offs)
-        nc.sync.dma_start(
-            x_sb[:, : PASSES * T].rearrange("p (s t) -> p s t", s=PASSES),
-            x_words.rearrange("s p t d -> p s (t d)").bitcast(I32),
-        )
-        w1_rows = w1_scales.rearrange("e s (q r) i -> r q (e s) i", r=4)
+        def load_x(s):
+            words = keep.tile([P, WINDOW], I32, name=f"x_sb{s}", align_bytes=64)
+            nc.vector.memset(words[:, T:], 0)
+            nc.sync.dma_start(words[:, :T], x_words[s].rearrange("p t d -> p (t d)").bitcast(I32))
+            return words
 
-        def load_w1_scales(first, last):
-            groups = slice(first * PASSES, last * PASSES)
-            for r in range(4):
-                nc.sync.dma_start(w1_plane[r:P:32, groups, :].bitcast(I32), w1_rows[r][:, groups, :].bitcast(I32))
-
-        def load_w1(first, last, tiles):
+        def load_w1(tiles):
             width = 2 * P * len(tiles)
-            words = keep.tile(
-                [P, (last - first) * PASSES, width], U8, name=f"w1_sb{first}_{tiles.start}", align_bytes=64
-            )
-            rows = w1_words[first:last].rearrange("e s p b -> p (e s) b")
+            words = keep.tile([P, E * PASSES, width], U8, name=f"w1_sb{tiles.start}", align_bytes=64)
+            rows = w1_words.rearrange("e s p b -> p (e s) b")
             nc.sync.dma_start(
                 words[:].bitcast(I32), rows[:, :, 2 * P * tiles.start : 2 * P * tiles.stop].bitcast(I32)
             )
@@ -99,21 +78,27 @@ def tile_moe_ser_none_kernel(
             )
             return raw
 
-        def load_gate(name, src, tag):
-            rows = keep.tile([P, 2, T], F32, name=name, tag=tag, align_bytes=64)
-            nc.sync.dma_start(rows[:], src.rearrange("r p t -> p r t"))
-            return rows
-
-        w1_sb = [load_w1(*FIRST_GROUPS[0], range(0, 4))]
-        load_w1_scales(*FIRST_GROUPS[0])
-        w1_sb.append(load_w1(*FIRST_GROUPS[1], range(0, 2)))
-        load_w1_scales(FIRST_GROUPS[0][1], E)
-        w1_sb[1].extend(load_w1(*FIRST_GROUPS[1], range(2, 4)))
+        offs_sb = load_list("offs_sb", offs)
+        x_sb = [load_x(0)]
+        x_rows = x_scales.rearrange("s (q r) t -> r q s t", r=4)
+        for r in range(4):
+            nc.sync.dma_start(
+                x_plane[r:P:32, : PASSES * T].rearrange("p (s t) -> p s t", s=PASSES).bitcast(I32), x_rows[r].bitcast(I32)
+            )
+        x_sb.append(load_x(1))
+        w2_sb = [load_w2(0, "w2_first")]
+        gate1_cols = keep.tile([P, 2, PACK], F32, name="gate1_cols")
+        nc.sync.dma_start(gate1_cols[:], gate1[:, 0, :].rearrange("r (p j) -> p r j", j=PACK))
+        w1_rows = w1_scales.rearrange("e s (q r) i -> r q (e s) i", r=4)
+        for r in range(4):
+            nc.sync.dma_start(w1_plane[r:P:32].bitcast(I32), w1_rows[r].bitcast(I32))
+        w1_sb = load_w1(range(0, 2)) + load_w1(range(2, 4))
         pos1_sb = load_list("pos1_sb", pos1)
         pos2_sb = load_list("pos2_sb", pos2)
-        w2_sb = [load_w2(0, "w2_first"), load_w2(1, "w2_second")]
+        w2_sb.append(load_w2(1, "w2_second"))
         offs2_sb = load_list("offs2_sb", offs2)
-        gate2_sb = load_gate("gate2_sb", gate2, "gate2")
+        gate2_sb = keep.tile([P, 2, T], F32, name="gate2_sb", align_bytes=64)
+        nc.sync.dma_start(gate2_sb[:], gate2.rearrange("r p t -> p r t"))
         pos3_sb = load_list("pos3_sb", pos3)
         pos4_sb = load_list("pos4_sb", pos4)
 
@@ -132,51 +117,61 @@ def tile_moe_ser_none_kernel(
                 gate1_sb[:, r, :].rearrange("m (p j) -> m p j", j=PACK), spread[:].rearrange("m (j p) -> m p j", j=PACK)
             )
 
-        h_sb = [keep.tile([P, S], F32, name=f"h_sb{m}", tag=f"h{m}", align_bytes=64) for m in range(ROW_TILES)]
-        def first_layer(g, m, first, last, index, copy):
-            start = FIRST_GROUPS[g][0]
-            acc = bank(index)
-            for s in range(PASSES):
-                for e in range(first, last):
-                    cols = slice((e - start) * C, (e - start + 1) * C)
-                    nc.tensor.matmul_mx(
-                        acc[:, (e - first) * C : (e - first + 1) * C],
-                        lhsT=w1_sb[g][m][:, (e - start) * PASSES + s, :].bitcast(FP4X4),
-                        lhsT_scale=w1_plane[:, e * PASSES + s, m * P : (m + 1) * P],
-                        rhs=xg[g][:, s, cols].bitcast(FP8X4),
-                        rhs_scale=sg[:, s, e * C : (e + 1) * C],
-                        start=(s == 0 and e == first),
-                        stop=(s == PASSES - 1 and e == last - 1),
-                    )
-            copy(h_sb[m][:, first * C : last * C], acc[:, : (last - first) * C])
-
-        sg = keep.tile([P, PASSES, S], U8, name="sg", align_bytes=64)
-        for s in range(PASSES):
-            nc.vector.tensor_copy(sg[:, s, :], x_plane[:, s * T : s * T + PLANE_WINDOW].indirect(offs_sb[:]))
-        xg = [keep.tile([P, PASSES, 4 * C], U32, name=f"xg{g}", align_bytes=64) for g in range(2)]
-        for g, s, lo, hi in ((0, 0, 0, 4), (0, 1, 0, 4), (1, 0, 4, 8), (1, 1, 4, 7), (1, 1, 7, 8)):
-            nc.vector.tensor_copy(
-                xg[g][:, s, (lo - 4 * g) * C : (hi - 4 * g) * C],
-                x_sb[:, s * T : s * T + WINDOW].bitcast(U32).indirect(entries(offs_sb, lo * C, hi * C)),
-            )
-        first_layer(0, 0, 0, 4, 0, nc.scalar.copy)
-        first_layer(0, 1, 0, 4, 1, nc.scalar.copy)
-        first_layer(1, 0, 4, 7, 4, nc.vector.tensor_copy)
-        first_layer(1, 0, 7, 8, 5, nc.scalar.copy)
-        first_layer(1, 1, 4, 8, 6, nc.scalar.copy)
-        for m in range(2, ROW_TILES):
-            first_layer(0, m, 0, 4, 2 + m, nc.scalar.copy)
-            first_layer(1, m, 4, 8, (5 + m) % 8, nc.scalar.copy)
-
-        def round_w2(half, tag):
-            grouped = keep.tile([P, E // 2, N, PACK], BF16, name=f"w2_bf{half}", tag=tag, align_bytes=64)
+        def round_w2(half):
+            grouped = keep.tile([P, E // 2, N, PACK], BF16, name=f"w2_bf{half}", align_bytes=64)
             nc.scalar.copy(
                 grouped[:].rearrange("p e (c i) j -> p e c j i", i=4),
                 w2_sb[half][:].rearrange("p e j (c i) -> p e c j i", i=4),
             )
             return grouped
 
-        w2_bf = [round_w2(0, "w2_bf0")]
+        w2_bf = [round_w2(0)]
+
+        h_sb = [keep.tile([P, S], F32, name=f"h_sb{m}", tag=f"h{m}", align_bytes=64) for m in range(ROW_TILES)]
+        sg = keep.tile([P, PASSES, S], U8, name="sg", align_bytes=64)
+        xg = [keep.tile([P, PASSES, 4 * C], U32, name=f"xg{g}", align_bytes=64) for g in range(2)]
+
+        def gather_words(s, lo, hi):
+            g = lo // 4
+            nc.vector.tensor_copy(
+                xg[g][:, s, (lo - 4 * g) * C : (hi - 4 * g) * C],
+                x_sb[s][:].bitcast(U32).indirect(entries(offs_sb, lo * C, hi * C)),
+            )
+
+        gather_words(0, 0, 4)
+        gather_words(0, 4, 8)
+        for s in range(PASSES):
+            nc.vector.tensor_copy(sg[:, s, :], x_plane[:, s * T : s * T + PLANE_WINDOW].indirect(offs_sb[:]))
+        gather_words(1, 0, 4)
+        gather_words(1, 4, 7)
+        gather_words(1, 7, 8)
+
+        def multiply(acc, s, m, first, last):
+            for e in range(first, last):
+                nc.tensor.matmul_mx(
+                    acc[:, (e - first) * C : (e - first + 1) * C],
+                    lhsT=w1_sb[m][:, e * PASSES + s, :].bitcast(FP4X4),
+                    lhsT_scale=w1_plane[:, e * PASSES + s, m * P : (m + 1) * P],
+                    rhs=xg[e // 4][:, s, (e % 4) * C : (e % 4 + 1) * C].bitcast(FP8X4),
+                    rhs_scale=sg[:, s, e * C : (e + 1) * C],
+                    start=(s == 0 and e == first),
+                    stop=(s == PASSES - 1 and e == last - 1),
+                )
+
+        early = ((0, 0, 4, nc.scalar.copy), (1, 0, 4, nc.scalar.copy), (0, 4, 7, nc.vector.tensor_copy),
+                 (0, 7, 8, nc.scalar.copy), (1, 4, 8, nc.scalar.copy))
+        accs = [bank(index) for index in range(len(early))]
+        for acc, (m, first, last, copy) in zip(accs, early):
+            multiply(acc, 0, m, first, last)
+        for acc, (m, first, last, copy) in zip(accs, early):
+            multiply(acc, 1, m, first, last)
+            copy(h_sb[m][:, first * C : last * C], acc[:, : (last - first) * C])
+        for index, (m, first) in zip((5, 6, 7, 0), ((2, 0), (2, 4), (3, 0), (3, 4))):
+            acc = bank(index)
+            for s in range(PASSES):
+                multiply(acc, s, m, first, first + 4)
+            nc.scalar.copy(h_sb[m][:, first * C : (first + 4) * C], acc[:])
+        w2_bf.append(round_w2(1))
 
         def gather_and_turn(blocks, tiles, total):
             toks = slice(blocks.start * P, blocks.stop * P)
@@ -218,13 +213,11 @@ def tile_moe_ser_none_kernel(
                 back[:, : len(halves) * width].rearrange("p (u t) -> p u t", t=width),
             )
 
-        c_rows = keep.tile([P, TOKEN_BLOCKS, 2, P, 2], BF16, name="c_rows", tag="w2_first", align_bytes=64)
+        c_rows = keep.tile([P, TOKEN_BLOCKS, 2, P, 2], BF16, name="c_rows", tag="w2_second", align_bytes=64)
         for m, index in enumerate((1, 2, 3)):
             total = bank(index)
             gather_and_turn(range(0, 4), range(m, m + 1), total)
             round_rows(nc.scalar.copy, c_rows[:], total, range(0, 4), range(m, m + 1))
-            if m == 1:
-                w2_bf.append(round_w2(1, "part1_1_0"))
         last_tile = range(3, 4)
         for blocks, index in ((range(0, 2), 4), (range(2, 3), 6)):
             total = bank(index)

@@ -27,6 +27,7 @@ TOKEN_BLOCKS = T // P
 SPARE = 192
 WINDOW = T + SPARE
 PLANE_WINDOW = 1408
+W2_START = T * 2 - P // 2
 SECOND_GROUPS = ((0, 2), (2, 4), (4, 6), (6, 7), (7, 8))
 
 
@@ -50,16 +51,19 @@ def tile_moe_ser_none_kernel(
             nc.sync.dma_start(lst[:], src)
             return lst
 
-        x_plane = keep.tile([P, T + PLANE_WINDOW], U8, name="x_plane", align_bytes=64)
-        w1_plane = keep.tile([P, E * PASSES, H], U8, name="w1_plane", align_bytes=64)
-        nc.gpsimd.memset(x_plane[:].bitcast(I32), 0)
-        nc.vector.memset(w1_plane[:].rearrange("p g i -> p (g i)").bitcast(I32), 0)
+        x_plane = keep.tile([P, PLANE_WINDOW], U8, name="x_plane", tag="x_plane", align_bytes=64)
+        nc.gpsimd.memset(x_plane[:, :T].bitcast(I32), 0)
+        nc.vector.memset(x_plane[:, T:].bitcast(I32), 0)
+        gate1_cols = keep.tile([P, 2, PACK], F32, name="gate1_cols")
+        nc.gpsimd.dma_start(gate1_cols[:], gate1[:, 0, :].rearrange("r (p j) -> p r j", j=PACK))
+        sg = [keep.tile([P, S], U8, name=f"sg{s}", align_bytes=64) for s in range(PASSES)]
+        nc.gpsimd.memset(sg[1][:].bitcast(I32), 0)
+        w1_planes = [keep.tile([P, E * PASSES, H // 2], U8, name=f"w1_plane{i}", align_bytes=64) for i in range(2)]
+        for plane in w1_planes:
+            nc.vector.memset(plane[:].rearrange("p g i -> p (g i)").bitcast(I32), 0)
 
-        def load_x(s):
-            words = keep.tile([P, WINDOW], I32, name=f"x_sb{s}", align_bytes=64)
-            nc.vector.memset(words[:, T:], 0)
-            nc.sync.dma_start(words[:, :T], x_words[s].rearrange("p t d -> p (t d)").bitcast(I32))
-            return words
+        x_sb = keep.tile([P, PASSES, WINDOW], I32, name="x_sb", align_bytes=64)
+        nc.vector.memset(x_sb[:, :, T:], 0)
 
         def load_w1(tiles):
             width = 2 * P * len(tiles)
@@ -70,32 +74,41 @@ def tile_moe_ser_none_kernel(
             )
             return [words[:, :, 2 * P * k : 2 * P * (k + 1)] for k in range(len(tiles))]
 
-        def load_w2(half, tag):
-            raw = keep.tile([P, E // 2, PACK, N], F32, name=f"w2_sb{half}", tag=tag, align_bytes=64)
+        def load_w2(first, last, raw):
             nc.sync.dma_start(
-                raw[:].rearrange("p e j n -> p e (j n)"),
-                w2[half * E // 2 : (half + 1) * E // 2].rearrange("e (p j) n -> p e (j n)", j=PACK),
+                raw.rearrange("p e j n -> p e (j n)"),
+                w2[first:last].rearrange("e (p j) n -> p e (j n)", j=PACK),
             )
-            return raw
+
+        def load_w1_scales(half, residues):
+            rows = w1_scales.rearrange("e s (q r) i -> r q (e s) i", r=4)
+            for r in residues:
+                nc.sync.dma_start(
+                    w1_planes[half][r:P:32].bitcast(I32),
+                    rows[r][:, :, half * H // 2 : (half + 1) * H // 2].bitcast(I32),
+                )
 
         offs_sb = load_list("offs_sb", offs)
-        x_sb = [load_x(0)]
-        x_rows = x_scales.rearrange("s (q r) t -> r q s t", r=4)
-        for r in range(4):
-            nc.sync.dma_start(
-                x_plane[r:P:32, : PASSES * T].rearrange("p (s t) -> p s t", s=PASSES).bitcast(I32), x_rows[r].bitcast(I32)
-            )
-        x_sb.append(load_x(1))
-        w2_sb = [load_w2(0, "w2_first")]
-        gate1_cols = keep.tile([P, 2, PACK], F32, name="gate1_cols")
-        nc.sync.dma_start(gate1_cols[:], gate1[:, 0, :].rearrange("r (p j) -> p r j", j=PACK))
-        w1_rows = w1_scales.rearrange("e s (q r) i -> r q (e s) i", r=4)
-        for r in range(4):
-            nc.sync.dma_start(w1_plane[r:P:32].bitcast(I32), w1_rows[r].bitcast(I32))
-        w1_sb = load_w1(range(0, 2)) + load_w1(range(2, 4))
+        nc.scalar.dma_start(x_sb[:, :, :T], x_words.rearrange("s p t d -> p s (t d)").bitcast(I32))
         pos1_sb = load_list("pos1_sb", pos1)
         pos2_sb = load_list("pos2_sb", pos2)
-        w2_sb.append(load_w2(1, "w2_second"))
+        for q in range(4):
+            nc.sync.dma_start(
+                x_plane[32 * q : 32 * q + 8, :T].bitcast(I32), x_scales[:, 4 * q : 4 * q + 4, :].bitcast(I32)
+            )
+        load_w1_scales(0, range(0, 2))
+        w1_sb = load_w1(range(0, 2))
+        load_w1_scales(0, range(2, 4))
+        w1_sb.extend(load_w1(range(2, 4)))
+        load_w1_scales(1, range(4))
+        shared = keep.tile([P, W2_START + E // 2 * PACK * N], F32, name="shared", tag="shared", align_bytes=64)
+        w2_raw = {0: shared[:, W2_START:].rearrange("p (e j n) -> p e j n", j=PACK, n=N)}
+        for first in (4, 6):
+            raw = keep.tile([P, 2, PACK, N], F32, name=f"w2_raw{first}", tag=f"ring{first}", align_bytes=64)
+            w2_raw[first] = raw[:]
+        load_w2(4, 6, w2_raw[4])
+        load_w2(0, 4, w2_raw[0])
+        load_w2(6, 8, w2_raw[6])
         offs2_sb = load_list("offs2_sb", offs2)
         gate2_sb = keep.tile([P, 2, T], F32, name="gate2_sb", align_bytes=64)
         nc.sync.dma_start(gate2_sb[:], gate2.rearrange("r p t -> p r t"))
@@ -117,31 +130,41 @@ def tile_moe_ser_none_kernel(
                 gate1_sb[:, r, :].rearrange("m (p j) -> m p j", j=PACK), spread[:].rearrange("m (j p) -> m p j", j=PACK)
             )
 
-        def round_w2(half):
-            grouped = keep.tile([P, E // 2, N, PACK], BF16, name=f"w2_bf{half}", align_bytes=64)
-            nc.scalar.copy(
+        def round_w2(copy, first, last, tag):
+            grouped = keep.tile([P, last - first, N, PACK], BF16, name=f"w2_bf{first}", tag=tag, align_bytes=64)
+            copy(
                 grouped[:].rearrange("p e (c i) j -> p e c j i", i=4),
-                w2_sb[half][:].rearrange("p e j (c i) -> p e c j i", i=4),
+                w2_raw[first].rearrange("p e j (c i) -> p e c j i", i=4),
             )
             return grouped
 
-        w2_bf = [round_w2(0)]
+        w2_codes = {}
+        w2_plane = keep.tile([P, E * N], U8, name="w2_plane", align_bytes=64)
+
+        def quantise_w2(grouped, first, last, tag):
+            codes = keep.tile([P, (last - first) * N], U32, name=f"w2_codes{first}", tag=tag, align_bytes=64)
+            nc.vector.quantize_mx(
+                out=codes[:].bitcast(FP8X4),
+                scales=w2_plane[:, first * N : last * N],
+                in_=grouped[:].rearrange("p e n j -> p (e n j)"),
+            )
+            for e in range(first, last):
+                w2_codes[e] = codes[:, (e - first) * N : (e - first + 1) * N]
 
         h_sb = [keep.tile([P, S], F32, name=f"h_sb{m}", tag=f"h{m}", align_bytes=64) for m in range(ROW_TILES)]
-        sg = keep.tile([P, PASSES, S], U8, name="sg", align_bytes=64)
-        xg = [keep.tile([P, PASSES, 4 * C], U32, name=f"xg{g}", align_bytes=64) for g in range(2)]
+        xg = keep.tile([P, PASSES, S], U32, name="xg", tag="x_plane", align_bytes=64)
 
         def gather_words(s, lo, hi):
-            g = lo // 4
             nc.vector.tensor_copy(
-                xg[g][:, s, (lo - 4 * g) * C : (hi - 4 * g) * C],
-                x_sb[s][:].bitcast(U32).indirect(entries(offs_sb, lo * C, hi * C)),
+                xg[:, s, lo * C : hi * C],
+                x_sb[:, s, :].bitcast(U32).indirect(entries(offs_sb, lo * C, hi * C)),
             )
 
+        nc.vector.tensor_copy(sg[0][:], x_plane[:].indirect(offs_sb[:]))
+        for r in range(4):
+            nc.scalar.dma_start(sg[1][r:P:32].bitcast(I32), sg[0][4 + r : P : 32].bitcast(I32))
         gather_words(0, 0, 4)
         gather_words(0, 4, 8)
-        for s in range(PASSES):
-            nc.vector.tensor_copy(sg[:, s, :], x_plane[:, s * T : s * T + PLANE_WINDOW].indirect(offs_sb[:]))
         gather_words(1, 0, 4)
         gather_words(1, 4, 7)
         gather_words(1, 7, 8)
@@ -151,27 +174,25 @@ def tile_moe_ser_none_kernel(
                 nc.tensor.matmul_mx(
                     acc[:, (e - first) * C : (e - first + 1) * C],
                     lhsT=w1_sb[m][:, e * PASSES + s, :].bitcast(FP4X4),
-                    lhsT_scale=w1_plane[:, e * PASSES + s, m * P : (m + 1) * P],
-                    rhs=xg[e // 4][:, s, (e % 4) * C : (e % 4 + 1) * C].bitcast(FP8X4),
-                    rhs_scale=sg[:, s, e * C : (e + 1) * C],
+                    lhsT_scale=w1_planes[m // 2][:, e * PASSES + s, (m % 2) * P : (m % 2 + 1) * P],
+                    rhs=xg[:, s, e * C : (e + 1) * C].bitcast(FP8X4),
+                    rhs_scale=sg[s][:, e * C : (e + 1) * C],
                     start=(s == 0 and e == first),
                     stop=(s == PASSES - 1 and e == last - 1),
                 )
 
-        early = ((0, 0, 4, nc.scalar.copy), (1, 0, 4, nc.scalar.copy), (0, 4, 7, nc.vector.tensor_copy),
-                 (0, 7, 8, nc.scalar.copy), (1, 4, 8, nc.scalar.copy))
-        accs = [bank(index) for index in range(len(early))]
-        for acc, (m, first, last, copy) in zip(accs, early):
-            multiply(acc, 0, m, first, last)
-        for acc, (m, first, last, copy) in zip(accs, early):
-            multiply(acc, 1, m, first, last)
-            copy(h_sb[m][:, first * C : last * C], acc[:, : (last - first) * C])
-        for index, (m, first) in zip((5, 6, 7, 0), ((2, 0), (2, 4), (3, 0), (3, 4))):
+        tile0 = ((0, 4, nc.scalar.copy), (4, 7, nc.vector.tensor_copy), (7, 8, nc.scalar.copy))
+        accs = [bank(index) for index in range(len(tile0))]
+        for acc, (first, last, copy) in zip(accs, tile0):
+            multiply(acc, 0, 0, first, last)
+        for acc, (first, last, copy) in zip(accs, tile0):
+            multiply(acc, 1, 0, first, last)
+            copy(h_sb[0][:, first * C : last * C], acc[:, : (last - first) * C])
+        for index, (m, first) in zip((3, 4, 5, 6, 7, 0), ((1, 0), (1, 4), (2, 0), (2, 4), (3, 0), (3, 4))):
             acc = bank(index)
             for s in range(PASSES):
                 multiply(acc, s, m, first, first + 4)
             nc.scalar.copy(h_sb[m][:, first * C : (first + 4) * C], acc[:])
-        w2_bf.append(round_w2(1))
 
         def gather_and_turn(blocks, tiles, total):
             toks = slice(blocks.start * P, blocks.stop * P)
@@ -213,33 +234,28 @@ def tile_moe_ser_none_kernel(
                 back[:, : len(halves) * width].rearrange("p (u t) -> p u t", t=width),
             )
 
-        c_rows = keep.tile([P, TOKEN_BLOCKS, 2, P, 2], BF16, name="c_rows", tag="w2_second", align_bytes=64)
-        for m, index in enumerate((1, 2, 3)):
+        c_rows = shared[:, : T * 2].bitcast(BF16).rearrange("t (q u p d) -> t q u p d", u=2, p=P, d=2)
+        for m, index in enumerate((1, 6, 0)):
             total = bank(index)
             gather_and_turn(range(0, 4), range(m, m + 1), total)
-            round_rows(nc.scalar.copy, c_rows[:], total, range(0, 4), range(m, m + 1))
+            round_rows(nc.scalar.copy, c_rows, total, range(0, 4), range(m, m + 1))
+            if m == 1:
+                w2_first = round_w2(nc.scalar.copy, 0, 4, "part1_1_0")
         last_tile = range(3, 4)
-        for blocks, index in ((range(0, 2), 4), (range(2, 3), 6)):
+        for blocks, index, back in ((range(2, 4), 4, 5), (range(1, 2), 0, 7)):
             total = bank(index)
             gather_and_turn(blocks, last_tile, total)
             round_rows(nc.scalar.copy, c_rows[:, blocks.start : blocks.stop], total, blocks, last_tile)
-            turn_back(nc.scalar.copy, c_rows[:, blocks.start : blocks.stop], blocks.start, range(0, 2), bank(index + 1))
+            turn_back(nc.scalar.copy, c_rows[:, blocks.start : blocks.stop], blocks.start, range(0, 2), bank(back))
         total = bank(4)
-        gather_and_turn(range(3, 4), last_tile, total)
-        round_rows(nc.vector.tensor_copy, c_rows[:, 3:4], total, range(3, 4), last_tile)
-        turn_back(nc.vector.tensor_copy, c_rows[:, 3:4], 3, range(0, 1), bank(0))
-        turn_back(nc.scalar.copy, c_rows[:, 3:4], 3, range(1, 2), bank(1))
+        gather_and_turn(range(0, 1), last_tile, total)
+        round_rows(nc.vector.tensor_copy, c_rows[:, 0:1], total, range(0, 1), last_tile)
+        turn_back(nc.vector.tensor_copy, c_rows[:, 0:1], 0, range(0, 1), bank(6))
+        turn_back(nc.scalar.copy, c_rows[:, 0:1], 0, range(1, 2), bank(1))
 
-        w2_codes = []
-        w2_plane = keep.tile([P, E * N], U8, name="w2_plane", align_bytes=64)
-        for g, tag in enumerate(("h3", "part3_1_3")):
-            cols = slice(4 * g * N, 4 * (g + 1) * N)
-            w2_codes.append(keep.tile([P, 4 * N], U32, name=f"w2_codes{g}", tag=tag, align_bytes=64))
-            nc.vector.quantize_mx(
-                out=w2_codes[g][:].bitcast(FP8X4),
-                scales=w2_plane[:, cols],
-                in_=w2_bf[g][:].rearrange("p e n j -> p (e n j)"),
-            )
+        quantise_w2(w2_first, 0, 4, "h3")
+        quantise_w2(round_w2(nc.vector.tensor_copy, 4, 6, "part3_1_0"), 4, 6, "w2_codes4")
+        w2_last = round_w2(nc.scalar.copy, 6, 8, "shared")
 
         windows = [c_words[:, u, :].bitcast(U32) for u in range(2)]
         y_sb = keep.tile([P, S], F32, name="y_sb")
@@ -248,12 +264,12 @@ def tile_moe_ser_none_kernel(
             lst = entries(offs2_sb, first * C, last * C)
             if last < E:
                 woven = keep.tile([P, width, 2], U32, name=f"woven{first}", align_bytes=64)
-                cg = keep.tile([P, 2, width], U32, name=f"cg{first}", tag="cg", bufs=2, align_bytes=64)
+                cg = keep.tile([P, 2, width], U32, name=f"cg{first}", tag=f"ring{4 + g % 2}", align_bytes=64)
                 for u in range(2):
                     nc.vector.tensor_copy(cg[:, u, :], windows[u].indirect(lst))
                 nc.scalar.copy(woven[:], cg[:].rearrange("p u s -> p s u"))
             else:
-                woven = keep.tile([P, width, 2], U32, name=f"woven{first}", tag="cg", bufs=2, align_bytes=64)
+                woven = keep.tile([P, width, 2], U32, name=f"woven{first}", tag=f"ring{4 + g % 2}", align_bytes=64)
                 for u in range(2):
                     nc.vector.tensor_copy(woven[:, :, u], windows[u].indirect(lst))
             codes = keep.tile([P, width], U32, name=f"codes{first}", align_bytes=64)
@@ -263,12 +279,14 @@ def tile_moe_ser_none_kernel(
                 scales=plane[:],
                 in_=woven[:].rearrange("p s u -> p (s u)").bitcast(BF16),
             )
+            if g == 0:
+                quantise_w2(w2_last, 6, 8, "woven0")
             acc = bank(2 + g)
             for e in range(first, last):
                 cols = slice((e - first) * C, (e - first + 1) * C)
                 nc.tensor.matmul_mx(
                     acc[:, cols],
-                    lhsT=w2_codes[e // 4][:, (e % 4) * N : (e % 4 + 1) * N].bitcast(FP8X4),
+                    lhsT=w2_codes[e].bitcast(FP8X4),
                     lhsT_scale=w2_plane[:, e * N : (e + 1) * N],
                     rhs=codes[:, cols].bitcast(FP8X4),
                     rhs_scale=plane[:, cols],

@@ -27,7 +27,7 @@ TOKEN_BLOCKS = T // P
 SPARE = 192
 WINDOW = T + SPARE
 PLANE_WINDOW = 1408
-W2_START = T * 2 - P // 2
+W2_START = T * 2 - 3 * P // 4
 SECOND_GROUPS = ((0, 2), (2, 4), (4, 6), (6, 7), (7, 8))
 
 
@@ -51,7 +51,7 @@ def tile_moe_ser_none_kernel(
             nc.sync.dma_start(lst[:], src)
             return lst
 
-        x_plane = keep.tile([P, PLANE_WINDOW], U8, name="x_plane", tag="x_plane", align_bytes=64)
+        x_plane = keep.tile([P, PLANE_WINDOW], U8, name="x_plane", align_bytes=64)
         nc.gpsimd.memset(x_plane[:, :T].bitcast(I32), 0)
         nc.vector.memset(x_plane[:, T:].bitcast(I32), 0)
         gate1_cols = keep.tile([P, 2, PACK], F32, name="gate1_cols")
@@ -65,14 +65,19 @@ def tile_moe_ser_none_kernel(
         x_sb = keep.tile([P, PASSES, WINDOW], I32, name="x_sb", align_bytes=64)
         nc.vector.memset(x_sb[:, :, T:], 0)
 
-        def load_w1(tiles):
+        w1_sb = {}
+
+        def load_w1(first, last, tiles):
             width = 2 * P * len(tiles)
-            words = keep.tile([P, E * PASSES, width], U8, name=f"w1_sb{tiles.start}", align_bytes=64)
-            rows = w1_words.rearrange("e s p b -> p (e s) b")
+            words = keep.tile([P, last - first, PASSES, width], U8, name=f"w1_sb{first}_{tiles.start}", align_bytes=64)
+            rows = w1_words[first:last].rearrange("e s p b -> p (e s) b")
             nc.sync.dma_start(
-                words[:].bitcast(I32), rows[:, :, 2 * P * tiles.start : 2 * P * tiles.stop].bitcast(I32)
+                words[:].rearrange("p e s b -> p (e s) b").bitcast(I32),
+                rows[:, :, 2 * P * tiles.start : 2 * P * tiles.stop].bitcast(I32),
             )
-            return [words[:, :, 2 * P * k : 2 * P * (k + 1)] for k in range(len(tiles))]
+            for e in range(first, last):
+                for k, m in enumerate(tiles):
+                    w1_sb[e, m] = words[:, e - first, :, 2 * P * k : 2 * P * (k + 1)]
 
         def load_w2(first, last, raw):
             nc.sync.dma_start(
@@ -89,25 +94,29 @@ def tile_moe_ser_none_kernel(
                 )
 
         offs_sb = load_list("offs_sb", offs)
-        nc.scalar.dma_start(x_sb[:, :, :T], x_words.rearrange("s p t d -> p s (t d)").bitcast(I32))
-        pos1_sb = load_list("pos1_sb", pos1)
-        pos2_sb = load_list("pos2_sb", pos2)
         for q in range(4):
             nc.sync.dma_start(
                 x_plane[32 * q : 32 * q + 8, :T].bitcast(I32), x_scales[:, 4 * q : 4 * q + 4, :].bitcast(I32)
             )
-        load_w1_scales(0, range(0, 2))
-        w1_sb = load_w1(range(0, 2))
-        load_w1_scales(0, range(2, 4))
-        w1_sb.extend(load_w1(range(2, 4)))
+        nc.sync.dma_start(x_sb[:, :, :T], x_words.rearrange("s p t d -> p s (t d)").bitcast(I32))
+        load_w1_scales(0, range(0, 1))
+        pos1_sb = load_list("pos1_sb", pos1)
+        load_w1(0, 8, range(0, 2))
+        load_w1_scales(0, range(1, 4))
+        nc.vector.tensor_copy(sg[0][:], x_plane[:].indirect(offs_sb[:]))
+        for r in range(4):
+            nc.sync.dma_start(sg[1][r:P:32].bitcast(I32), sg[0][4 + r : P : 32].bitcast(I32))
+        pos2_sb = load_list("pos2_sb", pos2)
+        load_w1(0, 4, range(2, 4))
         load_w1_scales(1, range(4))
+        load_w1(4, 8, range(2, 4))
         shared = keep.tile([P, W2_START + E // 2 * PACK * N], F32, name="shared", tag="shared", align_bytes=64)
         w2_raw = {0: shared[:, W2_START:].rearrange("p (e j n) -> p e j n", j=PACK, n=N)}
         for first in (4, 6):
             raw = keep.tile([P, 2, PACK, N], F32, name=f"w2_raw{first}", tag=f"ring{first}", align_bytes=64)
             w2_raw[first] = raw[:]
-        load_w2(4, 6, w2_raw[4])
         load_w2(0, 4, w2_raw[0])
+        load_w2(4, 6, w2_raw[4])
         load_w2(6, 8, w2_raw[6])
         offs2_sb = load_list("offs2_sb", offs2)
         gate2_sb = keep.tile([P, 2, T], F32, name="gate2_sb", align_bytes=64)
@@ -130,10 +139,17 @@ def tile_moe_ser_none_kernel(
                 gate1_sb[:, r, :].rearrange("m (p j) -> m p j", j=PACK), spread[:].rearrange("m (j p) -> m p j", j=PACK)
             )
 
-        def round_w2(copy, first, last, tag):
+        def w2_tile(first, last, tag):
             grouped = keep.tile([P, last - first, N, PACK], BF16, name=f"w2_bf{first}", tag=tag, align_bytes=64)
+            return grouped[:]
+
+        def codes_tile(first, last, tag):
+            codes = keep.tile([P, (last - first) * N], U32, name=f"w2_codes{first}", tag=tag, align_bytes=64)
+            return codes[:]
+
+        def round_w2(copy, first, grouped):
             copy(
-                grouped[:].rearrange("p e (c i) j -> p e c j i", i=4),
+                grouped.rearrange("p e (c i) j -> p e c j i", i=4),
                 w2_raw[first].rearrange("p e j (c i) -> p e c j i", i=4),
             )
             return grouped
@@ -141,18 +157,17 @@ def tile_moe_ser_none_kernel(
         w2_codes = {}
         w2_plane = keep.tile([P, E * N], U8, name="w2_plane", align_bytes=64)
 
-        def quantise_w2(grouped, first, last, tag):
-            codes = keep.tile([P, (last - first) * N], U32, name=f"w2_codes{first}", tag=tag, align_bytes=64)
+        def quantise_w2(grouped, first, last, codes):
             nc.vector.quantize_mx(
-                out=codes[:].bitcast(FP8X4),
+                out=codes.bitcast(FP8X4),
                 scales=w2_plane[:, first * N : last * N],
-                in_=grouped[:].rearrange("p e n j -> p (e n j)"),
+                in_=grouped.rearrange("p e n j -> p (e n j)"),
             )
             for e in range(first, last):
                 w2_codes[e] = codes[:, (e - first) * N : (e - first + 1) * N]
 
         h_sb = [keep.tile([P, S], F32, name=f"h_sb{m}", tag=f"h{m}", align_bytes=64) for m in range(ROW_TILES)]
-        xg = keep.tile([P, PASSES, S], U32, name="xg", tag="x_plane", align_bytes=64)
+        xg = keep.tile([P, PASSES, S], U32, name="xg", align_bytes=64)
 
         def gather_words(s, lo, hi):
             nc.vector.tensor_copy(
@@ -160,9 +175,6 @@ def tile_moe_ser_none_kernel(
                 x_sb[:, s, :].bitcast(U32).indirect(entries(offs_sb, lo * C, hi * C)),
             )
 
-        nc.vector.tensor_copy(sg[0][:], x_plane[:].indirect(offs_sb[:]))
-        for r in range(4):
-            nc.scalar.dma_start(sg[1][r:P:32].bitcast(I32), sg[0][4 + r : P : 32].bitcast(I32))
         gather_words(0, 0, 4)
         gather_words(0, 4, 8)
         gather_words(1, 0, 4)
@@ -173,7 +185,7 @@ def tile_moe_ser_none_kernel(
             for e in range(first, last):
                 nc.tensor.matmul_mx(
                     acc[:, (e - first) * C : (e - first + 1) * C],
-                    lhsT=w1_sb[m][:, e * PASSES + s, :].bitcast(FP4X4),
+                    lhsT=w1_sb[e, m][:, s, :].bitcast(FP4X4),
                     lhsT_scale=w1_planes[m // 2][:, e * PASSES + s, (m % 2) * P : (m % 2 + 1) * P],
                     rhs=xg[:, s, e * C : (e + 1) * C].bitcast(FP8X4),
                     rhs_scale=sg[s][:, e * C : (e + 1) * C],
@@ -188,7 +200,7 @@ def tile_moe_ser_none_kernel(
         for acc, (first, last, copy) in zip(accs, tile0):
             multiply(acc, 1, 0, first, last)
             copy(h_sb[0][:, first * C : last * C], acc[:, : (last - first) * C])
-        for index, (m, first) in zip((3, 4, 5, 6, 7, 0), ((1, 0), (1, 4), (2, 0), (2, 4), (3, 0), (3, 4))):
+        for index, (m, first) in zip((0, 1, 5, 6, 7, 3), ((1, 0), (1, 4), (2, 0), (3, 0), (2, 4), (3, 4))):
             acc = bank(index)
             for s in range(PASSES):
                 multiply(acc, s, m, first, first + 4)
@@ -219,43 +231,38 @@ def tile_moe_ser_none_kernel(
                 total[:, : len(blocks) * len(tiles) * P].rearrange("t (q p u d) -> t q u p d", q=len(blocks), u=2, d=2),
             )
 
-        def turn_back(copy, c_rows, token_block, halves, back):
-            for k in range(c_rows.shape[1]):
-                for j, u in enumerate(halves):
-                    place = j * c_rows.shape[1] + k
-                    nc.tensor.transpose(
-                        back[:, place * P : (place + 1) * P],
-                        c_rows[:, k, u, :, :].rearrange("t p d -> t (p d)").bitcast(F32),
-                        ident[:],
-                    )
-            width = c_rows.shape[1] * P
-            copy(
-                c_words[:, halves.start : halves.stop, token_block * P : token_block * P + width],
-                back[:, : len(halves) * width].rearrange("p (u t) -> p u t", t=width),
-            )
+        def turn_back(copy, blocks, u, back):
+            for k, q in enumerate(blocks):
+                nc.tensor.transpose(
+                    back[:, k * P : (k + 1) * P], c_rows[:, q, u].rearrange("t p d -> t (p d)").bitcast(F32), ident[:]
+                )
+            copy(c_words[:, u, blocks.start * P : blocks.stop * P], back[:, : len(blocks) * P])
 
         c_rows = shared[:, : T * 2].bitcast(BF16).rearrange("t (q u p d) -> t q u p d", u=2, p=P, d=2)
-        for m, index in enumerate((1, 6, 0)):
+        for m, index in enumerate((6, 7, 3)):
             total = bank(index)
             gather_and_turn(range(0, 4), range(m, m + 1), total)
             round_rows(nc.scalar.copy, c_rows, total, range(0, 4), range(m, m + 1))
-            if m == 1:
-                w2_first = round_w2(nc.scalar.copy, 0, 4, "part1_1_0")
+            if m == 0:
+                w2_first = round_w2(nc.scalar.copy, 0, w2_tile(0, 4, "w2_bf0"))
         last_tile = range(3, 4)
-        for blocks, index, back in ((range(2, 4), 4, 5), (range(1, 2), 0, 7)):
+        for blocks, index, back in ((range(2, 4), 4, 5), (range(1, 2), 3, 7)):
             total = bank(index)
             gather_and_turn(blocks, last_tile, total)
             round_rows(nc.scalar.copy, c_rows[:, blocks.start : blocks.stop], total, blocks, last_tile)
-            turn_back(nc.scalar.copy, c_rows[:, blocks.start : blocks.stop], blocks.start, range(0, 2), bank(back))
+            turn_back(nc.scalar.copy, blocks, 0, bank(back))
         total = bank(4)
         gather_and_turn(range(0, 1), last_tile, total)
         round_rows(nc.vector.tensor_copy, c_rows[:, 0:1], total, range(0, 1), last_tile)
-        turn_back(nc.vector.tensor_copy, c_rows[:, 0:1], 0, range(0, 1), bank(6))
-        turn_back(nc.scalar.copy, c_rows[:, 0:1], 0, range(1, 2), bank(1))
+        turn_back(nc.scalar.copy, range(1, 4), 1, bank(3))
+        turn_back(nc.scalar.copy, range(0, 1), 0, bank(6))
+        turn_back(nc.vector.tensor_copy, range(0, 1), 1, bank(1))
 
-        quantise_w2(w2_first, 0, 4, "h3")
-        quantise_w2(round_w2(nc.vector.tensor_copy, 4, 6, "part3_1_0"), 4, 6, "w2_codes4")
-        w2_last = round_w2(nc.scalar.copy, 6, 8, "shared")
+        w2_middle = round_w2(nc.vector.tensor_copy, 4, w2_tile(4, 6, "h3"))
+        early_codes = codes_tile(0, 6, "part3_1_0")
+        quantise_w2(w2_first, 0, 4, early_codes[:, : 4 * N])
+        quantise_w2(w2_middle, 4, 6, early_codes[:, 4 * N :])
+        w2_last = round_w2(nc.scalar.copy, 6, w2_tile(6, 8, "shared"))
 
         windows = [c_words[:, u, :].bitcast(U32) for u in range(2)]
         y_sb = keep.tile([P, S], F32, name="y_sb")
@@ -280,7 +287,7 @@ def tile_moe_ser_none_kernel(
                 in_=woven[:].rearrange("p s u -> p (s u)").bitcast(BF16),
             )
             if g == 0:
-                quantise_w2(w2_last, 6, 8, "woven0")
+                quantise_w2(w2_last, 6, 8, codes_tile(6, 8, "woven0"))
             acc = bank(2 + g)
             for e in range(first, last):
                 cols = slice((e - first) * C, (e - first + 1) * C)

@@ -28,7 +28,7 @@ SPARE = 192
 WINDOW = T + SPARE
 PLANE_WINDOW = 1408
 W2_START = T * 2 - 3 * P // 4
-SECOND_GROUPS = ((0, 2), (2, 4), (4, 6), (6, 7), (7, 8))
+SECOND_GROUPS = ((0, 2), (2, 4), (4, 6))
 
 
 def entries(lst, first, last):
@@ -126,6 +126,8 @@ def tile_moe_ser_none_kernel(
 
         ident = keep.tile([P, P], F32, name="ident")
         make_identity(nc, ident[:])
+        ident_bf = keep.tile([P, P], BF16, name="ident_bf")
+        make_identity(nc, ident_bf[:])
         c_words = keep.tile([P, 2, T], F32, name="c_words", align_bytes=64)
 
         gate1_sb = keep.tile([P, 2, T], F32, name="gate1_sb", align_bytes=64)
@@ -262,33 +264,26 @@ def tile_moe_ser_none_kernel(
         early_codes = codes_tile(0, 6, "part3_1_0")
         quantise_w2(w2_first, 0, 4, early_codes[:, : 4 * N])
         quantise_w2(w2_middle, 4, 6, early_codes[:, 4 * N :])
-        w2_last = round_w2(nc.scalar.copy, 6, w2_tile(6, 8, "shared"))
+        w2_last = round_w2(nc.scalar.copy, 6, w2_tile(6, 8, "h3"))
+
+        c_planes = keep.tile([P, 2, 2, T], BF16, name="c_planes", align_bytes=64)
+        for u, index in enumerate((0, 7)):
+            turned = psum.tile([P, 2, T], BF16, name=f"turned{u}", tag=f"bank{index}")
+            for d in range(2):
+                for q in range(TOKEN_BLOCKS):
+                    nc.tensor.transpose(turned[:, d, q * P : (q + 1) * P], c_rows[:, q, u, :, d], ident_bf[:])
+            nc.scalar.copy(c_planes[:, u], turned[:])
 
         windows = [c_words[:, u, :].bitcast(U32) for u in range(2)]
         y_sb = keep.tile([P, S], F32, name="y_sb")
-        for g, (first, last) in enumerate(SECOND_GROUPS):
+
+        def quantise_and_multiply(rows, first, last, tag, acc):
             width = (last - first) * C
-            lst = entries(offs2_sb, first * C, last * C)
-            if last < E:
-                woven = keep.tile([P, width, 2], U32, name=f"woven{first}", align_bytes=64)
-                cg = keep.tile([P, 2, width], U32, name=f"cg{first}", tag=f"ring{4 + g % 2}", align_bytes=64)
-                for u in range(2):
-                    nc.vector.tensor_copy(cg[:, u, :], windows[u].indirect(lst))
-                nc.scalar.copy(woven[:], cg[:].rearrange("p u s -> p s u"))
-            else:
-                woven = keep.tile([P, width, 2], U32, name=f"woven{first}", tag=f"ring{4 + g % 2}", align_bytes=64)
-                for u in range(2):
-                    nc.vector.tensor_copy(woven[:, :, u], windows[u].indirect(lst))
-            codes = keep.tile([P, width], U32, name=f"codes{first}", align_bytes=64)
+            codes = keep.tile([P, width], U32, name=f"codes{first}", tag=tag, align_bytes=64)
             plane = keep.tile([P, width], U8, name=f"plane{first}", align_bytes=64)
-            nc.vector.quantize_mx(
-                out=codes[:].bitcast(FP8X4),
-                scales=plane[:],
-                in_=woven[:].rearrange("p s u -> p (s u)").bitcast(BF16),
-            )
-            if g == 0:
+            nc.vector.quantize_mx(out=codes[:].bitcast(FP8X4), scales=plane[:], in_=rows)
+            if first == 0:
                 quantise_w2(w2_last, 6, 8, codes_tile(6, 8, "woven0"))
-            acc = bank(2 + g)
             for e in range(first, last):
                 cols = slice((e - first) * C, (e - first + 1) * C)
                 nc.tensor.matmul_mx(
@@ -301,6 +296,29 @@ def tile_moe_ser_none_kernel(
                     stop=True,
                 )
             nc.scalar.copy(y_sb[:, first * C : last * C], acc[:, :width])
+
+        last_rows = keep.tile([P, C, PACK], BF16, name="last_rows", align_bytes=64)
+        for u in range(2):
+            for d in range(2):
+                nc.scalar.activation(
+                    last_rows[:, :, 2 * u + d], c_planes[:, u, d, :].indirect(entries(offs2_sb, 7 * C, 8 * C)), COPY
+                )
+        for g, (first, last) in enumerate(SECOND_GROUPS):
+            width = (last - first) * C
+            lst = entries(offs2_sb, first * C, last * C)
+            woven = keep.tile([P, width, 2], U32, name=f"woven{first}", align_bytes=64)
+            cg = keep.tile([P, 2, width], U32, name=f"cg{first}", tag=f"ring{4 + g % 2}", align_bytes=64)
+            for u in range(2):
+                nc.vector.tensor_copy(cg[:, u, :], windows[u].indirect(lst))
+            nc.gpsimd.tensor_copy(woven[:], cg[:].rearrange("p u s -> p s u"))
+            quantise_and_multiply(
+                woven[:].rearrange("p s u -> p (s u)").bitcast(BF16), first, last, f"codes{first}", bank(2 + g)
+            )
+        woven = keep.tile([P, C, 2], U32, name="woven6", tag="ring5", align_bytes=64)
+        for u in range(2):
+            nc.vector.tensor_copy(woven[:, :, u], windows[u].indirect(entries(offs2_sb, 6 * C, 7 * C)))
+        quantise_and_multiply(last_rows[:].rearrange("p s j -> p (s j)"), 7, 8, "woven4", bank(5))
+        quantise_and_multiply(woven[:].rearrange("p s u -> p (s u)").bitcast(BF16), 6, 7, "codes6", bank(6))
 
         first_part = keep.tile([P, T], F32, name="first_part")
         nc.vector.tensor_tensor(first_part[:], y_sb[:].indirect(pos3_sb[:]), gate2_sb[:, 0, :], MULT)

@@ -282,8 +282,6 @@ def tile_moe_ser_none_kernel(
             codes = keep.tile([P, width], U32, name=f"codes{first}", tag=tag, align_bytes=64)
             plane = keep.tile([P, width], U8, name=f"plane{first}", align_bytes=64)
             nc.vector.quantize_mx(out=codes[:].bitcast(FP8X4), scales=plane[:], in_=rows)
-            if first == 0:
-                quantise_w2(w2_last, 6, 8, codes_tile(6, 8, "woven0"))
             for e in range(first, last):
                 cols = slice((e - first) * C, (e - first + 1) * C)
                 nc.tensor.matmul_mx(
@@ -317,6 +315,7 @@ def tile_moe_ser_none_kernel(
         woven = keep.tile([P, C, 2], U32, name="woven6", tag="ring5", align_bytes=64)
         for u in range(2):
             nc.vector.tensor_copy(woven[:, :, u], windows[u].indirect(entries(offs2_sb, 6 * C, 7 * C)))
+        quantise_w2(w2_last, 6, 8, codes_tile(6, 8, "ring4"))
         quantise_and_multiply(last_rows[:].rearrange("p s j -> p (s j)"), 7, 8, "woven4", bank(5))
         quantise_and_multiply(woven[:].rearrange("p s u -> p (s u)").bitcast(BF16), 6, 7, "codes6", bank(6))
 

@@ -54,8 +54,6 @@ def tile_moe_ser_none_kernel(
         x_plane = keep.tile([P, PLANE_WINDOW], U8, name="x_plane", align_bytes=64)
         nc.gpsimd.memset(x_plane[:, :T].bitcast(I32), 0)
         nc.vector.memset(x_plane[:, T:].bitcast(I32), 0)
-        gate1_cols = keep.tile([P, 2, PACK], F32, name="gate1_cols")
-        nc.gpsimd.dma_start(gate1_cols[:], gate1[:, 0, :].rearrange("r (p j) -> p r j", j=PACK))
         sg = [keep.tile([P, S], U8, name=f"sg{s}", align_bytes=64) for s in range(PASSES)]
         nc.gpsimd.memset(sg[1][:].bitcast(I32), 0)
         w1_planes = [keep.tile([P, E * PASSES, H // 2], U8, name=f"w1_plane{i}", align_bytes=64) for i in range(2)]
@@ -100,24 +98,25 @@ def tile_moe_ser_none_kernel(
             )
         nc.sync.dma_start(x_sb[:, :, :T], x_words.rearrange("s p t d -> p s (t d)").bitcast(I32))
         load_w1_scales(0, range(0, 1))
-        pos1_sb = load_list("pos1_sb", pos1)
+        gate1_cols = keep.tile([P, 2, PACK], F32, name="gate1_cols")
+        nc.sync.dma_start(gate1_cols[:], gate1[:, 0, :].rearrange("r (p j) -> p r j", j=PACK))
         load_w1(0, 8, range(0, 2))
         load_w1_scales(0, range(1, 4))
         nc.vector.tensor_copy(sg[0][:], x_plane[:].indirect(offs_sb[:]))
         for r in range(4):
             nc.sync.dma_start(sg[1][r:P:32].bitcast(I32), sg[0][4 + r : P : 32].bitcast(I32))
+        pos1_sb = load_list("pos1_sb", pos1)
         pos2_sb = load_list("pos2_sb", pos2)
         load_w1(0, 4, range(2, 4))
         load_w1_scales(1, range(4))
         load_w1(4, 8, range(2, 4))
         shared = keep.tile([P, W2_START + E // 2 * PACK * N], F32, name="shared", tag="shared", align_bytes=64)
         w2_raw = {0: shared[:, W2_START:].rearrange("p (e j n) -> p e j n", j=PACK, n=N)}
-        for first in (4, 6):
-            raw = keep.tile([P, 2, PACK, N], F32, name=f"w2_raw{first}", tag=f"ring{first}", align_bytes=64)
-            w2_raw[first] = raw[:]
+        w2_second = keep.tile([P, 4, PACK, N], F32, name="w2_second", align_bytes=64)
+        w2_raw[4] = w2_second[:, :2]
+        w2_raw[6] = w2_second[:, 2:]
         load_w2(0, 4, w2_raw[0])
-        load_w2(4, 6, w2_raw[4])
-        load_w2(6, 8, w2_raw[6])
+        load_w2(4, 8, w2_second[:])
         offs2_sb = load_list("offs2_sb", offs2)
         gate2_sb = keep.tile([P, 2, T], F32, name="gate2_sb", align_bytes=64)
         nc.sync.dma_start(gate2_sb[:], gate2.rearrange("r p t -> p r t"))

@@ -27,7 +27,6 @@ TOKEN_BLOCKS = T // P
 SPARE = 192
 WINDOW = T + SPARE
 PLANE_WINDOW = 1408
-W2_START = T * 2 - 3 * P // 4
 SECOND_GROUPS = ((0, 2), (2, 4), (4, 6))
 
 
@@ -51,15 +50,23 @@ def tile_moe_ser_none_kernel(
             nc.sync.dma_start(lst[:], src)
             return lst
 
+        def vector_gather(dst, window):
+            nc.vector.tensor_copy(dst, window)
+
+        def scalar_gather(dst, window):
+            nc.scalar.activation(dst, window, COPY)
+
         x_plane = keep.tile([P, PLANE_WINDOW], U8, name="x_plane", align_bytes=64)
         nc.gpsimd.memset(x_plane[:, :T].bitcast(I32), 0)
-        nc.vector.memset(x_plane[:, T:].bitcast(I32), 0)
+        gate1_rows = keep.tile([P, P], F32, name="gate1_rows")
+        nc.gpsimd.memset(gate1_rows[:], 0.0)
+        w1_plane = keep.tile([P, E * PASSES, H], U8, name="w1_plane", align_bytes=64)
+        nc.gpsimd.memset(w1_plane[:, :E].rearrange("p g i -> p (g i)").bitcast(I32), 0)
+        nc.vector.memset(w1_plane[:, E:].rearrange("p g i -> p (g i)").bitcast(I32), 0)
         sg = [keep.tile([P, S], U8, name=f"sg{s}", align_bytes=64) for s in range(PASSES)]
         nc.gpsimd.memset(sg[1][:].bitcast(I32), 0)
-        w1_planes = [keep.tile([P, E * PASSES, H // 2], U8, name=f"w1_plane{i}", align_bytes=64) for i in range(2)]
-        for plane in w1_planes:
-            nc.vector.memset(plane[:].rearrange("p g i -> p (g i)").bitcast(I32), 0)
 
+        nc.vector.memset(x_plane[:, T:].bitcast(I32), 0)
         x_sb = keep.tile([P, PASSES, WINDOW], I32, name="x_sb", align_bytes=64)
         nc.vector.memset(x_sb[:, :, T:], 0)
 
@@ -77,19 +84,21 @@ def tile_moe_ser_none_kernel(
                 for k, m in enumerate(tiles):
                     w1_sb[e, m] = words[:, e - first, :, 2 * P * k : 2 * P * (k + 1)]
 
-        def load_w2(first, last, raw):
+        w2_raw = {}
+
+        def load_w2(first, last):
+            raw = keep.tile([P, last - first, PACK, N], F32, name=f"w2_raw{first}", align_bytes=64)
             nc.sync.dma_start(
-                raw.rearrange("p e j n -> p e (j n)"),
+                raw[:].rearrange("p e j n -> p e (j n)"),
                 w2[first:last].rearrange("e (p j) n -> p e (j n)", j=PACK),
             )
+            for e in range(first, last):
+                w2_raw[e] = raw[:, e - first]
 
-        def load_w1_scales(half, residues):
+        def load_w1_scales(residues):
             rows = w1_scales.rearrange("e s (q r) i -> r q (e s) i", r=4)
             for r in residues:
-                nc.sync.dma_start(
-                    w1_planes[half][r:P:32].bitcast(I32),
-                    rows[r][:, :, half * H // 2 : (half + 1) * H // 2].bitcast(I32),
-                )
+                nc.sync.dma_start(w1_plane[r:P:32].bitcast(I32), rows[r].bitcast(I32))
 
         offs_sb = load_list("offs_sb", offs)
         for q in range(4):
@@ -97,26 +106,21 @@ def tile_moe_ser_none_kernel(
                 x_plane[32 * q : 32 * q + 8, :T].bitcast(I32), x_scales[:, 4 * q : 4 * q + 4, :].bitcast(I32)
             )
         nc.sync.dma_start(x_sb[:, :, :T], x_words.rearrange("s p t d -> p s (t d)").bitcast(I32))
-        load_w1_scales(0, range(0, 1))
-        gate1_cols = keep.tile([P, 2, PACK], F32, name="gate1_cols")
-        nc.sync.dma_start(gate1_cols[:], gate1[:, 0, :].rearrange("r (p j) -> p r j", j=PACK))
-        load_w1(0, 8, range(0, 2))
-        load_w1_scales(0, range(1, 4))
+        nc.sync.dma_start(
+            gate1_rows[: 2 * TOKEN_BLOCKS, :], gate1[:, 0, :].rearrange("r (q c) -> r q c", c=P)
+        )
+        load_w1_scales(range(4))
+        load_w1(0, 2, range(0, 4))
+        load_w1(2, 4, range(0, 4))
         nc.vector.tensor_copy(sg[0][:], x_plane[:].indirect(offs_sb[:]))
         for r in range(4):
             nc.sync.dma_start(sg[1][r:P:32].bitcast(I32), sg[0][4 + r : P : 32].bitcast(I32))
+        load_w1(4, 8, range(0, 2))
+        load_w1(4, 8, range(2, 4))
         pos1_sb = load_list("pos1_sb", pos1)
         pos2_sb = load_list("pos2_sb", pos2)
-        load_w1(0, 4, range(2, 4))
-        load_w1_scales(1, range(4))
-        load_w1(4, 8, range(2, 4))
-        shared = keep.tile([P, W2_START + E // 2 * PACK * N], F32, name="shared", tag="shared", align_bytes=64)
-        w2_raw = {0: shared[:, W2_START:].rearrange("p (e j n) -> p e j n", j=PACK, n=N)}
-        w2_second = keep.tile([P, 4, PACK, N], F32, name="w2_second", align_bytes=64)
-        w2_raw[4] = w2_second[:, :2]
-        w2_raw[6] = w2_second[:, 2:]
-        load_w2(0, 4, w2_raw[0])
-        load_w2(4, 8, w2_second[:])
+        load_w2(0, 4)
+        load_w2(4, 8)
         offs2_sb = load_list("offs2_sb", offs2)
         gate2_sb = keep.tile([P, 2, T], F32, name="gate2_sb", align_bytes=64)
         nc.sync.dma_start(gate2_sb[:], gate2.rearrange("r p t -> p r t"))
@@ -127,47 +131,13 @@ def tile_moe_ser_none_kernel(
         make_identity(nc, ident[:])
         ident_bf = keep.tile([P, P], BF16, name="ident_bf")
         make_identity(nc, ident_bf[:])
-        c_words = keep.tile([P, 2, T], F32, name="c_words", align_bytes=64)
 
-        gate1_sb = keep.tile([P, 2, T], F32, name="gate1_sb", align_bytes=64)
-        for r in range(2):
-            spread = bank(6 + r)
-            for j in range(PACK):
-                nc.tensor.transpose(
-                    spread[:, j * P : (j + 1) * P], gate1_cols[:, r, j : j + 1].to_broadcast([P, P]), ident[:]
-                )
-            nc.scalar.copy(
-                gate1_sb[:, r, :].rearrange("m (p j) -> m p j", j=PACK), spread[:].rearrange("m (j p) -> m p j", j=PACK)
-            )
+        gate1_cols = keep.tile([P, 2 * TOKEN_BLOCKS], F32, name="gate1_cols")
+        turned_gates = bank(7)
+        nc.tensor.transpose(turned_gates[:, :P], gate1_rows[:], ident[:])
+        nc.scalar.copy(gate1_cols[:], turned_gates[:, : 2 * TOKEN_BLOCKS])
 
-        def w2_tile(first, last, tag):
-            grouped = keep.tile([P, last - first, N, PACK], BF16, name=f"w2_bf{first}", tag=tag, align_bytes=64)
-            return grouped[:]
-
-        def codes_tile(first, last, tag):
-            codes = keep.tile([P, (last - first) * N], U32, name=f"w2_codes{first}", tag=tag, align_bytes=64)
-            return codes[:]
-
-        def round_w2(copy, first, grouped):
-            copy(
-                grouped.rearrange("p e (c i) j -> p e c j i", i=4),
-                w2_raw[first].rearrange("p e j (c i) -> p e c j i", i=4),
-            )
-            return grouped
-
-        w2_codes = {}
-        w2_plane = keep.tile([P, E * N], U8, name="w2_plane", align_bytes=64)
-
-        def quantise_w2(grouped, first, last, codes):
-            nc.vector.quantize_mx(
-                out=codes.bitcast(FP8X4),
-                scales=w2_plane[:, first * N : last * N],
-                in_=grouped.rearrange("p e n j -> p (e n j)"),
-            )
-            for e in range(first, last):
-                w2_codes[e] = codes[:, (e - first) * N : (e - first + 1) * N]
-
-        h_sb = [keep.tile([P, S], F32, name=f"h_sb{m}", tag=f"h{m}", align_bytes=64) for m in range(ROW_TILES)]
+        h_sb = [keep.tile([P, S], F32, name=f"h_sb{m}", align_bytes=64) for m in range(ROW_TILES)]
         xg = keep.tile([P, PASSES, S], U32, name="xg", align_bytes=64)
 
         def gather_words(s, lo, hi):
@@ -177,101 +147,119 @@ def tile_moe_ser_none_kernel(
             )
 
         gather_words(0, 0, 4)
-        gather_words(0, 4, 8)
         gather_words(1, 0, 4)
+        gather_words(0, 4, 8)
         gather_words(1, 4, 7)
         gather_words(1, 7, 8)
 
-        def multiply(acc, s, m, first, last):
-            for e in range(first, last):
-                nc.tensor.matmul_mx(
-                    acc[:, (e - first) * C : (e - first + 1) * C],
-                    lhsT=w1_sb[e, m][:, s, :].bitcast(FP4X4),
-                    lhsT_scale=w1_planes[m // 2][:, e * PASSES + s, (m % 2) * P : (m % 2 + 1) * P],
-                    rhs=xg[:, s, e * C : (e + 1) * C].bitcast(FP8X4),
-                    rhs_scale=sg[s][:, e * C : (e + 1) * C],
-                    start=(s == 0 and e == first),
-                    stop=(s == PASSES - 1 and e == last - 1),
-                )
-
-        tile0 = ((0, 4, nc.scalar.copy), (4, 7, nc.vector.tensor_copy), (7, 8, nc.scalar.copy))
-        accs = [bank(index) for index in range(len(tile0))]
-        for acc, (first, last, copy) in zip(accs, tile0):
-            multiply(acc, 0, 0, first, last)
-        for acc, (first, last, copy) in zip(accs, tile0):
-            multiply(acc, 1, 0, first, last)
-            copy(h_sb[0][:, first * C : last * C], acc[:, : (last - first) * C])
-        for index, (m, first) in zip((0, 1, 5, 6, 7, 3), ((1, 0), (1, 4), (2, 0), (3, 0), (2, 4), (3, 4))):
+        def multiply(index, m, first, last, copy):
             acc = bank(index)
             for s in range(PASSES):
-                multiply(acc, s, m, first, first + 4)
-            nc.scalar.copy(h_sb[m][:, first * C : (first + 4) * C], acc[:])
-
-        def gather_and_turn(blocks, tiles, total):
-            toks = slice(blocks.start * P, blocks.stop * P)
-            for k, m in enumerate(tiles):
-                for r, pos_sb in enumerate((pos1_sb, pos2_sb)):
-                    part = keep.tile([P, len(blocks) * P], F32, name=f"part{m}_{r}_{blocks.start}", align_bytes=64)
-                    nc.vector.tensor_tensor(
-                        part[:], h_sb[m][:].indirect(entries(pos_sb, toks.start, toks.stop)), gate1_sb[:, r, toks], MULT
+                for e in range(first, last):
+                    nc.tensor.matmul_mx(
+                        acc[:, (e - first) * C : (e - first + 1) * C],
+                        lhsT=w1_sb[e, m][:, s, :].bitcast(FP4X4),
+                        lhsT_scale=w1_plane[:, e * PASSES + s, m * P : (m + 1) * P],
+                        rhs=xg[:, s, e * C : (e + 1) * C].bitcast(FP8X4),
+                        rhs_scale=sg[s][:, e * C : (e + 1) * C],
+                        start=(s == 0 and e == first),
+                        stop=(s == PASSES - 1 and e == last - 1),
                     )
-                    for b in range(len(blocks)):
-                        place = b * len(tiles) + k
-                        nc.tensor.matmul(
-                            total[:, place * P : (place + 1) * P],
-                            part[:, b * P : (b + 1) * P],
-                            ident[:],
-                            is_transpose=True,
-                            start=(k == 0 and r == 0 and b == 0),
-                            stop=(k == len(tiles) - 1 and r == 1 and b == len(blocks) - 1),
-                        )
+            copy(h_sb[m][:, first * C : last * C], acc[:, : (last - first) * C])
 
-        def round_rows(copy, c_rows, total, blocks, tiles):
-            copy(
-                c_rows[:, :, :, tiles.start * 32 : tiles.stop * 32, :],
-                total[:, : len(blocks) * len(tiles) * P].rearrange("t (q p u d) -> t q u p d", q=len(blocks), u=2, d=2),
-            )
+        for m in range(3):
+            multiply(m, m, 0, 4, nc.scalar.copy)
+        multiply(3, 0, 4, 7, nc.vector.tensor_copy)
+        multiply(4, 0, 7, 8, nc.scalar.copy)
+        for index, m, first in ((5, 1, 4), (6, 2, 4), (3, 3, 0), (7, 3, 4)):
+            multiply(index, m, first, first + 4, nc.scalar.copy)
 
-        def turn_back(copy, blocks, u, back):
+        w2_bf = [keep.tile([P, 4, N, PACK], BF16, name=f"w2_bf{i}", tag=f"w2_bf{i}", align_bytes=64) for i in range(2)]
+        for e in range(E):
+            nc.gpsimd.tensor_scalar(w2_bf[e // 4][:, e % 4], w2_raw[e].rearrange("p j n -> p n j"), 1.0, 0.0, MULT, ADD)
+
+        turned = [[bank(index) for index in indices] for indices in ((1, 2, 4, 0), (5, 6, 3, 7))]
+        pos_sb = (pos1_sb, pos2_sb)
+
+        def gather_and_turn(gather, m, r, blocks):
+            part = keep.tile([P, len(blocks) * P], F32, name=f"part{m}_{r}_{blocks.start}", align_bytes=64)
+            gather(part[:], h_sb[m][:].indirect(entries(pos_sb[r], blocks.start * P, blocks.stop * P)))
             for k, q in enumerate(blocks):
+                nc.tensor.transpose(
+                    turned[r][q][:, m * P : (m + 1) * P],
+                    part[:, k * P : (k + 1) * P],
+                    ident[:],
+                )
+
+        every = range(TOKEN_BLOCKS)
+        gather_and_turn(vector_gather, 0, 0, every)
+        gather_and_turn(vector_gather, 0, 1, every)
+        gather_and_turn(scalar_gather, 1, 0, every)
+        gather_and_turn(vector_gather, 1, 1, every)
+        gather_and_turn(scalar_gather, 2, 0, every)
+        gather_and_turn(vector_gather, 2, 1, every)
+        gather_and_turn(scalar_gather, 3, 0, every)
+        gather_and_turn(vector_gather, 3, 1, range(0, 2))
+        gather_and_turn(vector_gather, 3, 1, range(2, 4))
+
+        w2_codes = {}
+        w2_plane = keep.tile([P, E * N], U8, name="w2_plane", align_bytes=64)
+
+        def quantise_w2(first, last, tag):
+            codes = keep.tile([P, (last - first) * N], U32, name=f"w2_codes{first}", tag=tag, align_bytes=64)
+            nc.vector.quantize_mx(
+                out=codes[:].bitcast(FP8X4),
+                scales=w2_plane[:, first * N : last * N],
+                in_=w2_bf[first // 4][:, first % 4 : first % 4 + last - first].rearrange("p e n j -> p (e n j)"),
+            )
+            for e in range(first, last):
+                w2_codes[e] = codes[:, (e - first) * N : (e - first + 1) * N]
+
+        quantise_w2(0, 4, "w2_codes0")
+        c_rows = keep.tile([P, TOKEN_BLOCKS, 2, P, 2], BF16, name="c_rows", tag="w2_bf0", align_bytes=64)
+        c_words = keep.tile([P, 2, T], F32, name="c_words", align_bytes=64)
+
+        def turn_back(copy, q, halves, back):
+            for k, u in enumerate(halves):
                 nc.tensor.transpose(
                     back[:, k * P : (k + 1) * P], c_rows[:, q, u].rearrange("t p d -> t (p d)").bitcast(F32), ident[:]
                 )
-            copy(c_words[:, u, blocks.start * P : blocks.stop * P], back[:, : len(blocks) * P])
+            copy(
+                c_words[:, halves.start : halves.stop, q * P : (q + 1) * P],
+                back[:, : len(halves) * P].rearrange("p (u t) -> p u t", t=P),
+            )
 
-        c_rows = shared[:, : T * 2].bitcast(BF16).rearrange("t (q u p d) -> t q u p d", u=2, p=P, d=2)
-        for m, index in enumerate((6, 7, 3)):
-            total = bank(index)
-            gather_and_turn(range(0, 4), range(m, m + 1), total)
-            round_rows(nc.scalar.copy, c_rows, total, range(0, 4), range(m, m + 1))
-            if m == 0:
-                w2_first = round_w2(nc.scalar.copy, 0, w2_tile(0, 4, "w2_bf0"))
-        last_tile = range(3, 4)
-        for blocks, index, back in ((range(2, 4), 4, 5), (range(1, 2), 3, 7)):
-            total = bank(index)
-            gather_and_turn(blocks, last_tile, total)
-            round_rows(nc.scalar.copy, c_rows[:, blocks.start : blocks.stop], total, blocks, last_tile)
-            turn_back(nc.scalar.copy, blocks, 0, bank(back))
-        total = bank(4)
-        gather_and_turn(range(0, 1), last_tile, total)
-        round_rows(nc.vector.tensor_copy, c_rows[:, 0:1], total, range(0, 1), last_tile)
-        turn_back(nc.scalar.copy, range(1, 4), 1, bank(3))
-        turn_back(nc.scalar.copy, range(0, 1), 0, bank(6))
-        turn_back(nc.vector.tensor_copy, range(0, 1), 1, bank(1))
+        def by_half(rows):
+            return rows[:].rearrange("t (p u d) -> t u p d", u=2, d=2)
 
-        w2_middle = round_w2(nc.vector.tensor_copy, 4, w2_tile(4, 6, "h3"))
-        early_codes = codes_tile(0, 6, "part3_1_0")
-        quantise_w2(w2_first, 0, 4, early_codes[:, : 4 * N])
-        quantise_w2(w2_middle, 4, 6, early_codes[:, 4 * N :])
-        w2_last = round_w2(nc.scalar.copy, 6, w2_tile(6, 8, "h3"))
+        scaled = []
+        for q in range(TOKEN_BLOCKS):
+            scaled.append(keep.tile([P, 2, P, 2], F32, name=f"scaled{q}", tag=f"scaled{q}", align_bytes=64))
+            nc.scalar.activation(scaled[q][:], by_half(turned[0][q]), COPY, scale=gate1_cols[:, q : q + 1])
+        for q in range(TOKEN_BLOCKS):
+            for u in range(2):
+                nc.vector.scalar_tensor_tensor(
+                    c_rows[:, q, u],
+                    by_half(turned[1][q])[:, u],
+                    gate1_cols[:, TOKEN_BLOCKS + q : TOKEN_BLOCKS + q + 1],
+                    scaled[q][:, u],
+                    MULT,
+                    ADD,
+                )
+        for q in range(TOKEN_BLOCKS - 1):
+            turn_back(nc.scalar.copy, q, range(0, 2), bank((1, 2, 4)[q]))
+        turn_back(nc.scalar.copy, TOKEN_BLOCKS - 1, range(0, 1), bank(0))
+        turn_back(nc.vector.tensor_copy, TOKEN_BLOCKS - 1, range(1, 2), bank(5))
+
+        quantise_w2(4, 6, "scaled3")
 
         c_planes = keep.tile([P, 2, 2, T], BF16, name="c_planes", align_bytes=64)
-        for u, index in enumerate((0, 7)):
-            turned = psum.tile([P, 2, T], BF16, name=f"turned{u}", tag=f"bank{index}")
+        for u, index in enumerate((6, 3)):
+            planes = psum.tile([P, 2, T], BF16, name=f"planes{u}", tag=f"bank{index}")
             for d in range(2):
                 for q in range(TOKEN_BLOCKS):
-                    nc.tensor.transpose(turned[:, d, q * P : (q + 1) * P], c_rows[:, q, u, :, d], ident_bf[:])
-            nc.scalar.copy(c_planes[:, u], turned[:])
+                    nc.tensor.transpose(planes[:, d, q * P : (q + 1) * P], c_rows[:, q, u, :, d], ident_bf[:])
+            nc.scalar.copy(c_planes[:, u], planes[:])
 
         windows = [c_words[:, u, :].bitcast(U32) for u in range(2)]
         y_sb = keep.tile([P, S], F32, name="y_sb")
@@ -304,30 +292,30 @@ def tile_moe_ser_none_kernel(
             width = (last - first) * C
             lst = entries(offs2_sb, first * C, last * C)
             woven = keep.tile([P, width, 2], U32, name=f"woven{first}", align_bytes=64)
-            cg = keep.tile([P, 2, width], U32, name=f"cg{first}", tag=f"ring{4 + g % 2}", align_bytes=64)
+            cg = keep.tile([P, 2, width], U32, name=f"cg{first}", tag=f"ring{g % 2}", align_bytes=64)
             for u in range(2):
                 nc.vector.tensor_copy(cg[:, u, :], windows[u].indirect(lst))
             nc.gpsimd.tensor_copy(woven[:], cg[:].rearrange("p u s -> p s u"))
             quantise_and_multiply(
-                woven[:].rearrange("p s u -> p (s u)").bitcast(BF16), first, last, f"codes{first}", bank(2 + g)
+                woven[:].rearrange("p s u -> p (s u)").bitcast(BF16), first, last, f"codes{first}", bank((1, 2, 4)[g])
             )
-        woven = keep.tile([P, C, 2], U32, name="woven6", tag="ring5", align_bytes=64)
+        woven = keep.tile([P, C, 2], U32, name="woven6", tag="ring1", align_bytes=64)
         for u in range(2):
             nc.vector.tensor_copy(woven[:, :, u], windows[u].indirect(entries(offs2_sb, 6 * C, 7 * C)))
-        quantise_w2(w2_last, 6, 8, codes_tile(6, 8, "ring4"))
-        quantise_and_multiply(last_rows[:].rearrange("p s j -> p (s j)"), 7, 8, "woven4", bank(5))
-        quantise_and_multiply(woven[:].rearrange("p s u -> p (s u)").bitcast(BF16), 6, 7, "codes6", bank(6))
+        quantise_w2(6, 8, "ring0")
+        quantise_and_multiply(last_rows[:].rearrange("p s j -> p (s j)"), 7, 8, "woven4", bank(0))
+        quantise_and_multiply(woven[:].rearrange("p s u -> p (s u)").bitcast(BF16), 6, 7, "codes6", bank(5))
 
+        halves = (slice(0, T // 2), slice(T // 2, T))
         first_part = keep.tile([P, T], F32, name="first_part")
         nc.vector.tensor_tensor(first_part[:], y_sb[:].indirect(pos3_sb[:]), gate2_sb[:, 0, :], MULT)
-        halves = (slice(0, T // 2), slice(T // 2, T))
         parts = []
         for hh, toks in enumerate(halves):
-            parts.append(keep.tile([P, toks.stop - toks.start], F32, name=f"second_part{hh}"))
-            nc.vector.tensor_tensor(
-                parts[hh][:], y_sb[:].indirect(entries(pos4_sb, toks.start, toks.stop)), gate2_sb[:, 1, toks], MULT
-            )
+            picked = keep.tile([P, T // 2], F32, name=f"picked{hh}")
+            scalar_gather(picked[:], y_sb[:].indirect(entries(pos4_sb, toks.start, toks.stop)))
+            parts.append(keep.tile([P, T // 2], F32, name=f"second_part{hh}"))
+            nc.vector.tensor_tensor(parts[hh][:], picked[:], gate2_sb[:, 1, toks], MULT)
         for hh, toks in enumerate(halves):
-            total = keep.tile([P, toks.stop - toks.start], F32, name=f"total{hh}")
+            total = keep.tile([P, T // 2], F32, name=f"total{hh}")
             nc.vector.tensor_tensor(total[:], first_part[:, toks], parts[hh][:], ADD)
             nc.sync.dma_start(out[:, toks], total[:])

@@ -60,11 +60,11 @@ def tile_moe_ser_none_kernel(
         nc.gpsimd.memset(x_plane[:, :T].bitcast(I32), 0)
         gate1_rows = keep.tile([P, P], F32, name="gate1_rows")
         nc.gpsimd.memset(gate1_rows[:], 0.0)
-        w1_plane = keep.tile([P, E * PASSES, H], U8, name="w1_plane", align_bytes=64)
-        nc.gpsimd.memset(w1_plane[:, :E].rearrange("p g i -> p (g i)").bitcast(I32), 0)
-        nc.vector.memset(w1_plane[:, E:].rearrange("p g i -> p (g i)").bitcast(I32), 0)
         sg = [keep.tile([P, S], U8, name=f"sg{s}", align_bytes=64) for s in range(PASSES)]
         nc.gpsimd.memset(sg[1][:].bitcast(I32), 0)
+        w1_planes = [keep.tile([P, E * PASSES, H // 2], U8, name=f"w1_plane{i}", align_bytes=64) for i in range(2)]
+        for plane in w1_planes:
+            nc.vector.memset(plane[:].rearrange("p g i -> p (g i)").bitcast(I32), 0)
 
         nc.vector.memset(x_plane[:, T:].bitcast(I32), 0)
         x_sb = keep.tile([P, PASSES, WINDOW], I32, name="x_sb", align_bytes=64)
@@ -74,7 +74,7 @@ def tile_moe_ser_none_kernel(
 
         def load_w1(first, last, tiles):
             width = 2 * P * len(tiles)
-            words = keep.tile([P, last - first, PASSES, width], U8, name=f"w1_sb{first}_{tiles.start}", align_bytes=64)
+            words = keep.tile([P, last - first, PASSES, width], U8, name=f"w1_sb{first}_{tiles.start}", tag=f"w1_sb{first}_{tiles.start}", align_bytes=64)
             rows = w1_words[first:last].rearrange("e s p b -> p (e s) b")
             nc.sync.dma_start(
                 words[:].rearrange("p e s b -> p (e s) b").bitcast(I32),
@@ -95,10 +95,13 @@ def tile_moe_ser_none_kernel(
             for e in range(first, last):
                 w2_raw[e] = raw[:, e - first]
 
-        def load_w1_scales(residues):
+        def load_w1_scales(half):
             rows = w1_scales.rearrange("e s (q r) i -> r q (e s) i", r=4)
-            for r in residues:
-                nc.sync.dma_start(w1_plane[r:P:32].bitcast(I32), rows[r].bitcast(I32))
+            for r in range(4):
+                nc.sync.dma_start(
+                    w1_planes[half][r:P:32].bitcast(I32),
+                    rows[r][:, :, half * H // 2 : (half + 1) * H // 2].bitcast(I32),
+                )
 
         offs_sb = load_list("offs_sb", offs)
         for q in range(4):
@@ -109,16 +112,17 @@ def tile_moe_ser_none_kernel(
         nc.sync.dma_start(
             gate1_rows[: 2 * TOKEN_BLOCKS, :], gate1[:, 0, :].rearrange("r (q c) -> r q c", c=P)
         )
-        load_w1_scales(range(4))
-        load_w1(0, 2, range(0, 4))
-        load_w1(2, 4, range(0, 4))
+        load_w1_scales(0)
+        load_w1(0, 4, range(0, 2))
         nc.vector.tensor_copy(sg[0][:], x_plane[:].indirect(offs_sb[:]))
         for r in range(4):
             nc.sync.dma_start(sg[1][r:P:32].bitcast(I32), sg[0][4 + r : P : 32].bitcast(I32))
         load_w1(4, 8, range(0, 2))
-        load_w1(4, 8, range(2, 4))
         pos1_sb = load_list("pos1_sb", pos1)
         pos2_sb = load_list("pos2_sb", pos2)
+        load_w1_scales(1)
+        load_w1(0, 4, range(2, 4))
+        load_w1(4, 8, range(2, 4))
         load_w2(0, 4)
         load_w2(4, 8)
         offs2_sb = load_list("offs2_sb", offs2)
@@ -152,37 +156,43 @@ def tile_moe_ser_none_kernel(
         gather_words(1, 4, 7)
         gather_words(1, 7, 8)
 
-        def multiply(index, m, first, last, copy):
-            acc = bank(index)
-            for s in range(PASSES):
-                for e in range(first, last):
-                    nc.tensor.matmul_mx(
-                        acc[:, (e - first) * C : (e - first + 1) * C],
-                        lhsT=w1_sb[e, m][:, s, :].bitcast(FP4X4),
-                        lhsT_scale=w1_plane[:, e * PASSES + s, m * P : (m + 1) * P],
-                        rhs=xg[:, s, e * C : (e + 1) * C].bitcast(FP8X4),
-                        rhs_scale=sg[s][:, e * C : (e + 1) * C],
-                        start=(s == 0 and e == first),
-                        stop=(s == PASSES - 1 and e == last - 1),
-                    )
-            copy(h_sb[m][:, first * C : last * C], acc[:, : (last - first) * C])
+        def multiply(acc, s, m, first, last):
+            for e in range(first, last):
+                nc.tensor.matmul_mx(
+                    acc[:, (e - first) * C : (e - first + 1) * C],
+                    lhsT=w1_sb[e, m][:, s, :].bitcast(FP4X4),
+                    lhsT_scale=w1_planes[m // 2][:, e * PASSES + s, (m % 2) * P : (m % 2 + 1) * P],
+                    rhs=xg[:, s, e * C : (e + 1) * C].bitcast(FP8X4),
+                    rhs_scale=sg[s][:, e * C : (e + 1) * C],
+                    start=(s == 0 and e == first),
+                    stop=(s == PASSES - 1 and e == last - 1),
+                )
 
-        for m in range(3):
-            multiply(m, m, 0, 4, nc.scalar.copy)
-        multiply(3, 0, 4, 7, nc.vector.tensor_copy)
-        multiply(4, 0, 7, 8, nc.scalar.copy)
-        for index, m, first in ((5, 1, 4), (6, 2, 4), (3, 3, 0), (7, 3, 4)):
-            multiply(index, m, first, first + 4, nc.scalar.copy)
+        def multiply_by_pass(groups):
+            accs = [bank(index) for index, m, first, last, copy in groups]
+            for acc, (index, m, first, last, copy) in zip(accs, groups):
+                multiply(acc, 0, m, first, last)
+            for acc, (index, m, first, last, copy) in zip(accs, groups):
+                multiply(acc, 1, m, first, last)
+                copy(h_sb[m][:, first * C : last * C], acc[:, : (last - first) * C])
+
+        multiply_by_pass(((0, 0, 0, 4, nc.scalar.copy), (1, 1, 0, 4, nc.scalar.copy)))
+        multiply_by_pass(((3, 0, 4, 7, nc.vector.tensor_copy), (4, 0, 7, 8, nc.scalar.copy)))
+        multiply_by_pass(((5, 1, 4, 8, nc.scalar.copy),))
+        for indices, first in (((2, 6, 7, 0), 0), ((1, 3, 4, 5), 4)):
+            for k, index in enumerate(indices):
+                lo = first + 2 * (k % 2)
+                multiply_by_pass(((index, 2 + k // 2, lo, lo + 2, nc.scalar.copy),))
 
         w2_bf = [keep.tile([P, 4, N, PACK], BF16, name=f"w2_bf{i}", tag=f"w2_bf{i}", align_bytes=64) for i in range(2)]
         for e in range(E):
             nc.gpsimd.tensor_scalar(w2_bf[e // 4][:, e % 4], w2_raw[e].rearrange("p j n -> p n j"), 1.0, 0.0, MULT, ADD)
 
-        turned = [[bank(index) for index in indices] for indices in ((1, 2, 4, 0), (5, 6, 3, 7))]
+        turned = [[bank(index) for index in indices] for indices in ((2, 6, 7, 0), (1, 3, 4, 5))]
         pos_sb = (pos1_sb, pos2_sb)
 
-        def gather_and_turn(gather, m, r, blocks):
-            part = keep.tile([P, len(blocks) * P], F32, name=f"part{m}_{r}_{blocks.start}", align_bytes=64)
+        def gather_and_turn(gather, m, r, blocks, tag=""):
+            part = keep.tile([P, len(blocks) * P], F32, name=f"part{m}_{r}_{blocks.start}", tag=tag, align_bytes=64)
             gather(part[:], h_sb[m][:].indirect(entries(pos_sb[r], blocks.start * P, blocks.stop * P)))
             for k, q in enumerate(blocks):
                 nc.tensor.transpose(
@@ -196,9 +206,10 @@ def tile_moe_ser_none_kernel(
         gather_and_turn(vector_gather, 0, 1, every)
         gather_and_turn(scalar_gather, 1, 0, every)
         gather_and_turn(vector_gather, 1, 1, every)
-        gather_and_turn(scalar_gather, 2, 0, every)
+        gather_and_turn(scalar_gather, 2, 0, every, "w1_sb4_2")
         gather_and_turn(vector_gather, 2, 1, every)
-        gather_and_turn(scalar_gather, 3, 0, every)
+        gather_and_turn(scalar_gather, 3, 0, range(0, 2))
+        gather_and_turn(vector_gather, 3, 0, range(2, 4))
         gather_and_turn(vector_gather, 3, 1, range(0, 2))
         gather_and_turn(vector_gather, 3, 1, range(2, 4))
 
@@ -215,8 +226,7 @@ def tile_moe_ser_none_kernel(
             for e in range(first, last):
                 w2_codes[e] = codes[:, (e - first) * N : (e - first + 1) * N]
 
-        quantise_w2(0, 4, "w2_codes0")
-        c_rows = keep.tile([P, TOKEN_BLOCKS, 2, P, 2], BF16, name="c_rows", tag="w2_bf0", align_bytes=64)
+        c_rows = keep.tile([P, TOKEN_BLOCKS, 2, P, 2], BF16, name="c_rows", align_bytes=64)
         c_words = keep.tile([P, 2, T], F32, name="c_words", align_bytes=64)
 
         def turn_back(copy, q, halves, back):
@@ -247,14 +257,14 @@ def tile_moe_ser_none_kernel(
                     ADD,
                 )
         for q in range(TOKEN_BLOCKS - 1):
-            turn_back(nc.scalar.copy, q, range(0, 2), bank((1, 2, 4)[q]))
+            turn_back(nc.scalar.copy, q, range(0, 2), bank((2, 6, 7)[q]))
         turn_back(nc.scalar.copy, TOKEN_BLOCKS - 1, range(0, 1), bank(0))
-        turn_back(nc.vector.tensor_copy, TOKEN_BLOCKS - 1, range(1, 2), bank(5))
+        turn_back(nc.vector.tensor_copy, TOKEN_BLOCKS - 1, range(1, 2), bank(1))
 
-        quantise_w2(4, 6, "scaled3")
+        quantise_w2(0, 4, "scaled3")
 
-        c_planes = keep.tile([P, 2, 2, T], BF16, name="c_planes", align_bytes=64)
-        for u, index in enumerate((6, 3)):
+        c_planes = keep.tile([P, 2, 2, T], BF16, name="c_planes", tag="c_planes", align_bytes=64)
+        for u, index in enumerate((3, 4)):
             planes = psum.tile([P, 2, T], BF16, name=f"planes{u}", tag=f"bank{index}")
             for d in range(2):
                 for q in range(TOKEN_BLOCKS):
@@ -262,7 +272,6 @@ def tile_moe_ser_none_kernel(
             nc.scalar.copy(c_planes[:, u], planes[:])
 
         windows = [c_words[:, u, :].bitcast(U32) for u in range(2)]
-        y_sb = keep.tile([P, S], F32, name="y_sb")
 
         def quantise_and_multiply(rows, first, last, tag, acc):
             width = (last - first) * C
@@ -282,29 +291,27 @@ def tile_moe_ser_none_kernel(
                 )
             nc.scalar.copy(y_sb[:, first * C : last * C], acc[:, :width])
 
-        last_rows = keep.tile([P, C, PACK], BF16, name="last_rows", align_bytes=64)
+        last_rows = keep.tile([P, 2 * C, PACK], BF16, name="last_rows", align_bytes=64)
         for u in range(2):
             for d in range(2):
                 nc.scalar.activation(
-                    last_rows[:, :, 2 * u + d], c_planes[:, u, d, :].indirect(entries(offs2_sb, 7 * C, 8 * C)), COPY
+                    last_rows[:, :, 2 * u + d], c_planes[:, u, d, :].indirect(entries(offs2_sb, 6 * C, 8 * C)), COPY
                 )
+        y_sb = keep.tile([P, S], F32, name="y_sb", tag="c_planes", align_bytes=64)
         for g, (first, last) in enumerate(SECOND_GROUPS):
             width = (last - first) * C
             lst = entries(offs2_sb, first * C, last * C)
-            woven = keep.tile([P, width, 2], U32, name=f"woven{first}", align_bytes=64)
+            woven = keep.tile([P, width, 2], U32, name=f"woven{first}", tag=f"woven{first}", align_bytes=64)
             cg = keep.tile([P, 2, width], U32, name=f"cg{first}", tag=f"ring{g % 2}", align_bytes=64)
             for u in range(2):
                 nc.vector.tensor_copy(cg[:, u, :], windows[u].indirect(lst))
             nc.gpsimd.tensor_copy(woven[:], cg[:].rearrange("p u s -> p s u"))
+            if first == 4:
+                quantise_w2(4, 8, "woven0")
             quantise_and_multiply(
-                woven[:].rearrange("p s u -> p (s u)").bitcast(BF16), first, last, f"codes{first}", bank((1, 2, 4)[g])
+                woven[:].rearrange("p s u -> p (s u)").bitcast(BF16), first, last, f"codes{first}", bank((2, 6, 7)[g])
             )
-        woven = keep.tile([P, C, 2], U32, name="woven6", tag="ring1", align_bytes=64)
-        for u in range(2):
-            nc.vector.tensor_copy(woven[:, :, u], windows[u].indirect(entries(offs2_sb, 6 * C, 7 * C)))
-        quantise_w2(6, 8, "ring0")
-        quantise_and_multiply(last_rows[:].rearrange("p s j -> p (s j)"), 7, 8, "woven4", bank(0))
-        quantise_and_multiply(woven[:].rearrange("p s u -> p (s u)").bitcast(BF16), 6, 7, "codes6", bank(5))
+        quantise_and_multiply(last_rows[:].rearrange("p s j -> p (s j)"), 6, 8, "woven2", bank(0))
 
         halves = (slice(0, T // 2), slice(T // 2, T))
         first_part = keep.tile([P, T], F32, name="first_part")

@@ -137,9 +137,18 @@ def tile_moe_ser_none_kernel(
         make_identity(nc, ident_bf[:])
 
         gate1_cols = keep.tile([P, 2 * TOKEN_BLOCKS], F32, name="gate1_cols")
-        turned_gates = bank(7)
+        turned_gates = bank(2)
         nc.tensor.transpose(turned_gates[:, :P], gate1_rows[:], ident[:])
         nc.scalar.copy(gate1_cols[:], turned_gates[:, : 2 * TOKEN_BLOCKS])
+        gate1_sb = keep.tile([P, 2, T], F32, name="gate1_sb", align_bytes=64)
+        for r in range(2):
+            spread = bank(6 + r)
+            for q in range(TOKEN_BLOCKS):
+                column = r * TOKEN_BLOCKS + q
+                nc.tensor.transpose(
+                    spread[:, q * P : (q + 1) * P], gate1_cols[:, column : column + 1].to_broadcast([P, P]), ident[:]
+                )
+            nc.scalar.copy(gate1_sb[:, r, :], spread[:])
 
         h_sb = [keep.tile([P, S], F32, name=f"h_sb{m}", align_bytes=64) for m in range(ROW_TILES)]
         xg = keep.tile([P, PASSES, S], U32, name="xg", align_bytes=64)
@@ -179,37 +188,53 @@ def tile_moe_ser_none_kernel(
         multiply_by_pass(((0, 0, 0, 4, nc.scalar.copy), (1, 1, 0, 4, nc.scalar.copy)))
         multiply_by_pass(((3, 0, 4, 7, nc.vector.tensor_copy), (4, 0, 7, 8, nc.scalar.copy)))
         multiply_by_pass(((5, 1, 4, 8, nc.scalar.copy),))
-        for indices, first in (((2, 6, 7, 0), 0), ((1, 3, 4, 5), 4)):
-            for k, index in enumerate(indices):
-                lo = first + 2 * (k % 2)
-                multiply_by_pass(((index, 2 + k // 2, lo, lo + 2, nc.scalar.copy),))
+        for index, m, first in ((2, 2, 0), (6, 3, 0), (7, 2, 4), (0, 3, 4)):
+            multiply_by_pass(((index, m, first, first + 4, nc.scalar.copy),))
 
         w2_bf = [keep.tile([P, 4, N, PACK], BF16, name=f"w2_bf{i}", tag=f"w2_bf{i}", align_bytes=64) for i in range(2)]
         for e in range(E):
             nc.gpsimd.tensor_scalar(w2_bf[e // 4][:, e % 4], w2_raw[e].rearrange("p j n -> p n j"), 1.0, 0.0, MULT, ADD)
 
-        turned = [[bank(index) for index in indices] for indices in ((2, 6, 7, 0), (1, 3, 4, 5))]
         pos_sb = (pos1_sb, pos2_sb)
+        c_rows = keep.tile([P, TOKEN_BLOCKS, 2, P, 2], BF16, name="c_rows", align_bytes=64)
+
+        for m, index, copy in ((0, 2, nc.scalar.copy), (1, 7, nc.vector.tensor_copy)):
+            total = bank(index)
+            for r in range(2):
+                part = keep.tile([P, T], F32, name=f"part{m}_{r}", align_bytes=64)
+                nc.vector.tensor_tensor(part[:], h_sb[m][:].indirect(pos_sb[r][:]), gate1_sb[:, r, :], MULT)
+                for q in range(TOKEN_BLOCKS):
+                    nc.tensor.matmul(
+                        total[:, q * P : (q + 1) * P],
+                        part[:, q * P : (q + 1) * P],
+                        ident[:],
+                        is_transpose=True,
+                        start=(r == 0 and q == 0),
+                        stop=(r == 1 and q == TOKEN_BLOCKS - 1),
+                    )
+            copy(
+                c_rows[:, :, :, 32 * m : 32 * (m + 1), :],
+                total[:].rearrange("t (q p u d) -> t q u p d", q=TOKEN_BLOCKS, u=2, d=2),
+            )
+
+        turned = [[bank(index) for index in indices] for indices in ((1, 3), (4, 5))]
+
+        def turned_rows(r, q):
+            return turned[r][q // 2][:, (q % 2) * 2 * P : (q % 2 + 1) * 2 * P]
 
         def gather_and_turn(gather, m, r, blocks, tag=""):
             part = keep.tile([P, len(blocks) * P], F32, name=f"part{m}_{r}_{blocks.start}", tag=tag, align_bytes=64)
             gather(part[:], h_sb[m][:].indirect(entries(pos_sb[r], blocks.start * P, blocks.stop * P)))
             for k, q in enumerate(blocks):
                 nc.tensor.transpose(
-                    turned[r][q][:, m * P : (m + 1) * P],
-                    part[:, k * P : (k + 1) * P],
-                    ident[:],
+                    turned_rows(r, q)[:, (m - 2) * P : (m - 1) * P], part[:, k * P : (k + 1) * P], ident[:]
                 )
 
         every = range(TOKEN_BLOCKS)
-        gather_and_turn(vector_gather, 0, 0, every)
-        gather_and_turn(vector_gather, 0, 1, every)
-        gather_and_turn(scalar_gather, 1, 0, every)
-        gather_and_turn(vector_gather, 1, 1, every)
         gather_and_turn(scalar_gather, 2, 0, every, "w1_sb4_2")
         gather_and_turn(vector_gather, 2, 1, every)
         gather_and_turn(scalar_gather, 3, 0, range(0, 2))
-        gather_and_turn(vector_gather, 3, 0, range(2, 4))
+        gather_and_turn(scalar_gather, 3, 0, range(2, 4))
         gather_and_turn(vector_gather, 3, 1, range(0, 2))
         gather_and_turn(vector_gather, 3, 1, range(2, 4))
 
@@ -226,7 +251,6 @@ def tile_moe_ser_none_kernel(
             for e in range(first, last):
                 w2_codes[e] = codes[:, (e - first) * N : (e - first + 1) * N]
 
-        c_rows = keep.tile([P, TOKEN_BLOCKS, 2, P, 2], BF16, name="c_rows", align_bytes=64)
         c_words = keep.tile([P, 2, T], F32, name="c_words", align_bytes=64)
 
         def turn_back(copy, q, halves, back):
@@ -240,25 +264,25 @@ def tile_moe_ser_none_kernel(
             )
 
         def by_half(rows):
-            return rows[:].rearrange("t (p u d) -> t u p d", u=2, d=2)
+            return rows.rearrange("t (p u d) -> t u p d", u=2, d=2)
 
         scaled = []
         for q in range(TOKEN_BLOCKS):
-            scaled.append(keep.tile([P, 2, P, 2], F32, name=f"scaled{q}", tag=f"scaled{q}", align_bytes=64))
-            nc.scalar.activation(scaled[q][:], by_half(turned[0][q]), COPY, scale=gate1_cols[:, q : q + 1])
+            scaled.append(keep.tile([P, 2, P // 2, 2], F32, name=f"scaled{q}", tag=f"scaled{q}", align_bytes=64))
+            nc.scalar.activation(scaled[q][:], by_half(turned_rows(0, q)), COPY, scale=gate1_cols[:, q : q + 1])
         for q in range(TOKEN_BLOCKS):
             for u in range(2):
                 nc.vector.scalar_tensor_tensor(
-                    c_rows[:, q, u],
-                    by_half(turned[1][q])[:, u],
+                    c_rows[:, q, u, P // 2 :],
+                    by_half(turned_rows(1, q))[:, u],
                     gate1_cols[:, TOKEN_BLOCKS + q : TOKEN_BLOCKS + q + 1],
                     scaled[q][:, u],
                     MULT,
                     ADD,
                 )
         for q in range(TOKEN_BLOCKS - 1):
-            turn_back(nc.scalar.copy, q, range(0, 2), bank((2, 6, 7)[q]))
-        turn_back(nc.scalar.copy, TOKEN_BLOCKS - 1, range(0, 1), bank(0))
+            turn_back(nc.scalar.copy, q, range(0, 2), bank((6, 0, 2)[q]))
+        turn_back(nc.scalar.copy, TOKEN_BLOCKS - 1, range(0, 1), bank(7))
         turn_back(nc.vector.tensor_copy, TOKEN_BLOCKS - 1, range(1, 2), bank(1))
 
         quantise_w2(0, 4, "scaled3")
@@ -309,9 +333,9 @@ def tile_moe_ser_none_kernel(
             if first == 4:
                 quantise_w2(4, 8, "woven0")
             quantise_and_multiply(
-                woven[:].rearrange("p s u -> p (s u)").bitcast(BF16), first, last, f"codes{first}", bank((2, 6, 7)[g])
+                woven[:].rearrange("p s u -> p (s u)").bitcast(BF16), first, last, f"codes{first}", bank((6, 0, 2)[g])
             )
-        quantise_and_multiply(last_rows[:].rearrange("p s j -> p (s j)"), 6, 8, "woven2", bank(0))
+        quantise_and_multiply(last_rows[:].rearrange("p s j -> p (s j)"), 6, 8, "woven2", bank(7))
 
         halves = (slice(0, T // 2), slice(T // 2, T))
         first_part = keep.tile([P, T], F32, name="first_part")

@@ -27,7 +27,6 @@ TOKEN_BLOCKS = T // P
 SPARE = 192
 WINDOW = T + SPARE
 PLANE_WINDOW = 1408
-SECOND_GROUPS = ((0, 2), (2, 4), (4, 6))
 
 
 def entries(lst, first, last):
@@ -94,10 +93,11 @@ def tile_moe_ser_none_kernel(
             )
             for e in range(first, last):
                 w2_raw[e] = raw[:, e - first]
+            return raw
 
-        def load_w1_scales(half):
+        def load_w1_scales(half, residues):
             rows = w1_scales.rearrange("e s (q r) i -> r q (e s) i", r=4)
-            for r in range(4):
+            for r in residues:
                 nc.sync.dma_start(
                     w1_planes[half][r:P:32].bitcast(I32),
                     rows[r][:, :, half * H // 2 : (half + 1) * H // 2].bitcast(I32),
@@ -109,22 +109,22 @@ def tile_moe_ser_none_kernel(
                 x_plane[32 * q : 32 * q + 8, :T].bitcast(I32), x_scales[:, 4 * q : 4 * q + 4, :].bitcast(I32)
             )
         nc.sync.dma_start(x_sb[:, :, :T], x_words.rearrange("s p t d -> p s (t d)").bitcast(I32))
+        load_w1_scales(0, range(0, 1))
         nc.sync.dma_start(
             gate1_rows[: 2 * TOKEN_BLOCKS, :], gate1[:, 0, :].rearrange("r (q c) -> r q c", c=P)
         )
-        load_w1_scales(0)
-        load_w1(0, 4, range(0, 2))
+        load_w1(0, 8, range(0, 2))
+        load_w1_scales(0, range(1, 4))
         nc.vector.tensor_copy(sg[0][:], x_plane[:].indirect(offs_sb[:]))
         for r in range(4):
             nc.sync.dma_start(sg[1][r:P:32].bitcast(I32), sg[0][4 + r : P : 32].bitcast(I32))
-        load_w1(4, 8, range(0, 2))
         pos1_sb = load_list("pos1_sb", pos1)
         pos2_sb = load_list("pos2_sb", pos2)
-        load_w1_scales(1)
         load_w1(0, 4, range(2, 4))
+        load_w1_scales(1, range(4))
         load_w1(4, 8, range(2, 4))
         load_w2(0, 4)
-        load_w2(4, 8)
+        w2_second = load_w2(4, 8)
         offs2_sb = load_list("offs2_sb", offs2)
         gate2_sb = keep.tile([P, 2, T], F32, name="gate2_sb", align_bytes=64)
         nc.sync.dma_start(gate2_sb[:], gate2.rearrange("r p t -> p r t"))
@@ -150,7 +150,7 @@ def tile_moe_ser_none_kernel(
                 )
             nc.scalar.copy(gate1_sb[:, r, :], spread[:])
 
-        h_sb = [keep.tile([P, S], F32, name=f"h_sb{m}", align_bytes=64) for m in range(ROW_TILES)]
+        h_sb = [keep.tile([P, S], F32, name=f"h_sb{m}", tag=f"h{m}", align_bytes=64) for m in range(ROW_TILES)]
         xg = keep.tile([P, PASSES, S], U32, name="xg", align_bytes=64)
 
         def gather_words(s, lo, hi):
@@ -160,8 +160,8 @@ def tile_moe_ser_none_kernel(
             )
 
         gather_words(0, 0, 4)
-        gather_words(1, 0, 4)
         gather_words(0, 4, 8)
+        gather_words(1, 0, 4)
         gather_words(1, 4, 7)
         gather_words(1, 7, 8)
 
@@ -185,18 +185,14 @@ def tile_moe_ser_none_kernel(
                 multiply(acc, 1, m, first, last)
                 copy(h_sb[m][:, first * C : last * C], acc[:, : (last - first) * C])
 
-        multiply_by_pass(((0, 0, 0, 4, nc.scalar.copy), (1, 1, 0, 4, nc.scalar.copy)))
-        multiply_by_pass(((3, 0, 4, 7, nc.vector.tensor_copy), (4, 0, 7, 8, nc.scalar.copy)))
-        multiply_by_pass(((5, 1, 4, 8, nc.scalar.copy),))
-        for index, m, first in ((2, 2, 0), (6, 3, 0), (7, 2, 4), (0, 3, 4)):
+        multiply_by_pass(
+            ((0, 0, 0, 4, nc.scalar.copy), (3, 0, 4, 7, nc.vector.tensor_copy), (4, 0, 7, 8, nc.scalar.copy))
+        )
+        for index, m, first in ((0, 1, 0), (3, 1, 4), (2, 2, 0), (6, 3, 0), (7, 2, 4), (0, 3, 4)):
             multiply_by_pass(((index, m, first, first + 4, nc.scalar.copy),))
 
-        w2_bf = [keep.tile([P, 4, N, PACK], BF16, name=f"w2_bf{i}", tag=f"w2_bf{i}", align_bytes=64) for i in range(2)]
-        for e in range(E):
-            nc.gpsimd.tensor_scalar(w2_bf[e // 4][:, e % 4], w2_raw[e].rearrange("p j n -> p n j"), 1.0, 0.0, MULT, ADD)
-
         pos_sb = (pos1_sb, pos2_sb)
-        c_rows = keep.tile([P, TOKEN_BLOCKS, 2, P, 2], BF16, name="c_rows", align_bytes=64)
+        c_rows = keep.tile([P, TOKEN_BLOCKS, 2, P, 2], BF16, name="c_rows", tag="c_rows", align_bytes=64)
 
         for m, index, copy in ((0, 2, nc.scalar.copy), (1, 7, nc.vector.tensor_copy)):
             total = bank(index)
@@ -216,6 +212,10 @@ def tile_moe_ser_none_kernel(
                 c_rows[:, :, :, 32 * m : 32 * (m + 1), :],
                 total[:].rearrange("t (q p u d) -> t q u p d", q=TOKEN_BLOCKS, u=2, d=2),
             )
+
+        w2_bf = [keep.tile([P, 4, N, PACK], BF16, name="w2_bf0", tag="h1", align_bytes=64)]
+        for e in range(4):
+            nc.gpsimd.tensor_scalar(w2_bf[0][:, e], w2_raw[e].rearrange("p j n -> p n j"), 1.0, 0.0, MULT, ADD)
 
         turned = [[bank(index) for index in indices] for indices in ((1, 3), (4, 5))]
 
@@ -241,12 +241,11 @@ def tile_moe_ser_none_kernel(
         w2_codes = {}
         w2_plane = keep.tile([P, E * N], U8, name="w2_plane", align_bytes=64)
 
-        def quantise_w2(first, last, tag):
-            codes = keep.tile([P, (last - first) * N], U32, name=f"w2_codes{first}", tag=tag, align_bytes=64)
+        def quantise_w2(rows, first, last, codes):
             nc.vector.quantize_mx(
-                out=codes[:].bitcast(FP8X4),
+                out=codes.bitcast(FP8X4),
                 scales=w2_plane[:, first * N : last * N],
-                in_=w2_bf[first // 4][:, first % 4 : first % 4 + last - first].rearrange("p e n j -> p (e n j)"),
+                in_=rows.rearrange("p e n j -> p (e n j)"),
             )
             for e in range(first, last):
                 w2_codes[e] = codes[:, (e - first) * N : (e - first + 1) * N]
@@ -285,23 +284,25 @@ def tile_moe_ser_none_kernel(
         turn_back(nc.scalar.copy, TOKEN_BLOCKS - 1, range(0, 1), bank(7))
         turn_back(nc.vector.tensor_copy, TOKEN_BLOCKS - 1, range(1, 2), bank(1))
 
-        quantise_w2(0, 4, "scaled3")
+        early_codes = keep.tile([P, 2 * N], U32, name="early_codes", tag="scaled3", align_bytes=64)
+        quantise_w2(w2_bf[0][:, :2], 0, 2, early_codes[:])
 
         c_planes = keep.tile([P, 2, 2, T], BF16, name="c_planes", tag="c_planes", align_bytes=64)
         for u, index in enumerate((3, 4)):
-            planes = psum.tile([P, 2, T], BF16, name=f"planes{u}", tag=f"bank{index}")
+            singles = psum.tile([P, 2, T], BF16, name=f"singles{u}", tag=f"bank{index}")
             for d in range(2):
                 for q in range(TOKEN_BLOCKS):
-                    nc.tensor.transpose(planes[:, d, q * P : (q + 1) * P], c_rows[:, q, u, :, d], ident_bf[:])
-            nc.scalar.copy(c_planes[:, u], planes[:])
+                    nc.tensor.transpose(singles[:, d, q * P : (q + 1) * P], c_rows[:, q, u, :, d], ident_bf[:])
+            nc.scalar.copy(c_planes[:, u], singles[:])
 
         windows = [c_words[:, u, :].bitcast(U32) for u in range(2)]
 
-        def quantise_and_multiply(rows, first, last, tag, acc):
-            width = (last - first) * C
-            codes = keep.tile([P, width], U32, name=f"codes{first}", tag=tag, align_bytes=64)
-            plane = keep.tile([P, width], U8, name=f"plane{first}", align_bytes=64)
-            nc.vector.quantize_mx(out=codes[:].bitcast(FP8X4), scales=plane[:], in_=rows)
+        def quantise_rows(rows, first, codes):
+            plane = keep.tile([P, codes.shape[1]], U8, name=f"plane{first}", align_bytes=64)
+            nc.vector.quantize_mx(out=codes.bitcast(FP8X4), scales=plane[:], in_=rows)
+            return plane
+
+        def multiply_second(codes, plane, first, last, acc):
             for e in range(first, last):
                 cols = slice((e - first) * C, (e - first + 1) * C)
                 nc.tensor.matmul_mx(
@@ -313,29 +314,62 @@ def tile_moe_ser_none_kernel(
                     start=True,
                     stop=True,
                 )
-            nc.scalar.copy(y_sb[:, first * C : last * C], acc[:, :width])
+            nc.scalar.copy(y_sb[:, first * C : last * C], acc[:, : (last - first) * C])
 
-        last_rows = keep.tile([P, 2 * C, PACK], BF16, name="last_rows", align_bytes=64)
+        def round_w2(grouped, first):
+            nc.scalar.copy(
+                grouped.rearrange("p e (c i) j -> p e c j i", i=4),
+                w2_second[:, first - 4 : first - 2].rearrange("p e j (c i) -> p e c j i", i=4),
+            )
+
+        w2_bf.append(keep.tile([P, 4, N, PACK], BF16, name="w2_bf1", tag="c_rows", align_bytes=64))
+        last_rows = keep.tile([P, C, PACK], BF16, name="last_rows", align_bytes=64)
         for u in range(2):
             for d in range(2):
                 nc.scalar.activation(
-                    last_rows[:, :, 2 * u + d], c_planes[:, u, d, :].indirect(entries(offs2_sb, 6 * C, 8 * C)), COPY
+                    last_rows[:, :, 2 * u + d], c_planes[:, u, d, :].indirect(entries(offs2_sb, 7 * C, 8 * C)), COPY
                 )
+        round_w2(w2_bf[1][:, :2], 4)
+        round_w2(w2_bf[1][:, 2:], 6)
         y_sb = keep.tile([P, S], F32, name="y_sb", tag="c_planes", align_bytes=64)
-        for g, (first, last) in enumerate(SECOND_GROUPS):
+
+        woven, codes, planes = {}, {}, {}
+
+        def gather_pairs(g, first, last):
             width = (last - first) * C
             lst = entries(offs2_sb, first * C, last * C)
-            woven = keep.tile([P, width, 2], U32, name=f"woven{first}", tag=f"woven{first}", align_bytes=64)
+            woven[first] = keep.tile([P, width, 2], U32, name=f"woven{first}", align_bytes=64)
             cg = keep.tile([P, 2, width], U32, name=f"cg{first}", tag=f"ring{g % 2}", align_bytes=64)
             for u in range(2):
                 nc.vector.tensor_copy(cg[:, u, :], windows[u].indirect(lst))
-            nc.gpsimd.tensor_copy(woven[:], cg[:].rearrange("p u s -> p s u"))
-            if first == 4:
-                quantise_w2(4, 8, "woven0")
-            quantise_and_multiply(
-                woven[:].rearrange("p s u -> p (s u)").bitcast(BF16), first, last, f"codes{first}", bank((6, 0, 2)[g])
+            nc.gpsimd.tensor_copy(woven[first][:], cg[:].rearrange("p u s -> p s u"))
+
+        def quantise_woven(first, last):
+            codes[first] = keep.tile([P, (last - first) * C], U32, name=f"codes{first}", align_bytes=64)
+            planes[first] = quantise_rows(
+                woven[first][:].rearrange("p s u -> p (s u)").bitcast(BF16), first, codes[first][:]
             )
-        quantise_and_multiply(last_rows[:].rearrange("p s j -> p (s j)"), 6, 8, "woven2", bank(7))
+
+        gather_pairs(0, 0, 2)
+        quantise_woven(0, 2)
+        multiply_second(codes[0], planes[0], 0, 2, bank(6))
+        gather_pairs(1, 2, 4)
+        quantise_woven(2, 4)
+        gather_pairs(2, 4, 6)
+        woven[6] = keep.tile([P, C, 2], U32, name="woven6", tag="ring1", align_bytes=64)
+        for u in range(2):
+            nc.vector.tensor_copy(woven[6][:, :, u], windows[u].indirect(entries(offs2_sb, 6 * C, 7 * C)))
+        late_codes = keep.tile([P, 6 * N + C], U32, name="late_codes", tag="ring0", align_bytes=64)
+        quantise_w2(w2_bf[0][:, 2:], 2, 4, late_codes[:, : 2 * N])
+        multiply_second(codes[2], planes[2], 2, 4, bank(0))
+        last_plane = quantise_rows(last_rows[:].rearrange("p s j -> p (s j)"), 7, late_codes[:, 6 * N :])
+        quantise_w2(w2_bf[1][:, :2], 4, 6, late_codes[:, 2 * N : 4 * N])
+        quantise_woven(4, 6)
+        multiply_second(codes[4], planes[4], 4, 6, bank(2))
+        quantise_w2(w2_bf[1][:, 2:], 6, 8, late_codes[:, 4 * N : 6 * N])
+        multiply_second(late_codes[:, 6 * N :], last_plane, 7, 8, bank(7))
+        quantise_woven(6, 7)
+        multiply_second(codes[6], planes[6], 6, 7, bank(1))
 
         halves = (slice(0, T // 2), slice(T // 2, T))
         first_part = keep.tile([P, T], F32, name="first_part")

@@ -131,7 +131,7 @@ def tile_moe_ser_none_kernel(
         pos3_sb = load_list("pos3_sb", pos3)
         pos4_sb = load_list("pos4_sb", pos4)
 
-        ident = keep.tile([P, P], F32, name="ident")
+        ident = keep.tile([P, P], F32, name="ident", tag="ident", align_bytes=64)
         make_identity(nc, ident[:])
         ident_bf = keep.tile([P, P], BF16, name="ident_bf")
         make_identity(nc, ident_bf[:])
@@ -287,6 +287,14 @@ def tile_moe_ser_none_kernel(
         early_codes = keep.tile([P, 2 * N], U32, name="early_codes", tag="scaled3", align_bytes=64)
         quantise_w2(w2_bf[0][:, :2], 0, 2, early_codes[:])
 
+        def round_w2(grouped, first):
+            nc.scalar.copy(
+                grouped.rearrange("p e (c i) j -> p e c j i", i=4),
+                w2_second[:, first - 4 : first - 2].rearrange("p e j (c i) -> p e c j i", i=4),
+            )
+
+        rounded4 = keep.tile([P, 2, N, PACK], BF16, name="rounded4", tag="ident", align_bytes=64)
+        round_w2(rounded4[:], 4)
         c_planes = keep.tile([P, 2, 2, T], BF16, name="c_planes", tag="c_planes", align_bytes=64)
         for u, index in enumerate((3, 4)):
             singles = psum.tile([P, 2, T], BF16, name=f"singles{u}", tag=f"bank{index}")
@@ -316,21 +324,14 @@ def tile_moe_ser_none_kernel(
                 )
             nc.scalar.copy(y_sb[:, first * C : last * C], acc[:, : (last - first) * C])
 
-        def round_w2(grouped, first):
-            nc.scalar.copy(
-                grouped.rearrange("p e (c i) j -> p e c j i", i=4),
-                w2_second[:, first - 4 : first - 2].rearrange("p e j (c i) -> p e c j i", i=4),
-            )
-
-        w2_bf.append(keep.tile([P, 4, N, PACK], BF16, name="w2_bf1", tag="c_rows", align_bytes=64))
         last_rows = keep.tile([P, C, PACK], BF16, name="last_rows", align_bytes=64)
         for u in range(2):
             for d in range(2):
                 nc.scalar.activation(
                     last_rows[:, :, 2 * u + d], c_planes[:, u, d, :].indirect(entries(offs2_sb, 7 * C, 8 * C)), COPY
                 )
-        round_w2(w2_bf[1][:, :2], 4)
-        round_w2(w2_bf[1][:, 2:], 6)
+        rounded6 = keep.tile([P, 2, N, PACK], BF16, name="rounded6", tag="c_rows", align_bytes=64)
+        round_w2(rounded6[:], 6)
         y_sb = keep.tile([P, S], F32, name="y_sb", tag="c_planes", align_bytes=64)
 
         woven, codes, planes = {}, {}, {}
@@ -363,10 +364,10 @@ def tile_moe_ser_none_kernel(
         quantise_w2(w2_bf[0][:, 2:], 2, 4, late_codes[:, : 2 * N])
         multiply_second(codes[2], planes[2], 2, 4, bank(0))
         last_plane = quantise_rows(last_rows[:].rearrange("p s j -> p (s j)"), 7, late_codes[:, 6 * N :])
-        quantise_w2(w2_bf[1][:, :2], 4, 6, late_codes[:, 2 * N : 4 * N])
+        quantise_w2(rounded4[:], 4, 6, late_codes[:, 2 * N : 4 * N])
         quantise_woven(4, 6)
         multiply_second(codes[4], planes[4], 4, 6, bank(2))
-        quantise_w2(w2_bf[1][:, 2:], 6, 8, late_codes[:, 4 * N : 6 * N])
+        quantise_w2(rounded6[:], 6, 8, late_codes[:, 4 * N : 6 * N])
         multiply_second(late_codes[:, 6 * N :], last_plane, 7, 8, bank(7))
         quantise_woven(6, 7)
         multiply_second(codes[6], planes[6], 6, 7, bank(1))

@@ -194,8 +194,8 @@ def tile_moe_ser_none_kernel(
         pos_sb = (pos1_sb, pos2_sb)
         c_rows = keep.tile([P, TOKEN_BLOCKS, 2, P, 2], BF16, name="c_rows", tag="c_rows", align_bytes=64)
 
-        for m, index, copy in ((0, 2, nc.scalar.copy), (1, 7, nc.vector.tensor_copy)):
-            total = bank(index)
+        totals = [bank(2), bank(7)]
+        for m, total in enumerate(totals):
             for r in range(2):
                 part = keep.tile([P, T], F32, name=f"part{m}_{r}", align_bytes=64)
                 nc.vector.tensor_tensor(part[:], h_sb[m][:].indirect(pos_sb[r][:]), gate1_sb[:, r, :], MULT)
@@ -208,10 +208,6 @@ def tile_moe_ser_none_kernel(
                         start=(r == 0 and q == 0),
                         stop=(r == 1 and q == TOKEN_BLOCKS - 1),
                     )
-            copy(
-                c_rows[:, :, :, 32 * m : 32 * (m + 1), :],
-                total[:].rearrange("t (q p u d) -> t q u p d", q=TOKEN_BLOCKS, u=2, d=2),
-            )
 
         w2_bf = [keep.tile([P, 4, N, PACK], BF16, name="w2_bf0", tag="h1", align_bytes=64)]
         for e in range(4):
@@ -231,12 +227,18 @@ def tile_moe_ser_none_kernel(
                 )
 
         every = range(TOKEN_BLOCKS)
-        gather_and_turn(scalar_gather, 2, 0, every, "w1_sb4_2")
+        gather_and_turn(scalar_gather, 2, 0, every)
         gather_and_turn(vector_gather, 2, 1, every)
         gather_and_turn(scalar_gather, 3, 0, range(0, 2))
         gather_and_turn(scalar_gather, 3, 0, range(2, 4))
         gather_and_turn(vector_gather, 3, 1, range(0, 2))
         gather_and_turn(vector_gather, 3, 1, range(2, 4))
+
+        for m, copy in enumerate((nc.scalar.copy, nc.vector.tensor_copy)):
+            copy(
+                c_rows[:, :, :, 32 * m : 32 * (m + 1), :],
+                totals[m][:].rearrange("t (q p u d) -> t q u p d", q=TOKEN_BLOCKS, u=2, d=2),
+            )
 
         w2_codes = {}
         w2_plane = keep.tile([P, E * N], U8, name="w2_plane", align_bytes=64)

@@ -113,8 +113,8 @@ def tile_moe_ser_none_kernel(
         nc.sync.dma_start(
             gate1_rows[: 2 * TOKEN_BLOCKS, :], gate1[:, 0, :].rearrange("r (q c) -> r q c", c=P)
         )
-        load_w1(0, 8, range(0, 2))
         load_w1_scales(0, range(1, 4))
+        load_w1(0, 8, range(0, 2))
         nc.vector.tensor_copy(sg[0][:], x_plane[:].indirect(offs_sb[:]))
         for r in range(4):
             nc.sync.dma_start(sg[1][r:P:32].bitcast(I32), sg[0][4 + r : P : 32].bitcast(I32))

@@ -57,17 +57,18 @@ def tile_moe_ser_none_kernel(
 
         x_plane = keep.tile([P, PLANE_WINDOW], U8, name="x_plane", align_bytes=64)
         nc.gpsimd.memset(x_plane[:, :T].bitcast(I32), 0)
+        nc.gpsimd.memset(x_plane[:, T:].bitcast(I32), 0)
         gate1_rows = keep.tile([P, P], F32, name="gate1_rows")
         nc.gpsimd.memset(gate1_rows[:], 0.0)
         sg = [keep.tile([P, S], U8, name=f"sg{s}", align_bytes=64) for s in range(PASSES)]
         nc.gpsimd.memset(sg[1][:].bitcast(I32), 0)
         w1_planes = [keep.tile([P, E * PASSES, H // 2], U8, name=f"w1_plane{i}", align_bytes=64) for i in range(2)]
-        for plane in w1_planes:
-            nc.vector.memset(plane[:].rearrange("p g i -> p (g i)").bitcast(I32), 0)
-
-        nc.vector.memset(x_plane[:, T:].bitcast(I32), 0)
-        x_sb = keep.tile([P, PASSES, WINDOW], I32, name="x_sb", align_bytes=64)
-        nc.vector.memset(x_sb[:, :, T:], 0)
+        nc.vector.memset(w1_planes[0][:].rearrange("p g i -> p (g i)").bitcast(I32), 0)
+        zeros = keep.tile([P, 1, H // 8], I32, name="zeros", align_bytes=64)
+        nc.vector.memset(zeros[:], 0)
+        nc.scalar.copy(w1_planes[1][:].bitcast(U32), zeros[:].bitcast(U32).to_broadcast([P, E * PASSES, H // 8]))
+        x_sb = keep.tile([P, PASSES * T + SPARE], I32, name="x_sb", align_bytes=64)
+        nc.vector.memset(x_sb[:, PASSES * T :], 0)
 
         w1_sb = {}
 
@@ -108,7 +109,7 @@ def tile_moe_ser_none_kernel(
             nc.sync.dma_start(
                 x_plane[32 * q : 32 * q + 8, :T].bitcast(I32), x_scales[:, 4 * q : 4 * q + 4, :].bitcast(I32)
             )
-        nc.sync.dma_start(x_sb[:, :, :T], x_words.rearrange("s p t d -> p s (t d)").bitcast(I32))
+        nc.sync.dma_start(x_sb[:, : PASSES * T].rearrange("p (s t) -> p s t", t=T), x_words.rearrange("s p t d -> p s (t d)").bitcast(I32))
         load_w1_scales(0, range(0, 1))
         nc.sync.dma_start(
             gate1_rows[: 2 * TOKEN_BLOCKS, :], gate1[:, 0, :].rearrange("r (q c) -> r q c", c=P)
@@ -134,7 +135,7 @@ def tile_moe_ser_none_kernel(
         ident = keep.tile([P, P], F32, name="ident", tag="ident", align_bytes=64)
         make_identity(nc, ident[:])
         ident_bf = keep.tile([P, P], BF16, name="ident_bf")
-        make_identity(nc, ident_bf[:])
+        nc.scalar.copy(ident_bf[:], ident[:])
 
         gate1_cols = keep.tile([P, 2 * TOKEN_BLOCKS], F32, name="gate1_cols")
         turned_gates = bank(2)
@@ -156,7 +157,7 @@ def tile_moe_ser_none_kernel(
         def gather_words(s, lo, hi):
             nc.vector.tensor_copy(
                 xg[:, s, lo * C : hi * C],
-                x_sb[:, s, :].bitcast(U32).indirect(entries(offs_sb, lo * C, hi * C)),
+                x_sb[:, s * T : s * T + WINDOW].bitcast(U32).indirect(entries(offs_sb, lo * C, hi * C)),
             )
 
         gather_words(0, 0, 4)

@@ -115,13 +115,14 @@ def tile_moe_ser_none_kernel(
             gate1_rows[: 2 * TOKEN_BLOCKS, :], gate1[:, 0, :].rearrange("r (q c) -> r q c", c=P)
         )
         load_w1_scales(0, range(1, 4))
-        load_w1(0, 8, range(0, 2))
+        load_w1(0, 4, range(0, 2))
+        load_w1(4, 8, range(0, 2))
         nc.vector.tensor_copy(sg[0][:], x_plane[:].indirect(offs_sb[:]))
         for r in range(4):
             nc.sync.dma_start(sg[1][r:P:32].bitcast(I32), sg[0][4 + r : P : 32].bitcast(I32))
         pos1_sb = load_list("pos1_sb", pos1)
-        pos2_sb = load_list("pos2_sb", pos2)
         load_w1(0, 4, range(2, 4))
+        pos2_sb = load_list("pos2_sb", pos2)
         load_w1_scales(1, range(4))
         load_w1(4, 8, range(2, 4))
         load_w2(0, 4)
@@ -163,7 +164,8 @@ def tile_moe_ser_none_kernel(
         gather_words(0, 0, 4)
         gather_words(0, 4, 8)
         gather_words(1, 0, 4)
-        gather_words(1, 4, 7)
+        gather_words(1, 4, 6)
+        gather_words(1, 6, 7)
         gather_words(1, 7, 8)
 
         def multiply(acc, s, m, first, last):
@@ -178,18 +180,26 @@ def tile_moe_ser_none_kernel(
                     stop=(s == PASSES - 1 and e == last - 1),
                 )
 
-        def multiply_by_pass(groups):
+        def multiply_by_pass(groups, second=(0,)):
             accs = [bank(index) for index, m, first, last, copy in groups]
             for acc, (index, m, first, last, copy) in zip(accs, groups):
                 multiply(acc, 0, m, first, last)
-            for acc, (index, m, first, last, copy) in zip(accs, groups):
+            for k in second:
+                acc, (index, m, first, last, copy) = accs[k], groups[k]
                 multiply(acc, 1, m, first, last)
                 copy(h_sb[m][:, first * C : last * C], acc[:, : (last - first) * C])
 
         multiply_by_pass(
-            ((0, 0, 0, 4, nc.scalar.copy), (3, 0, 4, 7, nc.vector.tensor_copy), (4, 0, 7, 8, nc.scalar.copy))
+            (
+                (0, 0, 0, 4, nc.scalar.copy),
+                (5, 1, 0, 4, nc.scalar.copy),
+                (3, 0, 4, 6, nc.scalar.copy),
+                (1, 0, 6, 7, nc.scalar.copy),
+                (4, 0, 7, 8, nc.vector.tensor_copy),
+            ),
+            second=(0, 2, 3, 4, 1),
         )
-        for index, m, first in ((0, 1, 0), (3, 1, 4), (2, 2, 0), (6, 3, 0), (7, 2, 4), (0, 3, 4)):
+        for index, m, first in ((3, 1, 4), (2, 2, 0), (6, 3, 0), (7, 2, 4), (0, 3, 4)):
             multiply_by_pass(((index, m, first, first + 4, nc.scalar.copy),))
 
         pos_sb = (pos1_sb, pos2_sb)
@@ -235,7 +245,7 @@ def tile_moe_ser_none_kernel(
         gather_and_turn(vector_gather, 3, 1, range(0, 2))
         gather_and_turn(vector_gather, 3, 1, range(2, 4))
 
-        for m, copy in enumerate((nc.scalar.copy, nc.vector.tensor_copy)):
+        for m, copy in enumerate((nc.scalar.copy, nc.scalar.copy)):
             copy(
                 c_rows[:, :, :, 32 * m : 32 * (m + 1), :],
                 totals[m][:].rearrange("t (q p u d) -> t q u p d", q=TOKEN_BLOCKS, u=2, d=2),
@@ -313,7 +323,7 @@ def tile_moe_ser_none_kernel(
             nc.vector.quantize_mx(out=codes.bitcast(FP8X4), scales=plane[:], in_=rows)
             return plane
 
-        def multiply_second(codes, plane, first, last, acc):
+        def multiply_second(codes, plane, first, last, acc, copy=nc.scalar.copy):
             for e in range(first, last):
                 cols = slice((e - first) * C, (e - first + 1) * C)
                 nc.tensor.matmul_mx(
@@ -325,7 +335,7 @@ def tile_moe_ser_none_kernel(
                     start=True,
                     stop=True,
                 )
-            nc.scalar.copy(y_sb[:, first * C : last * C], acc[:, : (last - first) * C])
+            copy(y_sb[:, first * C : last * C], acc[:, : (last - first) * C])
 
         last_rows = keep.tile([P, C, PACK], BF16, name="last_rows", align_bytes=64)
         for u in range(2):
@@ -335,7 +345,7 @@ def tile_moe_ser_none_kernel(
                 )
         rounded6 = keep.tile([P, 2, N, PACK], BF16, name="rounded6", tag="c_rows", align_bytes=64)
         round_w2(rounded6[:], 6)
-        y_sb = keep.tile([P, S], F32, name="y_sb", tag="c_planes", align_bytes=64)
+        y_sb = keep.tile([P, S], F32, name="y_sb", align_bytes=64)
 
         woven, codes, planes = {}, {}, {}
 
@@ -356,7 +366,7 @@ def tile_moe_ser_none_kernel(
 
         gather_pairs(0, 0, 2)
         quantise_woven(0, 2)
-        multiply_second(codes[0], planes[0], 0, 2, bank(6))
+        multiply_second(codes[0], planes[0], 0, 2, bank(6), nc.vector.tensor_copy)
         gather_pairs(1, 2, 4)
         quantise_woven(2, 4)
         gather_pairs(2, 4, 6)

@@ -106,7 +106,7 @@ def tile_moe_ser_none_kernel(
 
         offs_sb = load_list("offs_sb", offs)
         for q in range(4):
-            nc.sync.dma_start(
+            (nc.sync if q < 2 else nc.scalar).dma_start(
                 x_plane[32 * q : 32 * q + 8, :T].bitcast(I32), x_scales[:, 4 * q : 4 * q + 4, :].bitcast(I32)
             )
         nc.sync.dma_start(x_sb[:, : PASSES * T].rearrange("p (s t) -> p s t", t=T), x_words.rearrange("s p t d -> p s (t d)").bitcast(I32))

@@ -55,26 +55,26 @@ def tile_moe_ser_none_kernel(
         def scalar_gather(dst, window):
             nc.scalar.activation(dst, window, COPY)
 
-        x_plane = keep.tile([P, PLANE_WINDOW], U8, name="x_plane", align_bytes=64)
+        x_plane = keep.tile([P, PLANE_WINDOW], U8, name="x_plane", align_bytes=256)
         nc.gpsimd.memset(x_plane[:, :T].bitcast(I32), 0)
         nc.gpsimd.memset(x_plane[:, T:].bitcast(I32), 0)
         gate1_rows = keep.tile([P, P], F32, name="gate1_rows")
         nc.gpsimd.memset(gate1_rows[:], 0.0)
-        sg = [keep.tile([P, S], U8, name=f"sg{s}", align_bytes=64) for s in range(PASSES)]
+        sg = [keep.tile([P, S], U8, name=f"sg{s}", align_bytes=256) for s in range(PASSES)]
         nc.gpsimd.memset(sg[1][:].bitcast(I32), 0)
-        w1_planes = [keep.tile([P, E * PASSES, H // 2], U8, name=f"w1_plane{i}", align_bytes=64) for i in range(2)]
+        w1_planes = [keep.tile([P, E * PASSES, H // 2], U8, name=f"w1_plane{i}", align_bytes=256) for i in range(2)]
         nc.vector.memset(w1_planes[0][:].rearrange("p g i -> p (g i)").bitcast(I32), 0)
         zeros = keep.tile([P, 1, H // 8], I32, name="zeros", align_bytes=64)
         nc.vector.memset(zeros[:], 0)
         nc.scalar.copy(w1_planes[1][:].bitcast(U32), zeros[:].bitcast(U32).to_broadcast([P, E * PASSES, H // 8]))
-        x_sb = keep.tile([P, PASSES * T + SPARE], I32, name="x_sb", align_bytes=64)
+        x_sb = keep.tile([P, PASSES * T + SPARE], I32, name="x_sb", align_bytes=256)
         nc.vector.memset(x_sb[:, PASSES * T :], 0)
 
         w1_sb = {}
 
         def load_w1(first, last, tiles):
             width = 2 * P * len(tiles)
-            words = keep.tile([P, last - first, PASSES, width], U8, name=f"w1_sb{first}_{tiles.start}", tag=f"w1_sb{first}_{tiles.start}", align_bytes=64)
+            words = keep.tile([P, last - first, PASSES, width], U8, name=f"w1_sb{first}_{tiles.start}", tag=f"w1_sb{first}_{tiles.start}", align_bytes=256)
             rows = w1_words[first:last].rearrange("e s p b -> p (e s) b")
             nc.sync.dma_start(
                 words[:].rearrange("p e s b -> p (e s) b").bitcast(I32),
@@ -87,7 +87,7 @@ def tile_moe_ser_none_kernel(
         w2_raw = {}
 
         def load_w2(first, last):
-            raw = keep.tile([P, last - first, PACK, N], F32, name=f"w2_raw{first}", align_bytes=64)
+            raw = keep.tile([P, last - first, PACK, N], F32, name=f"w2_raw{first}", align_bytes=256)
             nc.sync.dma_start(
                 raw[:].rearrange("p e j n -> p e (j n)"),
                 w2[first:last].rearrange("e (p j) n -> p e (j n)", j=PACK),
@@ -124,11 +124,12 @@ def tile_moe_ser_none_kernel(
         load_w1(0, 4, range(2, 4))
         pos2_sb = load_list("pos2_sb", pos2)
         load_w1_scales(1, range(4))
-        load_w1(4, 8, range(2, 4))
+        load_w1(4, 6, range(2, 4))
+        load_w1(6, 8, range(2, 4))
         load_w2(0, 4)
         w2_second = load_w2(4, 8)
         offs2_sb = load_list("offs2_sb", offs2)
-        gate2_sb = keep.tile([P, 2, T], F32, name="gate2_sb", align_bytes=64)
+        gate2_sb = keep.tile([P, 2, T], F32, name="gate2_sb", align_bytes=256)
         nc.sync.dma_start(gate2_sb[:], gate2.rearrange("r p t -> p r t"))
         pos3_sb = load_list("pos3_sb", pos3)
         pos4_sb = load_list("pos4_sb", pos4)
@@ -199,13 +200,15 @@ def tile_moe_ser_none_kernel(
             ),
             second=(0, 2, 3, 4, 1),
         )
-        for index, m, first in ((3, 1, 4), (2, 2, 0), (6, 3, 0), (7, 2, 4), (0, 3, 4)):
+        for index, m, first in ((3, 1, 4), (2, 2, 0), (6, 3, 0)):
             multiply_by_pass(((index, m, first, first + 4, nc.scalar.copy),))
+        for index, m, first in ((7, 2, 4), (0, 3, 4), (1, 2, 6), (4, 3, 6)):
+            multiply_by_pass(((index, m, first, first + 2, nc.scalar.copy),))
 
         pos_sb = (pos1_sb, pos2_sb)
         c_rows = keep.tile([P, TOKEN_BLOCKS, 2, P, 2], BF16, name="c_rows", tag="c_rows", align_bytes=64)
 
-        totals = [bank(2), bank(7)]
+        totals = [bank(2), bank(4)]
         for m, total in enumerate(totals):
             for r in range(2):
                 part = keep.tile([P, T], F32, name=f"part{m}_{r}", align_bytes=64)
@@ -224,7 +227,7 @@ def tile_moe_ser_none_kernel(
         for e in range(4):
             nc.gpsimd.tensor_scalar(w2_bf[0][:, e], w2_raw[e].rearrange("p j n -> p n j"), 1.0, 0.0, MULT, ADD)
 
-        turned = [[bank(index) for index in indices] for indices in ((1, 3), (4, 5))]
+        turned = [[bank(index) for index in indices] for indices in ((1, 3), (7, 5))]
 
         def turned_rows(r, q):
             return turned[r][q // 2][:, (q % 2) * 2 * P : (q % 2 + 1) * 2 * P]

@@ -105,11 +105,12 @@ def tile_moe_ser_none_kernel(
                 )
 
         offs_sb = load_list("offs_sb", offs)
+        nc.sync.dma_start(x_sb[:, :T], x_words[0].rearrange("p t d -> p (t d)").bitcast(I32))
         for q in range(4):
             (nc.sync if q < 2 else nc.scalar).dma_start(
                 x_plane[32 * q : 32 * q + 8, :T].bitcast(I32), x_scales[:, 4 * q : 4 * q + 4, :].bitcast(I32)
             )
-        nc.sync.dma_start(x_sb[:, : PASSES * T].rearrange("p (s t) -> p s t", t=T), x_words.rearrange("s p t d -> p s (t d)").bitcast(I32))
+        nc.sync.dma_start(x_sb[:, T : PASSES * T], x_words[1].rearrange("p t d -> p (t d)").bitcast(I32))
         load_w1_scales(0, range(0, 1))
         nc.sync.dma_start(
             gate1_rows[: 2 * TOKEN_BLOCKS, :], gate1[:, 0, :].rearrange("r (q c) -> r q c", c=P)
@@ -117,6 +118,7 @@ def tile_moe_ser_none_kernel(
         load_w1_scales(0, range(1, 4))
         load_w1(0, 4, range(0, 2))
         load_w1(4, 8, range(0, 2))
+        w2_first = load_w2(0, 2)
         nc.vector.tensor_copy(sg[0][:], x_plane[:].indirect(offs_sb[:]))
         for r in range(4):
             nc.sync.dma_start(sg[1][r:P:32].bitcast(I32), sg[0][4 + r : P : 32].bitcast(I32))
@@ -126,8 +128,8 @@ def tile_moe_ser_none_kernel(
         load_w1_scales(1, range(4))
         load_w1(4, 6, range(2, 4))
         load_w1(6, 8, range(2, 4))
-        load_w2(0, 4)
-        w2_second = load_w2(4, 8)
+        load_w2(2, 6)
+        w2_last = load_w2(6, 8)
         offs2_sb = load_list("offs2_sb", offs2)
         gate2_sb = keep.tile([P, 2, T], F32, name="gate2_sb", align_bytes=256)
         nc.sync.dma_start(gate2_sb[:], gate2.rearrange("r p t -> p r t"))
@@ -168,6 +170,29 @@ def tile_moe_ser_none_kernel(
         gather_words(1, 4, 6)
         gather_words(1, 6, 7)
         gather_words(1, 7, 8)
+
+        w2_codes = {}
+        w2_plane = keep.tile([P, E * N], U8, name="w2_plane", align_bytes=64)
+
+        def quantise_w2(rows, first, last, codes):
+            nc.vector.quantize_mx(
+                out=codes.bitcast(FP8X4),
+                scales=w2_plane[:, first * N : last * N],
+                in_=rows.rearrange("p e n j -> p (e n j)"),
+            )
+            for e in range(first, last):
+                w2_codes[e] = codes[:, (e - first) * N : (e - first + 1) * N]
+
+        def round_w2(grouped, raw):
+            nc.scalar.copy(
+                grouped.rearrange("p e (c i) j -> p e c j i", i=4),
+                raw.rearrange("p e j (c i) -> p e c j i", i=4),
+            )
+
+        rounded0 = keep.tile([P, 2, N, PACK], BF16, name="rounded0", tag="rounded0", align_bytes=64)
+        round_w2(rounded0[:], w2_first[:])
+        first_codes = keep.tile([P, 2 * N], U32, name="first_codes", align_bytes=64)
+        quantise_w2(rounded0[:], 0, 2, first_codes[:])
 
         def multiply(acc, s, m, first, last):
             for e in range(first, last):
@@ -211,7 +236,7 @@ def tile_moe_ser_none_kernel(
         totals = [bank(2), bank(4)]
         for m, total in enumerate(totals):
             for r in range(2):
-                part = keep.tile([P, T], F32, name=f"part{m}_{r}", align_bytes=64)
+                part = keep.tile([P, T], F32, name=f"part{m}_{r}", tag="rounded0" if (m, r) == (0, 0) else "", align_bytes=64)
                 nc.vector.tensor_tensor(part[:], h_sb[m][:].indirect(pos_sb[r][:]), gate1_sb[:, r, :], MULT)
                 for q in range(TOKEN_BLOCKS):
                     nc.tensor.matmul(
@@ -225,7 +250,7 @@ def tile_moe_ser_none_kernel(
 
         w2_bf = [keep.tile([P, 4, N, PACK], BF16, name="w2_bf0", tag="h1", align_bytes=64)]
         for e in range(4):
-            nc.gpsimd.tensor_scalar(w2_bf[0][:, e], w2_raw[e].rearrange("p j n -> p n j"), 1.0, 0.0, MULT, ADD)
+            nc.gpsimd.tensor_scalar(w2_bf[0][:, e], w2_raw[2 + e].rearrange("p j n -> p n j"), 1.0, 0.0, MULT, ADD)
 
         turned = [[bank(index) for index in indices] for indices in ((1, 3), (7, 5))]
 
@@ -253,18 +278,6 @@ def tile_moe_ser_none_kernel(
                 c_rows[:, :, :, 32 * m : 32 * (m + 1), :],
                 totals[m][:].rearrange("t (q p u d) -> t q u p d", q=TOKEN_BLOCKS, u=2, d=2),
             )
-
-        w2_codes = {}
-        w2_plane = keep.tile([P, E * N], U8, name="w2_plane", align_bytes=64)
-
-        def quantise_w2(rows, first, last, codes):
-            nc.vector.quantize_mx(
-                out=codes.bitcast(FP8X4),
-                scales=w2_plane[:, first * N : last * N],
-                in_=rows.rearrange("p e n j -> p (e n j)"),
-            )
-            for e in range(first, last):
-                w2_codes[e] = codes[:, (e - first) * N : (e - first + 1) * N]
 
         c_words = keep.tile([P, 2, T], F32, name="c_words", align_bytes=64)
 
@@ -301,16 +314,10 @@ def tile_moe_ser_none_kernel(
         turn_back(nc.vector.tensor_copy, TOKEN_BLOCKS - 1, range(1, 2), bank(1))
 
         early_codes = keep.tile([P, 2 * N], U32, name="early_codes", tag="scaled3", align_bytes=64)
-        quantise_w2(w2_bf[0][:, :2], 0, 2, early_codes[:])
+        quantise_w2(w2_bf[0][:, :2], 2, 4, early_codes[:])
 
-        def round_w2(grouped, first):
-            nc.scalar.copy(
-                grouped.rearrange("p e (c i) j -> p e c j i", i=4),
-                w2_second[:, first - 4 : first - 2].rearrange("p e j (c i) -> p e c j i", i=4),
-            )
-
-        rounded4 = keep.tile([P, 2, N, PACK], BF16, name="rounded4", tag="ident", align_bytes=64)
-        round_w2(rounded4[:], 4)
+        rounded6 = keep.tile([P, 2, N, PACK], BF16, name="rounded6", tag="ident", align_bytes=64)
+        round_w2(rounded6[:], w2_last[:])
         c_planes = keep.tile([P, 2, 2, T], BF16, name="c_planes", tag="c_planes", align_bytes=64)
         for u, index in enumerate((3, 4)):
             singles = psum.tile([P, 2, T], BF16, name=f"singles{u}", tag=f"bank{index}")
@@ -346,8 +353,6 @@ def tile_moe_ser_none_kernel(
                 nc.scalar.activation(
                     last_rows[:, :, 2 * u + d], c_planes[:, u, d, :].indirect(entries(offs2_sb, 7 * C, 8 * C)), COPY
                 )
-        rounded6 = keep.tile([P, 2, N, PACK], BF16, name="rounded6", tag="c_rows", align_bytes=64)
-        round_w2(rounded6[:], 6)
         y_sb = keep.tile([P, S], F32, name="y_sb", align_bytes=64)
 
         woven, codes, planes = {}, {}, {}
@@ -369,22 +374,21 @@ def tile_moe_ser_none_kernel(
 
         gather_pairs(0, 0, 2)
         quantise_woven(0, 2)
-        multiply_second(codes[0], planes[0], 0, 2, bank(6), nc.vector.tensor_copy)
+        multiply_second(codes[0], planes[0], 0, 2, bank(6))
         gather_pairs(1, 2, 4)
         quantise_woven(2, 4)
         gather_pairs(2, 4, 6)
         woven[6] = keep.tile([P, C, 2], U32, name="woven6", tag="ring1", align_bytes=64)
         for u in range(2):
             nc.vector.tensor_copy(woven[6][:, :, u], windows[u].indirect(entries(offs2_sb, 6 * C, 7 * C)))
-        late_codes = keep.tile([P, 6 * N + C], U32, name="late_codes", tag="ring0", align_bytes=64)
-        quantise_w2(w2_bf[0][:, 2:], 2, 4, late_codes[:, : 2 * N])
         multiply_second(codes[2], planes[2], 2, 4, bank(0))
-        last_plane = quantise_rows(last_rows[:].rearrange("p s j -> p (s j)"), 7, late_codes[:, 6 * N :])
-        quantise_w2(rounded4[:], 4, 6, late_codes[:, 2 * N : 4 * N])
+        late_codes = keep.tile([P, 4 * N + C], U32, name="late_codes", tag="ring0", align_bytes=64)
+        quantise_w2(w2_bf[0][:, 2:], 4, 6, late_codes[:, : 2 * N])
         quantise_woven(4, 6)
         multiply_second(codes[4], planes[4], 4, 6, bank(2))
-        quantise_w2(rounded6[:], 6, 8, late_codes[:, 4 * N : 6 * N])
-        multiply_second(late_codes[:, 6 * N :], last_plane, 7, 8, bank(7))
+        last_plane = quantise_rows(last_rows[:].rearrange("p s j -> p (s j)"), 7, late_codes[:, 4 * N :])
+        quantise_w2(rounded6[:], 6, 8, late_codes[:, 2 * N : 4 * N])
+        multiply_second(late_codes[:, 4 * N :], last_plane, 7, 8, bank(7))
         quantise_woven(6, 7)
         multiply_second(codes[6], planes[6], 6, 7, bank(1))
 

@@ -128,7 +128,8 @@ def tile_moe_ser_none_kernel(
         load_w1_scales(1, range(4))
         load_w1(4, 6, range(2, 4))
         load_w1(6, 8, range(2, 4))
-        load_w2(2, 6)
+        load_w2(2, 4)
+        load_w2(4, 6)
         w2_last = load_w2(6, 8)
         offs2_sb = load_list("offs2_sb", offs2)
         gate2_sb = keep.tile([P, 2, T], F32, name="gate2_sb", align_bytes=256)
@@ -357,14 +358,14 @@ def tile_moe_ser_none_kernel(
 
         woven, codes, planes = {}, {}, {}
 
-        def gather_pairs(g, first, last):
+        def gather_pairs(g, first, last, weave=nc.gpsimd.tensor_copy):
             width = (last - first) * C
             lst = entries(offs2_sb, first * C, last * C)
             woven[first] = keep.tile([P, width, 2], U32, name=f"woven{first}", align_bytes=64)
             cg = keep.tile([P, 2, width], U32, name=f"cg{first}", tag=f"ring{g % 2}", align_bytes=64)
             for u in range(2):
                 nc.vector.tensor_copy(cg[:, u, :], windows[u].indirect(lst))
-            nc.gpsimd.tensor_copy(woven[first][:], cg[:].rearrange("p u s -> p s u"))
+            weave(woven[first][:], cg[:].rearrange("p u s -> p s u"))
 
         def quantise_woven(first, last):
             codes[first] = keep.tile([P, (last - first) * C], U32, name=f"codes{first}", align_bytes=64)
@@ -378,9 +379,7 @@ def tile_moe_ser_none_kernel(
         gather_pairs(1, 2, 4)
         quantise_woven(2, 4)
         gather_pairs(2, 4, 6)
-        woven[6] = keep.tile([P, C, 2], U32, name="woven6", tag="ring1", align_bytes=64)
-        for u in range(2):
-            nc.vector.tensor_copy(woven[6][:, :, u], windows[u].indirect(entries(offs2_sb, 6 * C, 7 * C)))
+        gather_pairs(1, 6, 7, nc.scalar.copy)
         multiply_second(codes[2], planes[2], 2, 4, bank(0))
         late_codes = keep.tile([P, 4 * N + C], U32, name="late_codes", tag="ring0", align_bytes=64)
         quantise_w2(w2_bf[0][:, 2:], 4, 6, late_codes[:, : 2 * N])

@@ -222,7 +222,7 @@ def tile_moe_ser_none_kernel(
                 (5, 1, 0, 4, nc.scalar.copy),
                 (3, 0, 4, 6, nc.scalar.copy),
                 (1, 0, 6, 7, nc.scalar.copy),
-                (4, 0, 7, 8, nc.vector.tensor_copy),
+                (4, 0, 7, 8, nc.scalar.copy),
             ),
             second=(0, 2, 3, 4, 1),
         )
@@ -274,7 +274,7 @@ def tile_moe_ser_none_kernel(
         gather_and_turn(vector_gather, 3, 1, range(0, 2))
         gather_and_turn(vector_gather, 3, 1, range(2, 4))
 
-        for m, copy in enumerate((nc.scalar.copy, nc.scalar.copy)):
+        for m, copy in enumerate((nc.scalar.copy, nc.vector.tensor_copy)):
             copy(
                 c_rows[:, :, :, 32 * m : 32 * (m + 1), :],
                 totals[m][:].rearrange("t (q p u d) -> t q u p d", q=TOKEN_BLOCKS, u=2, d=2),
@@ -320,12 +320,17 @@ def tile_moe_ser_none_kernel(
         rounded6 = keep.tile([P, 2, N, PACK], BF16, name="rounded6", tag="ident", align_bytes=64)
         round_w2(rounded6[:], w2_last[:])
         c_planes = keep.tile([P, 2, 2, T], BF16, name="c_planes", tag="c_planes", align_bytes=64)
+        last_rows = keep.tile([P, C, PACK], BF16, name="last_rows", align_bytes=64)
         for u, index in enumerate((3, 4)):
             singles = psum.tile([P, 2, T], BF16, name=f"singles{u}", tag=f"bank{index}")
             for d in range(2):
                 for q in range(TOKEN_BLOCKS):
                     nc.tensor.transpose(singles[:, d, q * P : (q + 1) * P], c_rows[:, q, u, :, d], ident_bf[:])
             nc.scalar.copy(c_planes[:, u], singles[:])
+            for d in range(2):
+                nc.scalar.activation(
+                    last_rows[:, :, 2 * u + d], c_planes[:, u, d, :].indirect(entries(offs2_sb, 7 * C, 8 * C)), COPY
+                )
 
         windows = [c_words[:, u, :].bitcast(U32) for u in range(2)]
 
@@ -348,12 +353,6 @@ def tile_moe_ser_none_kernel(
                 )
             copy(y_sb[:, first * C : last * C], acc[:, : (last - first) * C])
 
-        last_rows = keep.tile([P, C, PACK], BF16, name="last_rows", align_bytes=64)
-        for u in range(2):
-            for d in range(2):
-                nc.scalar.activation(
-                    last_rows[:, :, 2 * u + d], c_planes[:, u, d, :].indirect(entries(offs2_sb, 7 * C, 8 * C)), COPY
-                )
         y_sb = keep.tile([P, S], F32, name="y_sb", align_bytes=64)
 
         woven, codes, planes = {}, {}, {}

from contextlib import ExitStack

import concourse.mybir as mybir
from concourse.masks import make_identity

K, T, E, C, H, N = 1024, 512, 8, 128, 512, 128
S = E * C
FLOPS = 2 * S * K * H + 2 * S * H * N

F32 = mybir.dt.float32
BF16 = mybir.dt.bfloat16
I32 = mybir.dt.int32
U32 = mybir.dt.uint32
U16 = mybir.dt.uint16
U8 = mybir.dt.uint8
FP8X4 = mybir.dt.float8_e4m3fn_x4
FP4X4 = mybir.dt.float4_e2m1fn_x4
MULT = mybir.AluOpType.mult
ADD = mybir.AluOpType.add
COPY = mybir.ActivationFunctionType.Copy

P = 128
PACK = 4
PASSES = K // (P * PACK)
ROW_TILES = H // P
TOKEN_BLOCKS = T // P
SPARE = 192
WINDOW = T + SPARE
PLANE_WINDOW = 1408


def entries(lst, first, last):
    return lst[:, first // 16 : last // 16]


def tile_moe_ser_none_kernel(
    tc, x_words, x_scales, w1_words, w1_scales, w2, gate1, gate2, offs, pos1, pos2, offs2, pos3, pos4, out
):
    nc = tc.nc
    with ExitStack() as ctx:
        keep = ctx.enter_context(tc.tile_pool(name="keep", bufs=1))
        psum = ctx.enter_context(tc.psum_pool(name="psum", bufs=1))

        def bank(index):
            return psum.tile([P, 512], F32, name=f"bank{index}", tag=f"bank{index}")

        def load_list(name, src):
            lst = keep.tile(list(src.shape), U16, name=name)
            nc.sync.dma_start(lst[:], src)
            return lst

        def vector_gather(dst, window):
            nc.vector.tensor_copy(dst, window)

        def scalar_gather(dst, window):
            nc.scalar.activation(dst, window, COPY)

        x_plane = keep.tile([P, PLANE_WINDOW], U8, name="x_plane", align_bytes=256)
        nc.gpsimd.memset(x_plane[:, :T].bitcast(I32), 0)
        nc.gpsimd.memset(x_plane[:, T:].bitcast(I32), 0)
        gate1_rows = keep.tile([P, P], F32, name="gate1_rows")
        nc.gpsimd.memset(gate1_rows[:], 0.0)
        sg = [keep.tile([P, S], U8, name=f"sg{s}", align_bytes=256) for s in range(PASSES)]
        nc.gpsimd.memset(sg[1][:].bitcast(I32), 0)
        w1_planes = [keep.tile([P, E * PASSES, H // 2], U8, name=f"w1_plane{i}", align_bytes=256) for i in range(2)]
        nc.vector.memset(w1_planes[0][:].rearrange("p g i -> p (g i)").bitcast(I32), 0)
        zeros = keep.tile([P, 1, H // 8], I32, name="zeros", align_bytes=64)
        nc.vector.memset(zeros[:], 0)
        nc.scalar.copy(w1_planes[1][:].bitcast(U32), zeros[:].bitcast(U32).to_broadcast([P, E * PASSES, H // 8]))
        x_sb = keep.tile([P, PASSES * T + SPARE], I32, name="x_sb", align_bytes=256)
        nc.vector.memset(x_sb[:, PASSES * T :], 0)

        w1_sb = {}

        def load_w1(first, last, tiles):
            width = 2 * P * len(tiles)
            words = keep.tile([P, last - first, PASSES, width], U8, name=f"w1_sb{first}_{tiles.start}", tag=f"w1_sb{first}_{tiles.start}", align_bytes=256)
            rows = w1_words[first:last].rearrange("e s p b -> p (e s) b")
            nc.sync.dma_start(
                words[:].rearrange("p e s b -> p (e s) b").bitcast(I32),
                rows[:, :, 2 * P * tiles.start : 2 * P * tiles.stop].bitcast(I32),
            )
            for e in range(first, last):
                for k, m in enumerate(tiles):
                    w1_sb[e, m] = words[:, e - first, :, 2 * P * k : 2 * P * (k + 1)]

        w2_raw = {}

        def load_w2(first, last):
            raw = keep.tile([P, last - first, PACK, N], F32, name=f"w2_raw{first}", align_bytes=256)
            nc.sync.dma_start(
                raw[:].rearrange("p e j n -> p e (j n)"),
                w2[first:last].rearrange("e (p j) n -> p e (j n)", j=PACK),
            )
            for e in range(first, last):
                w2_raw[e] = raw[:, e - first]
            return raw

        def load_w1_scales(half, residues):
            rows = w1_scales.rearrange("e s (q r) i -> r q (e s) i", r=4)
            for r in residues:
                nc.sync.dma_start(
                    w1_planes[half][r:P:32].bitcast(I32),
                    rows[r][:, :, half * H // 2 : (half + 1) * H // 2].bitcast(I32),
                )

        offs_sb = load_list("offs_sb", offs)
        nc.sync.dma_start(x_sb[:, :T], x_words[0].rearrange("p t d -> p (t d)").bitcast(I32))
        for q in range(4):
            (nc.sync if q < 2 else nc.scalar).dma_start(
                x_plane[32 * q : 32 * q + 8, :T].bitcast(I32), x_scales[:, 4 * q : 4 * q + 4, :].bitcast(I32)
            )
        nc.sync.dma_start(x_sb[:, T : PASSES * T], x_words[1].rearrange("p t d -> p (t d)").bitcast(I32))
        load_w1_scales(0, range(0, 1))
        nc.sync.dma_start(
            gate1_rows[: 2 * TOKEN_BLOCKS, :], gate1[:, 0, :].rearrange("r (q c) -> r q c", c=P)
        )
        load_w1_scales(0, range(1, 4))
        load_w1(0, 4, range(0, 2))
        load_w1(4, 8, range(0, 2))
        w2_first = load_w2(0, 2)
        nc.vector.tensor_copy(sg[0][:], x_plane[:].indirect(offs_sb[:]))
        for r in range(4):
            nc.sync.dma_start(sg[1][r:P:32].bitcast(I32), sg[0][4 + r : P : 32].bitcast(I32))
        pos1_sb = load_list("pos1_sb", pos1)
        load_w1(0, 4, range(2, 4))
        pos2_sb = load_list("pos2_sb", pos2)
        load_w1_scales(1, range(4))
        load_w1(4, 6, range(2, 4))
        load_w1(6, 8, range(2, 4))
        load_w2(2, 4)
        load_w2(4, 6)
        w2_last = load_w2(6, 8)
        offs2_sb = load_list("offs2_sb", offs2)
        gate2_sb = keep.tile([P, 2, T], F32, name="gate2_sb", align_bytes=256)
        nc.sync.dma_start(gate2_sb[:], gate2.rearrange("r p t -> p r t"))
        pos3_sb = load_list("pos3_sb", pos3)
        pos4_sb = load_list("pos4_sb", pos4)

        ident = keep.tile([P, P], F32, name="ident", tag="ident", align_bytes=64)
        make_identity(nc, ident[:])
        ident_bf = keep.tile([P, P], BF16, name="ident_bf")
        nc.scalar.copy(ident_bf[:], ident[:])

        gate1_cols = keep.tile([P, 2 * TOKEN_BLOCKS], F32, name="gate1_cols")
        turned_gates = bank(2)
        nc.tensor.transpose(turned_gates[:, :P], gate1_rows[:], ident[:])
        nc.scalar.copy(gate1_cols[:], turned_gates[:, : 2 * TOKEN_BLOCKS])
        gate1_sb = keep.tile([P, 2, T], F32, name="gate1_sb", align_bytes=64)
        for r in range(2):
            spread = bank(6 + r)
            for q in range(TOKEN_BLOCKS):
                column = r * TOKEN_BLOCKS + q
                nc.tensor.transpose(
                    spread[:, q * P : (q + 1) * P], gate1_cols[:, column : column + 1].to_broadcast([P, P]), ident[:]
                )
            nc.scalar.copy(gate1_sb[:, r, :], spread[:])

        h_sb = [keep.tile([P, S], F32, name=f"h_sb{m}", tag=f"h{m}", align_bytes=64) for m in range(ROW_TILES)]
        xg = keep.tile([P, PASSES, S], U32, name="xg", align_bytes=64)

        def gather_words(s, lo, hi):
            nc.vector.tensor_copy(
                xg[:, s, lo * C : hi * C],
                x_sb[:, s * T : s * T + WINDOW].bitcast(U32).indirect(entries(offs_sb, lo * C, hi * C)),
            )

        gather_words(0, 0, 4)
        gather_words(0, 4, 8)
        gather_words(1, 0, 4)
        gather_words(1, 4, 6)
        gather_words(1, 6, 7)
        gather_words(1, 7, 8)

        w2_codes = {}
        w2_plane = keep.tile([P, E * N], U8, name="w2_plane", align_bytes=64)

        def quantise_w2(rows, first, last, codes):
            nc.vector.quantize_mx(
                out=codes.bitcast(FP8X4),
                scales=w2_plane[:, first * N : last * N],
                in_=rows.rearrange("p e n j -> p (e n j)"),
            )
            for e in range(first, last):
                w2_codes[e] = codes[:, (e - first) * N : (e - first + 1) * N]

        def round_w2(grouped, raw):
            nc.scalar.copy(
                grouped.rearrange("p e (c i) j -> p e c j i", i=4),
                raw.rearrange("p e j (c i) -> p e c j i", i=4),
            )

        rounded0 = keep.tile([P, 2, N, PACK], BF16, name="rounded0", tag="rounded0", align_bytes=64)
        round_w2(rounded0[:], w2_first[:])
        first_codes = keep.tile([P, 2 * N], U32, name="first_codes", align_bytes=64)
        quantise_w2(rounded0[:], 0, 2, first_codes[:])

        def multiply(acc, s, m, first, last):
            for e in range(first, last):
                nc.tensor.matmul_mx(
                    acc[:, (e - first) * C : (e - first + 1) * C],
                    lhsT=w1_sb[e, m][:, s, :].bitcast(FP4X4),
                    lhsT_scale=w1_planes[m // 2][:, e * PASSES + s, (m % 2) * P : (m % 2 + 1) * P],
                    rhs=xg[:, s, e * C : (e + 1) * C].bitcast(FP8X4),
                    rhs_scale=sg[s][:, e * C : (e + 1) * C],
                    start=(s == 0 and e == first),
                    stop=(s == PASSES - 1 and e == last - 1),
                )

        def multiply_by_pass(groups, second=(0,)):
            accs = [bank(index) for index, m, first, last, copy in groups]
            for acc, (index, m, first, last, copy) in zip(accs, groups):
                multiply(acc, 0, m, first, last)
            for k in second:
                acc, (index, m, first, last, copy) = accs[k], groups[k]
                multiply(acc, 1, m, first, last)
                copy(h_sb[m][:, first * C : last * C], acc[:, : (last - first) * C])

        multiply_by_pass(
            (
                (0, 0, 0, 4, nc.scalar.copy),
                (5, 1, 0, 4, nc.scalar.copy),
                (3, 0, 4, 6, nc.scalar.copy),
                (1, 0, 6, 7, nc.scalar.copy),
                (4, 0, 7, 8, nc.scalar.copy),
            ),
            second=(0, 2, 3, 4, 1),
        )
        for index, m, first in ((3, 1, 4), (2, 2, 0), (6, 3, 0)):
            multiply_by_pass(((index, m, first, first + 4, nc.scalar.copy),))
        for index, m, first in ((7, 2, 4), (0, 3, 4), (1, 2, 6), (4, 3, 6)):
            multiply_by_pass(((index, m, first, first + 2, nc.scalar.copy),))

        pos_sb = (pos1_sb, pos2_sb)
        c_rows = keep.tile([P, TOKEN_BLOCKS, 2, P, 2], BF16, name="c_rows", tag="c_rows", align_bytes=64)

        totals = [bank(2), bank(4)]
        for m, total in enumerate(totals):
            for r in range(2):
                part = keep.tile([P, T], F32, name=f"part{m}_{r}", tag="rounded0" if (m, r) == (0, 0) else "", align_bytes=64)
                nc.vector.tensor_tensor(part[:], h_sb[m][:].indirect(pos_sb[r][:]), gate1_sb[:, r, :], MULT)
                for q in range(TOKEN_BLOCKS):
                    nc.tensor.matmul(
                        total[:, q * P : (q + 1) * P],
                        part[:, q * P : (q + 1) * P],
                        ident[:],
                        is_transpose=True,
                        start=(r == 0 and q == 0),
                        stop=(r == 1 and q == TOKEN_BLOCKS - 1),
                    )

        w2_bf = [keep.tile([P, 4, N, PACK], BF16, name="w2_bf0", tag="h1", align_bytes=64)]
        for e in range(4):
            nc.gpsimd.tensor_scalar(w2_bf[0][:, e], w2_raw[2 + e].rearrange("p j n -> p n j"), 1.0, 0.0, MULT, ADD)

        turned = [[bank(index) for index in indices] for indices in ((1, 3), (7, 5))]

        def turned_rows(r, q):
            return turned[r][q // 2][:, (q % 2) * 2 * P : (q % 2 + 1) * 2 * P]

        def gather_and_turn(gather, m, r, blocks, tag=""):
            part = keep.tile([P, len(blocks) * P], F32, name=f"part{m}_{r}_{blocks.start}", tag=tag, align_bytes=64)
            gather(part[:], h_sb[m][:].indirect(entries(pos_sb[r], blocks.start * P, blocks.stop * P)))
            for k, q in enumerate(blocks):
                nc.tensor.transpose(
                    turned_rows(r, q)[:, (m - 2) * P : (m - 1) * P], part[:, k * P : (k + 1) * P], ident[:]
                )

        every = range(TOKEN_BLOCKS)
        gather_and_turn(scalar_gather, 2, 0, every)
        gather_and_turn(vector_gather, 2, 1, every)
        gather_and_turn(scalar_gather, 3, 0, range(0, 2))
        gather_and_turn(scalar_gather, 3, 0, range(2, 4))
        gather_and_turn(vector_gather, 3, 1, range(0, 2))
        gather_and_turn(vector_gather, 3, 1, range(2, 4))

        for m, copy in enumerate((nc.scalar.copy, nc.vector.tensor_copy)):
            copy(
                c_rows[:, :, :, 32 * m : 32 * (m + 1), :],
                totals[m][:].rearrange("t (q p u d) -> t q u p d", q=TOKEN_BLOCKS, u=2, d=2),
            )

        c_words = keep.tile([P, 2, T], F32, name="c_words", align_bytes=64)

        def turn_back(copy, q, halves, back):
            for k, u in enumerate(halves):
                nc.tensor.transpose(
                    back[:, k * P : (k + 1) * P], c_rows[:, q, u].rearrange("t p d -> t (p d)").bitcast(F32), ident[:]
                )
            copy(
                c_words[:, halves.start : halves.stop, q * P : (q + 1) * P],
                back[:, : len(halves) * P].rearrange("p (u t) -> p u t", t=P),
            )

        def by_half(rows):
            return rows.rearrange("t (p u d) -> t u p d", u=2, d=2)

        scaled = []
        for q in range(TOKEN_BLOCKS):
            scaled.append(keep.tile([P, 2, P // 2, 2], F32, name=f"scaled{q}", tag=f"scaled{q}", align_bytes=64))
            nc.scalar.activation(scaled[q][:], by_half(turned_rows(0, q)), COPY, scale=gate1_cols[:, q : q + 1])
        for q in range(TOKEN_BLOCKS):
            for u in range(2):
                nc.vector.scalar_tensor_tensor(
                    c_rows[:, q, u, P // 2 :],
                    by_half(turned_rows(1, q))[:, u],
                    gate1_cols[:, TOKEN_BLOCKS + q : TOKEN_BLOCKS + q + 1],
                    scaled[q][:, u],
                    MULT,
                    ADD,
                )
        for q in range(TOKEN_BLOCKS - 1):
            turn_back(nc.scalar.copy, q, range(0, 2), bank((6, 0, 2)[q]))
        turn_back(nc.scalar.copy, TOKEN_BLOCKS - 1, range(0, 1), bank(7))
        turn_back(nc.vector.tensor_copy, TOKEN_BLOCKS - 1, range(1, 2), bank(1))

        early_codes = keep.tile([P, 2 * N], U32, name="early_codes", tag="scaled3", align_bytes=64)
        quantise_w2(w2_bf[0][:, :2], 2, 4, early_codes[:])

        rounded6 = keep.tile([P, 2, N, PACK], BF16, name="rounded6", tag="ident", align_bytes=64)
        round_w2(rounded6[:], w2_last[:])
        c_planes = keep.tile([P, 2, 2, T], BF16, name="c_planes", tag="c_planes", align_bytes=64)
        last_rows = keep.tile([P, C, PACK], BF16, name="last_rows", align_bytes=64)
        for u, index in enumerate((3, 4)):
            singles = psum.tile([P, 2, T], BF16, name=f"singles{u}", tag=f"bank{index}")
            for d in range(2):
                for q in range(TOKEN_BLOCKS):
                    nc.tensor.transpose(singles[:, d, q * P : (q + 1) * P], c_rows[:, q, u, :, d], ident_bf[:])
            nc.scalar.copy(c_planes[:, u], singles[:])
            for d in range(2):
                nc.scalar.activation(
                    last_rows[:, :, 2 * u + d], c_planes[:, u, d, :].indirect(entries(offs2_sb, 7 * C, 8 * C)), COPY
                )

        windows = [c_words[:, u, :].bitcast(U32) for u in range(2)]

        def quantise_rows(rows, first, codes):
            plane = keep.tile([P, codes.shape[1]], U8, name=f"plane{first}", align_bytes=64)
            nc.vector.quantize_mx(out=codes.bitcast(FP8X4), scales=plane[:], in_=rows)
            return plane

        def multiply_second(codes, plane, first, last, acc, copy=nc.scalar.copy):
            for e in range(first, last):
                cols = slice((e - first) * C, (e - first + 1) * C)
                nc.tensor.matmul_mx(
                    acc[:, cols],
                    lhsT=w2_codes[e].bitcast(FP8X4),
                    lhsT_scale=w2_plane[:, e * N : (e + 1) * N],
                    rhs=codes[:, cols].bitcast(FP8X4),
                    rhs_scale=plane[:, cols],
                    start=True,
                    stop=True,
                )
            copy(y_sb[:, first * C : last * C], acc[:, : (last - first) * C])

        y_sb = keep.tile([P, S], F32, name="y_sb", align_bytes=64)

        woven, codes, planes = {}, {}, {}

        def gather_pairs(g, first, last, weave=nc.gpsimd.tensor_copy):
            width = (last - first) * C
            lst = entries(offs2_sb, first * C, last * C)
            woven[first] = keep.tile([P, width, 2], U32, name=f"woven{first}", align_bytes=64)
            cg = keep.tile([P, 2, width], U32, name=f"cg{first}", tag=f"ring{g % 2}", align_bytes=64)
            for u in range(2):
                nc.vector.tensor_copy(cg[:, u, :], windows[u].indirect(lst))
            weave(woven[first][:], cg[:].rearrange("p u s -> p s u"))

        def quantise_woven(first, last):
            codes[first] = keep.tile([P, (last - first) * C], U32, name=f"codes{first}", align_bytes=64)
            planes[first] = quantise_rows(
                woven[first][:].rearrange("p s u -> p (s u)").bitcast(BF16), first, codes[first][:]
            )

        gather_pairs(0, 0, 2)
        quantise_woven(0, 2)
        multiply_second(codes[0], planes[0], 0, 2, bank(6))
        gather_pairs(1, 2, 4)
        quantise_woven(2, 4)
        gather_pairs(2, 4, 6)
        gather_pairs(1, 6, 7, nc.scalar.copy)
        multiply_second(codes[2], planes[2], 2, 4, bank(0))
        late_codes = keep.tile([P, 4 * N + C], U32, name="late_codes", tag="ring0", align_bytes=64)
        quantise_w2(w2_bf[0][:, 2:], 4, 6, late_codes[:, : 2 * N])
        quantise_woven(4, 6)
        multiply_second(codes[4], planes[4], 4, 6, bank(2))
        last_plane = quantise_rows(last_rows[:].rearrange("p s j -> p (s j)"), 7, late_codes[:, 4 * N :])
        quantise_w2(rounded6[:], 6, 8, late_codes[:, 2 * N : 4 * N])
        multiply_second(late_codes[:, 4 * N :], last_plane, 7, 8, bank(7))
        quantise_woven(6, 7)
        multiply_second(codes[6], planes[6], 6, 7, bank(1))

        halves = (slice(0, T // 2), slice(T // 2, T))
        first_part = keep.tile([P, T], F32, name="first_part")
        nc.vector.tensor_tensor(first_part[:], y_sb[:].indirect(pos3_sb[:]), gate2_sb[:, 0, :], MULT)
        parts = []
        for hh, toks in enumerate(halves):
            picked = keep.tile([P, T // 2], F32, name=f"picked{hh}")
            scalar_gather(picked[:], y_sb[:].indirect(entries(pos4_sb, toks.start, toks.stop)))
            parts.append(keep.tile([P, T // 2], F32, name=f"second_part{hh}"))
            nc.vector.tensor_tensor(parts[hh][:], picked[:], gate2_sb[:, 1, toks], MULT)
        for hh, toks in enumerate(halves):
            total = keep.tile([P, T // 2], F32, name=f"total{hh}")
            nc.vector.tensor_tensor(total[:], first_part[:, toks], parts[hh][:], ADD)
            nc.sync.dma_start(out[:, toks], total[:])
